import numpy as np, ml_dtypes
CORES = [25,29,65,69,153,157,193,197]
N = 8
import mx_ref
BF = ml_dtypes.bfloat16
def gcols(t, e):
    v = np.concatenate([t.reshape(8, 16, -1, 4), np.zeros((8, 16, 1, 4), BF)], axis=2)
    return np.ascontiguousarray(np.stack([v[g][:, e[g]] for g in range(8)])).reshape(128, -1)
def tile(rs):
    return np.stack(rs, axis=2).reshape(128, -1).astype(BF)
def cut(t, i, w=512):
    return t[:, w * i:w * i + w]
def pick(q, e):
    c = np.concatenate([q[0].reshape(128, -1, 4), np.zeros((128, 1, 4), np.uint8)], axis=1); s = np.concatenate([q[1], np.ones((16, 1), np.uint8)], axis=1)
    return (np.ascontiguousarray(c[:, e].reshape(128, -1)), np.ascontiguousarray(s[:, e]))
def join(*qs):
    return (np.concatenate([q[0] for q in qs], axis=1), np.concatenate([q[1] for q in qs], axis=1))
def put(q, e, v):
    c, s = q[0].reshape(128, -1, 4).copy(), q[1].copy(); c[:, e] = v[0].reshape(128, -1, 4); s[:, e] = v[1]
    return (c.reshape(128, -1), s)
def pk(c, s):
    return (np.ascontiguousarray(c), mx_ref.live(s))
def emit(q):
    return q[0], q[1]
def packed(v, rng):
    q = [mx_ref.quantize(np.ascontiguousarray(v[r])) for r in range(N)]
    return np.stack([a for a, b in q]), np.stack([mx_ref.plane(b, rng) for a, b in q])
def values_of_codes():
    e, c = np.zeros((128, 128, 4), np.float32), np.zeros((128, 2, 4), np.uint8)
    e[np.arange(128), np.arange(128), 0] = 1
    c[:127, :, 0] = np.arange(256).reshape(2, 128).T[:127]
    return mx_ref.matmul(mx_ref.quantize(e.reshape(128, 512).astype(BF)), (c.reshape(128, 8), np.full((16, 2), 127, np.uint8))).T.reshape(-1).astype(np.float64)
CODE_VALUE, SCALE_VALUE = values_of_codes(), 2.0 ** (np.arange(256) - 127.0)
def decode(q):
    return (CODE_VALUE[q[0]].reshape(16, 8, -1, 4) * SCALE_VALUE[q[1]][:, None, :, None] + 0.0).reshape(128, -1).astype(np.float32)
def f(rng, *shape):
    return mx_ref.flush((rng.standard_normal(shape, dtype=np.float32) * np.exp2(rng.integers(-2, 3, shape[:-1] + (1,)))).astype(BF))
def wide(rng, *shape, cols=0):
    v = rng.standard_normal(shape, dtype=np.float32) * np.exp2(rng.integers(-12, 13, shape)).astype(np.float32)
    if cols: v *= np.repeat(np.exp2(rng.integers(-cols, cols + 1, shape[:-2] + (1, shape[-1] // 4))) * (rng.random(shape[:-2] + (1, shape[-1] // 4)) > 0.0625), 4, axis=-1).astype(np.float32)
    return mx_ref.flush(v.astype(BF))
C, K, R = 320, 64, 2
def choose(p):
    o = np.argsort(-(p[::16] + np.float32(0.0)), axis=1, kind="stable")
    return np.sort(o[:, :K], axis=1), np.sort(o[:, C - K:], axis=1)
def edit(hi, lo):
    e = []
    for g in range(8):
        stay = np.delete(np.arange(C), lo[g])
        key = np.concatenate([2 * stay, 2 * hi[g] + 1])
        e.append(np.concatenate([stay, C + np.arange(K)])[np.argsort(key)])
    return np.stack(e)
def numbers_of(rng):
    return {"x": np.array(f(rng, N, 128, 4 * C)), "u": np.array(f(rng, N, 128, 512)), "v": np.array(f(rng, N, 128, 512))}
def weights(rng, w, z):
    wc, ws = packed(w, rng)
    zc, zs = packed(z, rng)
    return {"wc": wc, "ws": ws, "zc": zc, "zs": zs}
def still(rng):
    w = np.zeros((N, 128, 4, 128, 4), np.float32)
    i = np.arange(128)
    for b in range(4): w[:, i, b, i, b] = 64
    return weights(rng, w.reshape(N, 128, 2048).astype(BF), np.zeros((N, 128, 2048), BF))
def signs(rng):
    return np.stack([rng.permutation(8) % 2 * 2.0 - 1.0 for r in range(N)])
def marks():
    n = np.arange(K)
    h = C - 2 * K
    v = np.ones((8, C), np.float32)
    cases = ((n, h + K + n), (h + K + n, n), (2 * n, 2 * n + 1), (2 * n + 1, 2 * n), (h + 2 * n, h + 2 * n + 1), (h + 2 * n + 1, h + 2 * n), (n, K + n), (K + n, n))
    for g in range(8):
        v[g, cases[g][0]] = 4
        v[g, cases[g][1]] = -2
    return v
def setup_inputs(rng):
    return {**numbers_of(rng), **weights(rng, f(rng, N, 128, 2048), f(rng, N, 128, 2048))}
def setup_inputs_ties(rng):
    d = numbers_of(rng)
    e = rng.permutation(N)
    x = d["x"].reshape(N, 8, 16, C, 4)
    for r in range(N):
        k = np.zeros(C, int) if r == e[0] else rng.permutation(C) % 3
        a = x[r][:, :8, :3].copy()
        a[:, :, 2] = 0
        x[r][:, :8] = a[:, :, k]
    x[e[1]] = 0
    u = d["u"].reshape(N, 8, 16, 128, 4)
    u[:, :, 8:, ::16] = 0
    w = np.array(f(rng, N, 128, 2048)).reshape(N, 8, 16, 4, 8, 16, 4)
    z = np.array(f(rng, N, 128, 2048)).reshape(N, 8, 16, 4, 8, 16, 4)
    for a in (w, z): a[:, :, 8:, :, :, :8] = 0
    return {"x": x.reshape(N, 128, 4 * C), "u": u.reshape(N, 128, 512), "v": d["v"], **weights(rng, w.reshape(N, 128, 2048), z.reshape(N, 128, 2048))}
def setup_inputs_ends(rng):
    d = numbers_of(rng)
    x = d["x"].reshape(N, 8, 16, C, 4)
    u = d["u"].reshape(N, 8, 16, 128, 4)
    x[:, :, 0] = 0
    u[:, :, :, ::16] = 0
    for r in range(N): x[r, :, 0, :, 0] = marks()[rng.permutation(8)].astype(BF)
    for g in range(8): u[:, g, 0, 16 * g, 0] = 1
    w = f(rng, N, 128, 2048).astype(np.float32).reshape(N, 8, 16, 4, 8, 16, 4)
    z = f(rng, N, 128, 2048).astype(np.float32).reshape(N, 8, 16, 4, 8, 16, 4)
    for a in (w, z):
        a[:, :, 15] = 0
        a[:, :, :, :, :, 15] *= np.float32(8192)
    return {**d, "x": x.reshape(N, 128, 4 * C), "u": u.reshape(N, 128, 512), **weights(rng, w.reshape(N, 128, 2048).astype(BF), z.reshape(N, 128, 2048).astype(BF))}
def setup_inputs_near(rng):
    d = numbers_of(rng)
    x = d["x"].astype(np.float32).reshape(N, 8, 16, C, 4)
    s = np.minimum((np.arange(C) + 1) // 2, 255)
    g = ((s[:, None] >> np.arange(8)) & 1) * np.exp2(np.arange(8) - 23.0)
    x[:, :, 0] = 0
    x[:, :, 0, :, 0] = signs(rng)[:, :, None]
    for r in rng.permutation(N)[:N // 2]:
        x[r, :, 0, C - 1, 0] = 16
        x[r, :, 0, 0, 0] = -16
    x[:, :, 8] = g[:, :4]
    x[:, :, 9] = g[:, 4:]
    x[:, :, 10:] = rng.integers(4, 8, (N, 8, 6, C, 4)) * rng.choice([-1.0, 1.0], (N, 8, 6, C, 4)) * 2.0 ** -20
    k = np.exp2(-1.0 * rng.permutation(np.arange(N) * 30 // (N - 1))).astype(np.float32).astype(BF)
    u = d["u"].reshape(N, 128, 128, 4)
    u[:, :, ::16] = 0
    for h in range(0, 128, 16):
        u[:, h, h, 0] = k
        u[:, h + 8:h + 10, h] = k[:, None, None]
    return {"x": x.reshape(N, 128, 4 * C).astype(BF), "u": u.reshape(N, 128, 512), "v": d["v"], **still(rng)}
def setup_inputs_huge(rng):
    d = numbers_of(rng)
    x = 2.0 ** 30 * (0.6 + 0.4 * rng.random((N, 128, C, 4)))
    c = np.stack([rng.permutation(C) % 2 * 2.0 - 1.0 for r in range(N)])
    c[rng.permutation(N) < N // 2] = 1
    x *= c[:, None, :, None]
    u = d["u"].reshape(N, 128, 128, 4)
    a = 2.0 ** 30 * (1 - 0.25 * rng.random((N, 128, 8, 4))) * signs(rng)[:, None, :, None]
    u[:, :, ::16] = a.astype(np.float32).astype(BF)
    return {"x": x.astype(np.float32).reshape(N, 128, 4 * C).astype(BF), "u": u.reshape(N, 128, 512), "v": d["v"], **still(rng)}
def setup_inputs_spread(rng):
    d = setup_inputs(rng)
    d["x"] = wide(rng, N, 128, 4 * C, cols=6)
    return d
def check_inputs(d):
    b = []
    for k in ("x", "u", "v"):
        a = np.abs(d[k].astype(np.float32))
        if not (np.isfinite(a).all() and ((a == 0) | (a >= 2.0 ** -30) & (a <= 2.0 ** 30)).all()): b.append("a value of " + k)
    return b
def reference(x, u, v, wc, ws, zc, zs):
    qu = [mx_ref.quantize(u[r]) for r in range(N)]
    w, z = [pk(wc[r], ws[r]) for r in range(N)], [pk(zc[r], zs[r]) for r in range(N)]
    now = [x[r] for r in range(N)]
    behind = (np.arange(C) + 1) % C
    ol = np.zeros((N, 8, C), np.float32)
    for t in range(R):
        hi, lo, border = [], [], []
        for r in range(N):
            h, l = choose(mx_ref.matmul(qu[r], mx_ref.quantize(now[r])))
            hi.append(h)
            lo.append(l)
            border.append(mx_ref.quantize(gcols(now[r], l)))
        came = decode(join(*border)).astype(BF)
        for r in range(N):
            a = (r - 1) % N
            e = edit(hi[r], lo[r])
            q = mx_ref.quantize(gcols(np.concatenate([now[r], cut(came, a, 4 * K)], axis=1), e))
            made = []
            for b in range(4):
                c = np.arange(128 * b, 128 * b + 128)
                made.append((mx_ref.matmul(pick(w[r], c), q) + mx_ref.matmul(pick(z[r], c), q)[:, behind]) * np.float32(0.015625))
            now[r] = tile(made)
            ol[r] = np.take_along_axis(np.concatenate([np.tile(np.arange(C), (8, 1)), C + lo[a]], axis=1), e, axis=1)
    y = np.zeros((N, 128, C), np.float32)
    oc, osc = np.zeros((N, 128, 4 * C), np.uint8), np.zeros((N, 16, C), np.uint8)
    for r in range(N):
        q = mx_ref.quantize(now[r])
        y[r] = mx_ref.matmul(mx_ref.quantize(v[r]), q)
        oc[r], osc[r] = emit(q)
    return {"y": y, "ol": ol, "oc": oc, "osc": osc}

@@ -1,0 +1,469 @@
+from concourse.mybir import dt, AluOpType as A, ActivationFunctionType as F
+
+C, K, R = 320, 64, 2
+Q4, U8, BF, FP, I32, U16 = "float8_e4m3fn_x4", "uint8", "bfloat16", "float32", "int32", "uint16"
+NPIV = C // 16
+OWN = (1, 3, 5, 7, 9, 11)
+PLAN = "o o f f o f f o f f o f f o f f f f f f"
+H = C // 2
+
+
+def sb(n, t):
+    return ("sbuf", [128, n], t)
+
+
+SCRATCH = {
+    "ut": sb(512, BF), "vt": sb(512, BF), "uq": sb(128, Q4), "us": sb(128, U8), "u3q": sb(384, Q4), "u3s": sb(384, U8),
+    "vq": sb(128, Q4), "vs": sb(128, U8),
+    "wq": sb(512, Q4), "wp": sb(512, U8), "zq": sb(512, Q4), "zp": sb(512, U8),
+    "x0": sb(4 * (C + K), BF), "x1": sb(4 * (C + K), BF), "x2": sb(4 * C, BF),
+    "xq": sb(C, Q4), "xs": sb(C, U8),
+    "tt": sb(C, FP), "msk": sb(NPIV * C, BF), "cnt": sb(NPIV * H, BF),
+    "zz": sb(2 * C, BF), "rows": sb(3 * 336, BF), "cut": sb(2 * NPIV, BF),
+    "yb": sb(C, BF), "yr": sb(C, BF), "wr": sb(C, BF), "eq": sb(C, BF), "vr": sb(C, BF), "mx": sb(H, BF), "nn": sb(1, FP),
+    "lm": sb(4 * C, BF), "lc": sb(4 * H, BF),
+    "sel": sb(3 * C, BF), "sm": sb(6 * NPIV, FP), "er": sb(2 * (C + K), BF),
+    "offb": sb(16, U16), "offt": sb(4 * NPIV, U16), "offd": sb(NPIV, U16), "offe": sb(NPIV, U16), "offu": sb(24, U16),
+    "offl": sb(4, U16), "larr": sb(4, U16), "rl": sb(4, U16),
+    "bt": sb(1024, BF), "bq0": sb(128, Q4), "bs0": sb(128, U8), "bq1": sb(128, Q4), "bs1": sb(128, U8),
+    "lq": sb(256, Q4), "ls": sb(256, U8),
+    "rq0": sb(K, Q4), "rs0": sb(K, U8), "rq1": sb(K, Q4), "rs1": sb(K, U8),
+    "tb": sb(4 * C + 8, BF), "tq": sb(C, Q4), "ts": sb(C, U8), "t2q": sb(C, Q4), "t2s": sb(C, U8),
+    "ew": sb(520, BF), "idn": sb(128, BF), "eq4": sb(512, Q4), "es4": sb(512, U8),
+    "iu": sb(24, I32), "qi": sb(2, I32), "qf": sb(1, FP), "kk": sb(NPIV, FP), "kq": sb(NPIV, FP), "twoc": sb(NPIV, FP),
+    "thr": sb(4, BF), "thrh": sb(1, FP), "jm": sb(C, BF), "csel": sb(C, BF), "chold": sb(C, BF), "cval": sb(C, BF),
+    "olw": sb(C + K, FP), "olr": sb(C, FP), "yo": sb(C, FP),
+}
+for _b in range(8):
+    SCRATCH["p%d" % _b] = ("psum", [128, 512], FP)
+
+POOLS = {"v": 50, "s": 28, "t": 16, "g": 10, "d": 16}
+SEMAPHORES = ["aq0", "aq1", "as0", "as1", "al", "sent"] + ["%s%d" % (k, i) for k in POOLS for i in range(POOLS[k])]
+
+
+def bits(engines):
+    m = 0
+    for e in engines:
+        m |= 1 << e
+    return m
+
+
+def route(T, topo, r):
+    src, dst = T.cores[r], T.cores[(r + 1) % len(T.cores)]
+    if topo.may_write(src, dst):
+        return dst, None, None
+    able = [c for c in topo.cores_of(src) if T.rank_of(c) is None and topo.may_write(c, dst)]
+    near = [c for c in able if topo.die(c) == topo.die(src)]
+    far = [c for c in able if topo.die(c) != topo.die(src)]
+    first = (near or able)[0]
+    rest = [c for c in far + near if c != first]
+    return dst, first, (rest or able)[0]
+
+
+def halves(topo, src, dst):
+    e = topo.engines(src, dst)
+    return e[0::2], e[1::2]
+
+
+def land(T, t):
+    a = 0 if t == 0 else 192
+    return T.lq[:, a:a + K].bitcast(dt.uint8), T.ls[:, a:a + K]
+
+
+def hand_on(g, core, T, topo):
+    sent = 0
+    for r in range(len(T.cores)):
+        dst, cq, cs = route(T, topo, r)
+        if core not in (cq, cs):
+            continue
+        ea, eb = halves(topo, T.cores[r], core)
+        out = topo.engines(core, dst)
+        rid, pid = topo.addr(dst, core)
+        jobs = []
+        for t in range(R):
+            lq, ls = land(T, t)
+            if core == cq:
+                jobs.append(("aq%d" % t, len(ea), lq, T["rq%d" % t][:].bitcast(dt.uint8)))
+            if core == cs:
+                jobs.append(("as%d" % t, len(eb), ls, T["rs%d" % t][:]))
+        if core == cs:
+            jobs.append(("al", len(eb), T.larr[:], T.rl[:]))
+        for sem, n, o, i in jobs:
+            g.wait_ge(T.sem[sem], n)
+            g.remote_dma(o, i, T.sem[sem], T.sem.sent, pid, rid, bits(out))
+            sent += len(out)
+    if sent:
+        g.wait_ge(T.sem.sent, sent)
+
+
+def emit(g, T, ops):
+    queue = {"v": g.vector, "s": g.scalar, "t": g.tensor, "g": g, "y": g.sync}
+    sets = {}
+    for i, o in enumerate(ops):
+        if o[4][:1] == "+":
+            sets.setdefault(o[4], []).append(i)
+    writer, readers, known = {}, {}, {q: set() for q in queue}
+    waits, before, needed = [], [], set()
+    for i, (q, fn, rd, wr, kind) in enumerate(ops):
+        deps = set()
+        if q != "x":
+            for k in rd:
+                if k in writer:
+                    deps.add(writer[k])
+                if k[0] == "#":
+                    deps.update(j for j in readers.get(k, ()) if ops[j][0] != q)
+            for k in wr:
+                if k in writer and not (kind == "acc" and k[0] == "#"):
+                    deps.add(writer[k])
+                deps.update(readers.get(k, ()))
+        mine = []
+        for d in sorted(deps, reverse=True):
+            if d not in known[q]:
+                members = sets.get(ops[d][4], [d])
+                assert members[-1] < i, "a wait inside a set"
+                mine.append(members[-1])
+                for j in members:
+                    known[q].add(j)
+                    known[q].update(before[j])
+        waits.append(mine)
+        needed.update(mine)
+        before.append(frozenset(known[q]) if q != "x" else frozenset())
+        for k in rd:
+            readers.setdefault(k, []).append(i)
+        for k in wr:
+            writer[k] = i
+            readers[k] = []
+    last = {p: [] for p in POOLS}
+    mark = {}
+    for i, (q, fn, rd, wr, kind) in enumerate(ops):
+        if q == "x":
+            mark[i] = fn
+            continue
+        for d in waits[i]:
+            queue[q].wait_ge(T.sem[mark[d][0]], mark[d][1])
+        if fn is None:
+            continue
+        ins = fn(queue[q])
+        members = sets.get(kind, [i])
+        end = members[-1]
+        if end not in needed:
+            continue
+        p = "d" if kind == "dma" else q
+        step = 16 if kind == "dma" else 1
+        if i == members[0]:
+            free = [n for n, (j, c) in enumerate(last[p]) if j in before[i]]
+            if free:
+                n = free[0]
+            else:
+                n = len(last[p])
+                assert n < POOLS[p], "out of semaphores: " + p
+                last[p].append((i, 0))
+            last[p][n] = (end, last[p][n][1] + step * len(members))
+            mark[end] = ("%s%d" % (p, n), last[p][n][1])
+        ins.then_inc(T.sem[mark[end][0]], step)
+
+
+def rank_program(g, core, T, topo):
+    rank = T.rank_of(core)
+    if rank is None:
+        hand_on(g, core, T, topo)
+        return
+    n_ranks = len(T.cores)
+    ops = []
+
+    def op(q, fn, rd, wr, kind=""):
+        ops.append((q, fn, list(rd), list(wr), kind))
+
+    def dma(q, out, in_, rd, wr):
+        op(q, lambda e: e.dma_start(out, in_), rd, wr, "dma")
+
+    def ts(out, in0, s1, o0, rd, wr, s2=None, o1=None, kind=""):
+        if o1 is None:
+            op("v", lambda e: e.tensor_scalar(out, in0, s1, None, o0), rd, wr, kind)
+        else:
+            op("v", lambda e: e.tensor_scalar(out, in0, s1, s2, o0, o1), rd, wr, kind)
+
+    def tt(out, a, b, o, rd, wr, kind=""):
+        op("v", lambda e: e.tensor_tensor(out, a, b, o), rd, wr, kind)
+
+    def scan(out, a, b, init, o0, o1, rd, wr, kind=""):
+        op("v", lambda e: e.tensor_tensor_scan(out, a, b, init, o0, o1), rd, wr, kind)
+
+    def copy(out, in_, rd, wr, kind=""):
+        op("v", lambda e: e.tensor_copy(out, in_), rd, wr, kind)
+
+    def act(out, in_, f, rd, wr, kind="", **kw):
+        op("s", lambda e: e.activation(out, in_, f, **kw), rd, wr, kind)
+
+    def fill(ap, c, wr):
+        op("v", lambda e: e.memset(ap, c), [], wr)
+
+    def quant(q, s, in_, rd, wr, kind=""):
+        op("v", lambda e: e.quantize_mx(q, s, in_), rd, wr, kind)
+
+    def mm(bank, n, lq, ls, rq, rs, rd, start=True, stop=True):
+        op("t", lambda e: e.matmul_mx(T["p%d" % bank][:, 0:n], lq, ls, rq, rs, start, stop), rd, ["#%d" % bank],
+           "" if start else "acc")
+
+    def iota(out, pattern, base, cm, wr, small=False):
+        if small:
+            op("g", lambda e: e.iota(out, pattern, base, cm, allow_small_or_imprecise_dtypes=True), [], wr)
+        else:
+            op("g", lambda e: e.iota(out, pattern, base, cm), [], wr)
+
+    dst, cq, cs = route(T, topo, rank)
+    prev = (rank - 1) % n_ranks
+    _, pq, ps = route(T, topo, prev)
+    if pq is None:
+        ea, eb = halves(topo, T.cores[prev], core)
+        nq, ns = len(ea), len(eb)
+    else:
+        nq, ns = len(topo.engines(pq, core)), len(topo.engines(ps, core))
+    sent = [0]
+
+    def send(out, in_, sem, to, half, rd):
+        eng = halves(topo, core, to)[half]
+        rid, pid = topo.addr(to, core)
+        sent[0] += len(eng)
+        op("g", lambda e: e.remote_dma(out, in_, T.sem[sem], T.sem.sent, pid, rid, bits(eng)), rd, [])
+
+    for t in range(R):
+        op("x", ("aq%d" % t, nq), [], ["lq%d" % t])
+        op("x", ("as%d" % t, ns), [], ["ls%d" % t])
+    op("x", ("al", ns), [], ["larr"])
+
+    X = [T.x0, T.x1, T.x2]
+    XK = [["x0"] * 4, ["x1_%d" % b for b in range(4)], ["x2_%d" % b for b in range(4)]]
+    Lr, Nr, Ar = 0, 336, 672
+
+    dma("y", T.ut[:], T.u[:], [], ["ut"])
+    dma("s", T.x0[:, 0:4 * C], T.x[:], [], ["x0"])
+    dma("y", T.wq[:].bitcast(dt.uint8), T.wc[:], ["x0"], ["wq"])
+    dma("y", T.zq[:].bitcast(dt.uint8), T.zc[:], [], ["zq"])
+    dma("y", T.wp[:], T.ws[:], [], ["wp"])
+    dma("y", T.zp[:], T.zs[:], [], ["zp"])
+    dma("y", T.vt[:], T.v[:], [], ["vt"])
+
+    fill(T.idn[:], 1.0, ["idn"])
+    iota(T.iu[:, 0:8], [[16, 8]], 0, 0, ["iu0"])
+    op("g", lambda e: e.affine_select(T.idn[:], T.idn[:], [[-1, 128]], A.is_equal, 0.0, 0, 1), ["idn"], ["idn"])
+    iota(T.iu[:, 8:24], [[16, 2], [32, 4], [0, 2]], 0, 0, ["iu1"])
+    iota(T.qi[:, 0:1], [[0, 1]], 0, 1, ["qi0"])
+    iota(T.kk[:], [[16, NPIV]], 0, 0, ["kk"], True)
+    iota(T.jm[:], [[0, NPIV], [1, 16]], 0, 0, ["jm"], True)
+    iota(T.cval[:], [[1, C]], -192, 0, ["cval"], True)
+    iota(T.olw[:, 0:C], [[1, C]], 0, 0, ["olw0"], True)
+    fill(T.ew[:], 0.0, ["ew"])
+    fill(T.bt[:, 256:768], 0.0, ["btz"])
+    fill(T.zz[:], 0.0, ["zz0", "zz1"])
+    fill(T.rows[:, 0::336], 0.0, ["rows0"])
+    copy(T.ew[:, 3:515:4], T.idn[:], ["idn"], ["ew"])
+    quant(T.lq[:, 64:192], T.ls[:, 64:192], T.bt[:, 256:768], ["btz"], ["lz"], "+e")
+    fill(T.er[:], 128.0, ["er0", "er1"])
+    for b in range(4):
+        quant(T.eq4[:, 128 * b:128 * b + 128], T.es4[:, 128 * b:128 * b + 128], T.ew[:, 3 - b:515 - b], ["ew"], ["e%d" % b], "+e")
+    copy(T.offu[:], T.iu[:], ["iu0", "iu1"], ["offu"])
+    ts(T.qi[:, 1:2], T.qi[:, 0:1], 15, A.bitwise_and, ["qi0"], ["qi1"])
+    quant(T.uq[:], T.us[:], T.ut[:], ["ut"], ["uq"])
+    copy(T.qf[:], T.qi[:, 1:2], ["qi1"], ["qf"])
+    copy(T.u3q[:].bitcast(dt.uint32), T.uq[:].bitcast(dt.uint32).indirect(T.offu[:]), ["uq", "offu"], ["u3q"])
+    act(T.u3s[:], T.us[:].indirect(T.offu[:]), F.Copy, ["uq", "offu"], ["u3s"])
+    act(T.kq[:], T.kk[:], F.Identity, ["kk", "qf"], ["kq"], bias=T.qf[:])
+    act(T.twoc[:], T.kq[:], F.Copy, ["kq"], ["twoc"], "+k", scale=2.0)
+    act(T.thr[:], T.kq[:, 0:4], F.Copy, ["kq"], ["thr"], "+k")
+    act(T.thrh[:], T.kq[:, 3:4], F.Identity, ["kq"], ["thrh"], "+k", bias=0.5)
+
+    def useg(i):
+        return T.u3q[:, 128 * i:128 * i + 128], T.u3s[:, 128 * i:128 * i + 128]
+
+    ends = T.cnt[:, H - 1::H]
+    cnts = ["cnt%d" % k for k in range(NPIV)]
+
+    def count(k, t):
+        scan(T.cnt[:, H * k:H * k + H], T.msk[:, C * k:C * k + H], T.msk[:, C * k + H:C * k + C], -256.0, A.add, A.add,
+             ["m%d" % k], ["cnt%d" % k], "+cnt%d" % t)
+
+    def cut(side, limit, row):
+        c = T.cut[:, NPIV * side:NPIV * side + NPIV]
+        z = T.zz[:, C * side:C * side + C]
+        ts(c, ends, float(limit), A.is_ge, cnts, ["cut%d" % side], -512.0, A.mult)
+        tt(T.zz[:, C * side:C * side + C:16], ends, c, A.min, cnts + ["cut%d" % side], ["zz%d" % side])
+        scan(T.yb[:], T.chold[:], z, 0.0, A.mult, A.add, ["chold", "zz%d" % side], ["yb"])
+        op("v", lambda e: e.transpose(T.yr[:], T.yb[:]), ["yb"], ["yr"])
+        act(T.wr[:], T.yr[:], F.Relu, ["yr"], ["wr"], bias=-1.0, scale=-1.0 / 256)
+        scan(T.mx[:], T.yr[:, 0:H], T.yr[:, H:C], -1024.0, A.max, A.max, ["yr"], ["mx"])
+        top = T.mx[:, H - 1:H]
+        ts(T.eq[:], T.yr[:], top, A.is_equal, ["yr", "mx"], ["eq"])
+        if limit:
+            ts(T.nn[:], top, float(-limit), A.add, ["mx"], ["nn"])
+            scan(T.vr[:], T.eq[:], T.wr[:], T.nn[:], A.add, A.add, ["eq", "wr", "nn"], ["vr"])
+        else:
+            scan(T.vr[:], T.eq[:], T.wr[:], top, A.add, A.add, ["eq", "wr", "mx"], ["vr"])
+        scan(T.rows[:, row + 1:row + 1 + C], T.wr[:], T.vr[:], 0.0, A.add, A.max, ["wr", "vr"], ["row%d" % row])
+
+    def select(slot, row, rd, kind=""):
+        scan(T.sel[:, C * slot:C * slot + C], T.csel[:], row, 0.0, A.add, A.min, ["csel"] + rd, ["sel%d" % slot], kind)
+
+    def picked(slot):
+        return T.sel[:, C * slot + 15:C * slot + C:16]
+
+    def sm(i):
+        return T.sm[:, NPIV * i:NPIV * i + NPIV]
+
+    for t in range(R):
+        x, xk = X[t], XK[t]
+        last = t == R - 1
+        quant(T.xq[:], T.xs[:], x[:, 0:4 * C], xk, ["xq"])
+        for bank, i in ((0, 0), (1, 1), (2, 2), (3, 2)):
+            a, b = useg(i)
+            mm(bank, C, a, b, T.xq[:], T.xs[:], ["u3q", "u3s", "xq"])
+        if t == 0:
+            ts(T.chold[:], T.jm[:], 0.0, A.is_gt, ["jm"], ["chold"])
+        op("v", lambda e: e.transpose(T.tt[:, 0:64], T.p0[:, 0:64]), ["#0"], ["tta"])
+        op("v", lambda e: e.transpose(T.tt[:, 64:C], T.p0[:, 64:C]), ["#0"], ["ttb"])
+
+        def tk(k):
+            return "tta" if 16 * k < 64 else "ttb"
+
+        theirs = [k for k in range(NPIV) if k % 2 == 0] + [k for k in range(NPIV) if k % 2 and k not in OWN]
+        for k in theirs:
+            bank = 3 if k % 2 else 1
+            act(T.msk[:, C * k:C * k + C], T["p%d" % bank][:, 0:C], F.Sign, ["#%d" % bank, tk(k)], ["m%d" % k],
+                bias=T.tt[:, 16 * k:16 * k + 1], scale=-1.0)
+        if t == 0:
+            act(T.csel[:], T.jm[:], F.Abs, ["jm", "qf"], ["csel"], bias=T.qf[:], scale=-1.0)
+            act(T.csel[:], T.csel[:], F.Relu, ["csel"], ["csel"], bias=1024.0, scale=-1024.0)
+
+        def own(k):
+            ts(T.msk[:, C * k:C * k + C], T.p2[:, 0:C], T.tt[:, 16 * k:16 * k + 1], A.is_gt, ["#2", tk(k)], ["m%d" % k])
+
+        def flags(k):
+            m = T.msk[:, C * k:C * k + C]
+            ts(m, m, 0.0, A.is_lt, ["m%d" % k], ["m%d" % k])
+
+        mine, other, done = list(OWN), list(theirs), []
+        for s in PLAN.split():
+            k = (mine if s == "o" else other).pop(0)
+            (own if s == "o" else flags)(k)
+            if done:
+                count(done.pop(0), t)
+            done.append(k)
+        count(done.pop(0), t)
+
+        cut(0, 0, Lr)
+        lrow = T.rows[:, Lr + 1:Lr + 1 + C]
+        act(T.lm[:, 3 * C:4 * C], lrow, F.Sign, ["row0", "thrh"], ["lm3"], bias=T.thrh[:], scale=-1.0)
+        for k in range(3):
+            ts(T.lm[:, C * k:C * k + C], lrow, T.thr[:, k:k + 1], A.is_le, ["row0", "thr"], ["lm%d" % k], 2.0, A.mult)
+        for k in range(4):
+            scan(T.lc[:, H * k:H * k + H], T.lm[:, C * k:C * k + H], T.lm[:, C * k + H:C * k + C], 0.0 if k == 3 else -320.0,
+                 A.add, A.add, ["lm%d" % k], ["lc%d" % k], "+lc%d" % t)
+        lcs = ["lc%d" % k for k in range(4)]
+        lends = T.lc[:, H - 1::H]
+        b0 = 0 if t == 0 else 768
+        for j in (2, 3, 0, 1):
+            ts(T.offb[:, 4 * j:4 * j + 4], lends, 2.0, A.mult, lcs, ["offb%d" % j], float(640 + j), A.add)
+        for j in (2, 0, 3, 1):
+            o, i = T.bt[:, b0 + j:b0 + 4 * K:4], x[:, 0:4 * C].indirect(T.offb[:, 4 * j:4 * j + 4])
+            if j >= 2:
+                act(o, i, F.Copy, xk + ["offb%d" % j], ["bt%d_%d" % (t, j)], "+bs%d" % t)
+            else:
+                copy(o, i, xk + ["offb%d" % j], ["bt%d_%d" % (t, j)], "+bv%d" % t)
+        bq, bs = T["bq%d" % t], T["bs%d" % t]
+        quant(bq[:], bs[:], T.bt[:, 512 * t:512 * t + 512], ["btz"] + ["bt%d_%d" % (t, j) for j in range(4)], ["bq%d" % t])
+        c0 = K * t
+        lq, ls = land(T, t)
+        src_q, src_s = bq[:, c0:c0 + K].bitcast(dt.uint8), bs[:, c0:c0 + K]
+        if cq is None:
+            send(lq, src_q, "aq%d" % t, dst, 0, ["bq%d" % t])
+            send(ls, src_s, "as%d" % t, dst, 1, ["bq%d" % t])
+        else:
+            send(T["rq%d" % t][:].bitcast(dt.uint8), src_q, "aq%d" % t, cq, 0, ["bq%d" % t])
+            send(T["rs%d" % t][:], src_s, "as%d" % t, cs, 1, ["bq%d" % t])
+        if last:
+            ts(T.offl[:], lends, 0.5, A.mult, lcs, ["offl"], 160.0, A.add)
+            if cq is None:
+                send(T.larr[:], T.offl[:], "al", dst, 1, ["offl"])
+            else:
+                send(T.rl[:], T.offl[:], "al", cs, 1, ["offl"])
+
+        cut(1, -192, Nr)
+        select(0, T.rows[:, Lr:Lr + C], ["row0", "rows0"])
+        select(1, T.rows[:, Lr + 1:Lr + 1 + C], ["row0"])
+        select(2, T.rows[:, Nr:Nr + C], ["row336", "rows0"])
+        ts(sm(0), picked(0), 383.0, A.mult, ["sel0"], ["sm0"], kind="+a%d" % t)
+        ts(sm(1), picked(1), 384.0, A.mult, ["sel1"], ["sm1"], -64.0, A.add, "+a%d" % t)
+        tt(sm(2), picked(0), picked(2), A.add, ["sel0", "sel2"], ["sm2"])
+        tt(sm(3), sm(1), sm(0), A.subtract, ["sm0", "sm1"], ["sm3"], "+b%d" % t)
+        tt(sm(4), T.twoc[:], sm(2), A.subtract, ["twoc", "sm2"], ["sm4"], "+b%d" % t)
+        tt(sm(5), sm(3), sm(4), A.max, ["sm3", "sm4"], ["sm5"])
+        copy(T.offd[:], sm(5), ["sm5"], ["offd"])
+        e0 = (C + K) * t
+        copy(T.er[:, e0:e0 + C + K].indirect(T.offd[:]), T.cval[:], ["cval", "offd"], ["er%d" % t])
+        ts(T.eq[:], T.er[:, e0:e0 + C], 127.5, A.is_gt, ["er%d" % t], ["eq"])
+        select(2, T.er[:, e0:e0 + C], ["er%d" % t])
+        scan(T.rows[:, Ar + 1:Ar + 1 + C], T.eq[:], T.eq[:], 0.0, A.add, A.max, ["eq"], ["row672"])
+        ts(sm(2), picked(2), 4.0, A.mult, ["sel2"], ["sm2"], 768.0, A.add)
+        select(0, T.rows[:, Ar:Ar + C], ["row672", "rows0"])
+        select(1, T.rows[:, Ar + 1:Ar + 1 + C], ["row672"])
+        ts(sm(0), picked(0), 1532.0, A.mult, ["sel0"], ["sm0"], kind="+c%d" % t)
+        ts(sm(1), picked(1), 1536.0, A.mult, ["sel1"], ["sm1"], -256.0, A.add, "+c%d" % t)
+        tt(sm(3), sm(1), sm(0), A.subtract, ["sm0", "sm1"], ["sm3"])
+        tt(sm(5), sm(3), sm(2), A.max, ["sm3", "sm2"], ["sm5"])
+        for j in (2, 3, 0, 1):
+            ts(T.offt[:, NPIV * j:NPIV * j + NPIV], sm(5), float(j), A.add, ["sm5"], ["offt%d" % j])
+
+        m0 = 128 * t
+        for b in range(4):
+            mm(4 + b, 128, T.eq4[:, 128 * b:128 * b + 128], T.es4[:, 128 * b:128 * b + 128], T.lq[:, m0:m0 + 128],
+               T.ls[:, m0:m0 + 128], ["e%d" % b, "lz", "lq%d" % t, "ls%d" % t])
+        for b in range(4):
+            act(x[:, 4 * C + b:4 * (C + K):4], T["p%d" % (4 + b)][:, c0:c0 + K], F.Copy, ["#%d" % (4 + b)],
+                ["ar%d_%d" % (t, b)], "+ar%d" % t)
+
+        for j in (2, 0, 3, 1):
+            o, i = T.tb[:, j:4 * C:4], x[:].indirect(T.offt[:, NPIV * j:NPIV * j + NPIV])
+            rd = xk + ["ar%d_%d" % (t, b) for b in range(4)] + ["offt%d" % j]
+            if j >= 2:
+                act(o, i, F.Copy, rd, ["tb%d" % j], "+ts%d" % t)
+            else:
+                copy(o, i, rd, ["tb%d" % j], "+tv%d" % t)
+        tbs = ["tb%d" % j for j in range(4)]
+        act(T.tb[:, 4 * C:4 * C + 4], T.tb[:, 0:4], F.Copy, tbs, ["tbw"])
+        quant(T.tq[:], T.ts[:], T.tb[:, 0:4 * C], tbs, ["tq"])
+        if last:
+            ts(T.offe[:], sm(5), 0.25, A.mult, ["sm5"], ["offe"])
+        quant(T.t2q[:], T.t2s[:], T.tb[:, 4:4 * C + 4], tbs + ["tbw"], ["t2q"])
+        if t == 0:
+            quant(T.vq[:], T.vs[:], T.vt[:], ["vt"], ["vq"])
+        if last:
+            act(T.olw[:, C:C + K], T.olw[:, 0:C].indirect(T.larr[:]), F.Identity, ["olw0", "larr"], ["olw1"], bias=float(C))
+            act(T.olr[:], T.olw[:].indirect(T.offe[:]), F.Copy, ["olw0", "olw1", "offe"], ["olr"])
+            dma("y", T.ol[:], T.olr[0:128:16, :], ["olr"], ["o3"])
+        for w, b in ((1, 0), (1, 1), (1, 2), (0, 0), (0, 1), (0, 2), (1, 3), (0, 3)):
+            cols = slice(128 * b, 128 * b + 128)
+            if w:
+                mm(b, C, T.wq[:, cols], T.wp[:, cols], T.tq[:], T.ts[:], ["wq", "wp", "tq"], True, False)
+            else:
+                mm(b, C, T.zq[:, cols], T.zp[:, cols], T.t2q[:], T.t2s[:], ["zq", "zp", "t2q"], False, True)
+        for b in range(4):
+            o, i = X[t + 1][:, b:4 * C:4], T["p%d" % b][:, 0:C]
+            if b % 2 == 0:
+                act(o, i, F.Copy, ["#%d" % b], [XK[t + 1][b]], "+xs%d" % t, scale=0.015625)
+            else:
+                ts(o, i, 0.015625, A.mult, ["#%d" % b], [XK[t + 1][b]], kind="+xv%d" % t)
+
+    for h in range(2):
+        quant(T.xq[:, H * h:H * h + H], T.xs[:, H * h:H * h + H], T.x2[:, 4 * H * h:4 * H * (h + 1)], XK[2],
+              ["xq", "fq0"] if h == 0 else ["fq1"])
+        mm(4 + h, H, T.vq[:], T.vs[:], T.xq[:, H * h:H * h + H], T.xs[:, H * h:H * h + H], ["vq", "fq%d" % h])
+    both = ["fq0", "fq1"]
+    dma("y", T.oc[:], T.xq[:].bitcast(dt.uint8), both, ["o0"])
+    for k in range(4):
+        dma("y" if k < 2 else "s", T.osc[4 * k:4 * k + 4, :], T.xs[32 * k:32 * k + 4, :], both, ["o1_%d" % k])
+    copy(T.yo[:, 0:H], T.p4[:, 0:H], ["#4"], ["yo0"], "+y")
+    copy(T.yo[:, H:C], T.p5[:, 0:H], ["#5"], ["yo1"], "+y")
+    dma("y", T.y[:], T.yo[:], ["yo0", "yo1"], ["o2"])
+    op("y", None, ["o0", "o2", "o3"] + ["o1_%d" % k for k in range(4)], [])
+    emit(g, T, ops)
+    g.wait_ge(T.sem.sent, sent[0])

@@ -3,8 +3,7 @@ from concourse.mybir import dt, AluOpType as A, ActivationFunctionType as F
 C, K, R = 320, 64, 2
 Q4, U8, BF, FP, I32, U16 = "float8_e4m3fn_x4", "uint8", "bfloat16", "float32", "int32", "uint16"
 NPIV = C // 16
-OWN = (1, 3, 5, 7, 9, 11)
-PLAN = "o o f f o f f o f f o f f o f f f f f f"
+NS = 7
 H = C // 2
 
 
@@ -18,9 +17,10 @@ SCRATCH = {
     "wq": sb(512, Q4), "wp": sb(512, U8), "zq": sb(512, Q4), "zp": sb(512, U8),
     "x0": sb(4 * (C + K), BF), "x1": sb(4 * (C + K), BF), "x2": sb(4 * C, BF),
     "xq": sb(C, Q4), "xs": sb(C, U8),
-    "tt": sb(C, FP), "msk": sb(NPIV * C, BF), "cnt": sb(NPIV * H, BF),
+    "tt": sb(C, FP), "msk": sb(NPIV * C, BF), "cnt": sb(NPIV * H, BF), "gsum": sb(NS, FP),
     "zz": sb(2 * C, BF), "rows": sb(3 * 336, BF), "cut": sb(2 * NPIV, BF),
-    "yb": sb(C, BF), "yr": sb(C, BF), "wr": sb(C, BF), "eq": sb(C, BF), "vr": sb(C, BF), "mx": sb(H, BF), "nn": sb(1, FP),
+    "yb": sb(2 * C, BF), "yr": sb(2 * C, BF), "wr": sb(2 * C, BF), "eq": sb(2 * C, BF), "vr": sb(2 * C, BF),
+    "mx": sb(2 * H, BF), "nn": sb(1, FP),
     "lm": sb(4 * C, BF), "lc": sb(4 * H, BF),
     "sel": sb(3 * C, BF), "sm": sb(6 * NPIV, FP), "er": sb(2 * (C + K), BF),
     "offb": sb(16, U16), "offt": sb(4 * NPIV, U16), "offd": sb(NPIV, U16), "offe": sb(NPIV, U16), "offu": sb(24, U16),
@@ -279,27 +279,31 @@ def rank_program(g, core, T, topo):
     ends = T.cnt[:, H - 1::H]
     cnts = ["cnt%d" % k for k in range(NPIV)]
 
-    def count(k, t):
-        scan(T.cnt[:, H * k:H * k + H], T.msk[:, C * k:C * k + H], T.msk[:, C * k + H:C * k + C], -256.0, A.add, A.add,
-             ["m%d" % k], ["cnt%d" % k], "+cnt%d" % t)
+    def cut(s, limit, row):
+        def k(name):
+            return "%s%d" % (name, s)
 
-    def cut(side, limit, row):
-        c = T.cut[:, NPIV * side:NPIV * side + NPIV]
-        z = T.zz[:, C * side:C * side + C]
-        ts(c, ends, float(limit), A.is_ge, cnts, ["cut%d" % side], -512.0, A.mult)
-        tt(T.zz[:, C * side:C * side + C:16], ends, c, A.min, cnts + ["cut%d" % side], ["zz%d" % side])
-        scan(T.yb[:], T.chold[:], z, 0.0, A.mult, A.add, ["chold", "zz%d" % side], ["yb"])
-        op("v", lambda e: e.transpose(T.yr[:], T.yb[:]), ["yb"], ["yr"])
-        act(T.wr[:], T.yr[:], F.Relu, ["yr"], ["wr"], bias=-1.0, scale=-1.0 / 256)
-        scan(T.mx[:], T.yr[:, 0:H], T.yr[:, H:C], -1024.0, A.max, A.max, ["yr"], ["mx"])
-        top = T.mx[:, H - 1:H]
-        ts(T.eq[:], T.yr[:], top, A.is_equal, ["yr", "mx"], ["eq"])
-        if limit:
-            ts(T.nn[:], top, float(-limit), A.add, ["mx"], ["nn"])
-            scan(T.vr[:], T.eq[:], T.wr[:], T.nn[:], A.add, A.add, ["eq", "wr", "nn"], ["vr"])
-        else:
-            scan(T.vr[:], T.eq[:], T.wr[:], top, A.add, A.add, ["eq", "wr", "mx"], ["vr"])
-        scan(T.rows[:, row + 1:row + 1 + C], T.wr[:], T.vr[:], 0.0, A.add, A.max, ["wr", "vr"], ["row%d" % row])
+        def w(buf, n=C):
+            return buf[:, n * s:n * s + n]
+
+        c, top = w(T.cut, NPIV), T.mx[:, H * s + H - 1:H * s + H]
+        first = (T.nn[:], "nn") if limit else (top, k("mx"))
+        return {
+            "c": lambda: ts(c, ends, float(limit), A.is_ge, cnts, [k("cut")], -512.0, A.mult),
+            "z": lambda: tt(T.zz[:, C * s:C * s + C:16], ends, c, A.min, cnts + [k("cut")], [k("zz")]),
+            "spread": lambda: scan(w(T.yb), T.chold[:], w(T.zz), 0.0, A.mult, A.add, ["chold", k("zz")], [k("yb")]),
+            "turn": lambda: op("v", lambda e: e.transpose(w(T.yr), w(T.yb)), [k("yb")], [k("yr")]),
+            "out": lambda: act(w(T.wr), w(T.yr), F.Relu, [k("yr")], [k("wr")], bias=-1.0, scale=-1.0 / 256),
+            "top": lambda: scan(w(T.mx, H), T.yr[:, C * s:C * s + H], T.yr[:, C * s + H:C * s + C], -1024.0, A.max, A.max,
+                                [k("yr")], [k("mx")]),
+            "eq": lambda: ts(w(T.eq), w(T.yr), top, A.is_equal, [k("yr"), k("mx")], [k("eq")]),
+            "n": lambda: ts(T.nn[:], top, float(-limit), A.add, [k("mx")], ["nn"]),
+            "v": lambda: scan(w(T.vr), w(T.eq), w(T.wr), first[0], A.add, A.add, [k("eq"), k("wr"), first[1]], [k("vr")]),
+            "run": lambda: scan(T.rows[:, row + 1:row + 1 + C], w(T.wr), w(T.vr), 0.0, A.add, A.max, [k("wr"), k("vr")],
+                                ["row%d" % row]),
+        }
+
+    lo, hi = cut(0, 0, Lr), cut(1, -192, Nr)
 
     def select(slot, row, rd, kind=""):
         scan(T.sel[:, C * slot:C * slot + C], T.csel[:], row, 0.0, A.add, A.min, ["csel"] + rd, ["sel%d" % slot], kind)
@@ -310,11 +314,14 @@ def rank_program(g, core, T, topo):
     def sm(i):
         return T.sm[:, NPIV * i:NPIV * i + NPIV]
 
+    def mrow(k):
+        return T.msk[:, C * k:C * k + C]
+
     for t in range(R):
         x, xk = X[t], XK[t]
         last = t == R - 1
         quant(T.xq[:], T.xs[:], x[:, 0:4 * C], xk, ["xq"])
-        for bank, i in ((0, 0), (1, 1), (2, 2), (3, 2)):
+        for bank, i in ((0, 0), (1, 1), (2, 2), (3, 1)):
             a, b = useg(i)
             mm(bank, C, a, b, T.xq[:], T.xs[:], ["u3q", "u3s", "xq"])
         if t == 0:
@@ -325,39 +332,48 @@ def rank_program(g, core, T, topo):
         def tk(k):
             return "tta" if 16 * k < 64 else "ttb"
 
-        theirs = [k for k in range(NPIV) if k % 2 == 0] + [k for k in range(NPIV) if k % 2 and k not in OWN]
-        for k in theirs:
-            bank = 3 if k % 2 else 1
-            act(T.msk[:, C * k:C * k + C], T["p%d" % bank][:, 0:C], F.Sign, ["#%d" % bank, tk(k)], ["m%d" % k],
-                bias=T.tt[:, 16 * k:16 * k + 1], scale=-1.0)
+        for i in range(NS + 1):
+            if i < NS:
+                k = 2 * i
+                act(mrow(k), T.p1[:, 0:C], F.Sign, ["#1", tk(k)], ["m%d" % k], bias=T.tt[:, 16 * k:16 * k + 1], scale=-1.0)
+            if i > 0:
+                k = 2 * i - 2
+                act(mrow(k), mrow(k), F.Relu, ["m%d" % k], ["m%d" % k, "gs%d" % k], "+gs%d" % t, scale=-1.0,
+                    accum_out=T.gsum[:, i - 1:i])
+        act(T.cnt[:, H - 1:2 * H * NS:2 * H], T.gsum[:], F.Identity, ["gs%d" % (2 * i) for i in range(NS)],
+            ["cnt%d" % (2 * i) for i in range(NS)], bias=-256.0)
         if t == 0:
             act(T.csel[:], T.jm[:], F.Abs, ["jm", "qf"], ["csel"], bias=T.qf[:], scale=-1.0)
-            act(T.csel[:], T.csel[:], F.Relu, ["csel"], ["csel"], bias=1024.0, scale=-1024.0)
+        mine = [k for k in range(NPIV) if k % 2] + [k for k in range(2 * NS, NPIV, 2)]
+        for i in range(len(mine) + 1):
+            if i < len(mine):
+                k = mine[i]
+                bank = 2 if k % 2 else 3
+                ts(mrow(k), T["p%d" % bank][:, 0:C], T.tt[:, 16 * k:16 * k + 1], A.is_gt, ["#%d" % bank, tk(k)], ["m%d" % k])
+            if i > 0:
+                k = mine[i - 1]
+                scan(T.cnt[:, H * k:H * k + H], T.msk[:, C * k:C * k + H], T.msk[:, C * k + H:C * k + C], -256.0, A.add,
+                     A.add, ["m%d" % k], ["cnt%d" % k], "+cnt%d" % t)
 
-        def own(k):
-            ts(T.msk[:, C * k:C * k + C], T.p2[:, 0:C], T.tt[:, 16 * k:16 * k + 1], A.is_gt, ["#2", tk(k)], ["m%d" % k])
-
-        def flags(k):
-            m = T.msk[:, C * k:C * k + C]
-            ts(m, m, 0.0, A.is_lt, ["m%d" % k], ["m%d" % k])
-
-        mine, other, done = list(OWN), list(theirs), []
-        for s in PLAN.split():
-            k = (mine if s == "o" else other).pop(0)
-            (own if s == "o" else flags)(k)
-            if done:
-                count(done.pop(0), t)
-            done.append(k)
-        count(done.pop(0), t)
-
-        cut(0, 0, Lr)
+        for step in ("c", "z", "spread", "turn", "out", "top"):
+            lo[step]()
+            hi[step]()
+        lo["eq"]()
+        hi["n"]()
+        lo["v"]()
+        hi["eq"]()
+        lo["run"]()
+        hi["v"]()
         lrow = T.rows[:, Lr + 1:Lr + 1 + C]
         act(T.lm[:, 3 * C:4 * C], lrow, F.Sign, ["row0", "thrh"], ["lm3"], bias=T.thrh[:], scale=-1.0)
+        if t == 0:
+            act(T.csel[:], T.csel[:], F.Relu, ["csel"], ["csel"], bias=1024.0, scale=-1024.0)
         for k in range(3):
             ts(T.lm[:, C * k:C * k + C], lrow, T.thr[:, k:k + 1], A.is_le, ["row0", "thr"], ["lm%d" % k], 2.0, A.mult)
         for k in range(4):
             scan(T.lc[:, H * k:H * k + H], T.lm[:, C * k:C * k + H], T.lm[:, C * k + H:C * k + C], 0.0 if k == 3 else -320.0,
                  A.add, A.add, ["lm%d" % k], ["lc%d" % k], "+lc%d" % t)
+        hi["run"]()
         lcs = ["lc%d" % k for k in range(4)]
         lends = T.lc[:, H - 1::H]
         b0 = 0 if t == 0 else 768
@@ -369,6 +385,7 @@ def rank_program(g, core, T, topo):
                 act(o, i, F.Copy, xk + ["offb%d" % j], ["bt%d_%d" % (t, j)], "+bs%d" % t)
             else:
                 copy(o, i, xk + ["offb%d" % j], ["bt%d_%d" % (t, j)], "+bv%d" % t)
+        select(0, T.rows[:, Lr:Lr + C], ["row0", "rows0"])
         bq, bs = T["bq%d" % t], T["bs%d" % t]
         quant(bq[:], bs[:], T.bt[:, 512 * t:512 * t + 512], ["btz"] + ["bt%d_%d" % (t, j) for j in range(4)], ["bq%d" % t])
         c0 = K * t
@@ -380,29 +397,27 @@ def rank_program(g, core, T, topo):
         else:
             send(T["rq%d" % t][:].bitcast(dt.uint8), src_q, "aq%d" % t, cq, 0, ["bq%d" % t])
             send(T["rs%d" % t][:], src_s, "as%d" % t, cs, 1, ["bq%d" % t])
+
+        select(1, T.rows[:, Lr + 1:Lr + 1 + C], ["row0"])
+        select(2, T.rows[:, Nr:Nr + C], ["row336", "rows0"])
+        ts(sm(0), picked(0), 383.0, A.mult, ["sel0"], ["sm0"], kind="+a%d" % t)
+        tt(sm(2), T.twoc[:], picked(0), A.subtract, ["sel0", "twoc"], ["sm2"], "+a%d" % t)
+        ts(sm(1), picked(1), 384.0, A.mult, ["sel1"], ["sm1"], -64.0, A.add, "+a%d" % t)
         if last:
             ts(T.offl[:], lends, 0.5, A.mult, lcs, ["offl"], 160.0, A.add)
             if cq is None:
                 send(T.larr[:], T.offl[:], "al", dst, 1, ["offl"])
             else:
                 send(T.rl[:], T.offl[:], "al", cs, 1, ["offl"])
-
-        cut(1, -192, Nr)
-        select(0, T.rows[:, Lr:Lr + C], ["row0", "rows0"])
-        select(1, T.rows[:, Lr + 1:Lr + 1 + C], ["row0"])
-        select(2, T.rows[:, Nr:Nr + C], ["row336", "rows0"])
-        ts(sm(0), picked(0), 383.0, A.mult, ["sel0"], ["sm0"], kind="+a%d" % t)
-        ts(sm(1), picked(1), 384.0, A.mult, ["sel1"], ["sm1"], -64.0, A.add, "+a%d" % t)
-        tt(sm(2), picked(0), picked(2), A.add, ["sel0", "sel2"], ["sm2"])
+        tt(sm(4), sm(2), picked(2), A.subtract, ["sel2", "sm2"], ["sm4"], "+b%d" % t)
         tt(sm(3), sm(1), sm(0), A.subtract, ["sm0", "sm1"], ["sm3"], "+b%d" % t)
-        tt(sm(4), T.twoc[:], sm(2), A.subtract, ["twoc", "sm2"], ["sm4"], "+b%d" % t)
         tt(sm(5), sm(3), sm(4), A.max, ["sm3", "sm4"], ["sm5"])
         copy(T.offd[:], sm(5), ["sm5"], ["offd"])
         e0 = (C + K) * t
         copy(T.er[:, e0:e0 + C + K].indirect(T.offd[:]), T.cval[:], ["cval", "offd"], ["er%d" % t])
-        ts(T.eq[:], T.er[:, e0:e0 + C], 127.5, A.is_gt, ["er%d" % t], ["eq"])
+        ts(T.eq[:, 0:C], T.er[:, e0:e0 + C], 127.5, A.is_gt, ["er%d" % t], ["eq0"])
         select(2, T.er[:, e0:e0 + C], ["er%d" % t])
-        scan(T.rows[:, Ar + 1:Ar + 1 + C], T.eq[:], T.eq[:], 0.0, A.add, A.max, ["eq"], ["row672"])
+        scan(T.rows[:, Ar + 1:Ar + 1 + C], T.eq[:, 0:C], T.eq[:, 0:C], 0.0, A.add, A.max, ["eq0"], ["row672"])
         ts(sm(2), picked(2), 4.0, A.mult, ["sel2"], ["sm2"], 768.0, A.add)
         select(0, T.rows[:, Ar:Ar + C], ["row672", "rows0"])
         select(1, T.rows[:, Ar + 1:Ar + 1 + C], ["row672"])

@@ -5,6 +5,7 @@ Q4, U8, BF, FP, I32, U16 = "float8_e4m3fn_x4", "uint8", "bfloat16", "float32", "
 NPIV = C // 16
 NS = 7
 H = C // 2
+RUNS = ((0, H - 2), (H - 2, C))
 
 
 def sb(n, t):
@@ -21,7 +22,7 @@ SCRATCH = {
     "zz": sb(2 * C, BF), "rows": sb(3 * 336, BF), "cut": sb(2 * NPIV, BF),
     "yb": sb(2 * C, BF), "yr": sb(2 * C, BF), "wr": sb(2 * C, BF), "eq": sb(2 * C, BF), "vr": sb(2 * C, BF),
     "mx": sb(2 * H, BF), "nn": sb(1, FP),
-    "lm": sb(4 * C, BF), "lc": sb(4 * H, BF),
+    "lm": sb(4 * C, BF), "lc": sb(4 * H, FP),
     "sel": sb(3 * C, BF), "sm": sb(6 * NPIV, FP), "er": sb(2 * (C + K), BF),
     "offb": sb(16, U16), "offt": sb(4 * NPIV, U16), "offd": sb(NPIV, U16), "offe": sb(NPIV, U16), "offu": sb(24, U16),
     "offl": sb(4, U16), "larr": sb(4, U16), "rl": sb(4, U16),
@@ -31,13 +32,13 @@ SCRATCH = {
     "tb": sb(4 * C + 8, BF), "tq": sb(C, Q4), "ts": sb(C, U8), "t2q": sb(C, Q4), "t2s": sb(C, U8),
     "ew": sb(520, BF), "idn": sb(128, BF), "eq4": sb(512, Q4), "es4": sb(512, U8),
     "iu": sb(24, I32), "qi": sb(2, I32), "qf": sb(1, FP), "kk": sb(NPIV, FP), "kq": sb(NPIV, FP), "twoc": sb(NPIV, FP),
-    "thr": sb(4, BF), "thrh": sb(1, FP), "jm": sb(C, BF), "csel": sb(C, BF), "chold": sb(C, BF), "cval": sb(C, BF),
+    "thr": sb(4, BF), "thrh": sb(4, FP), "jm": sb(C, BF), "csel": sb(C, BF), "chold": sb(C, BF), "cval": sb(C, BF),
     "olw": sb(C + K, FP), "olr": sb(C, FP), "yo": sb(C, FP),
 }
 for _b in range(8):
     SCRATCH["p%d" % _b] = ("psum", [128, 512], FP)
 
-POOLS = {"v": 50, "s": 28, "t": 16, "g": 10, "d": 16}
+POOLS = {"v": 52, "s": 30, "t": 24, "g": 10, "d": 20}
 SEMAPHORES = ["aq0", "aq1", "as0", "as1", "al", "sent"] + ["%s%d" % (k, i) for k in POOLS for i in range(POOLS[k])]
 
 
@@ -233,8 +234,10 @@ def rank_program(g, core, T, topo):
     op("x", ("al", ns), [], ["larr"])
 
     X = [T.x0, T.x1, T.x2]
-    XK = [["x0"] * 4, ["x1_%d" % b for b in range(4)], ["x2_%d" % b for b in range(4)]]
     Lr, Nr, Ar = 0, 336, 672
+
+    def xkeys(t, h):
+        return ["x0"] if t == 0 else ["x%d_%d_%d" % (t, h, b) for b in range(4)]
 
     dma("y", T.ut[:], T.u[:], [], ["ut"])
     dma("s", T.x0[:, 0:4 * C], T.x[:], [], ["x0"])
@@ -244,10 +247,10 @@ def rank_program(g, core, T, topo):
     dma("y", T.zp[:], T.zs[:], [], ["zp"])
     dma("y", T.vt[:], T.v[:], [], ["vt"])
 
-    fill(T.idn[:], 1.0, ["idn"])
     iota(T.iu[:, 0:8], [[16, 8]], 0, 0, ["iu0"])
-    op("g", lambda e: e.affine_select(T.idn[:], T.idn[:], [[-1, 128]], A.is_equal, 0.0, 0, 1), ["idn"], ["idn"])
     iota(T.iu[:, 8:24], [[16, 2], [32, 4], [0, 2]], 0, 0, ["iu1"])
+    fill(T.idn[:], 1.0, ["idn"])
+    op("g", lambda e: e.affine_select(T.idn[:], T.idn[:], [[-1, 128]], A.is_equal, 0.0, 0, 1), ["idn"], ["idn"])
     iota(T.qi[:, 0:1], [[0, 1]], 0, 1, ["qi0"])
     iota(T.kk[:], [[16, NPIV]], 0, 0, ["kk"], True)
     iota(T.jm[:], [[0, NPIV], [1, 16]], 0, 0, ["jm"], True)
@@ -257,12 +260,10 @@ def rank_program(g, core, T, topo):
     fill(T.bt[:, 256:768], 0.0, ["btz"])
     fill(T.zz[:], 0.0, ["zz0", "zz1"])
     fill(T.rows[:, 0::336], 0.0, ["rows0"])
-    copy(T.ew[:, 3:515:4], T.idn[:], ["idn"], ["ew"])
-    quant(T.lq[:, 64:192], T.ls[:, 64:192], T.bt[:, 256:768], ["btz"], ["lz"], "+e")
     fill(T.er[:], 128.0, ["er0", "er1"])
-    for b in range(4):
-        quant(T.eq4[:, 128 * b:128 * b + 128], T.es4[:, 128 * b:128 * b + 128], T.ew[:, 3 - b:515 - b], ["ew"], ["e%d" % b], "+e")
     copy(T.offu[:], T.iu[:], ["iu0", "iu1"], ["offu"])
+    quant(T.lq[:, 64:192], T.ls[:, 64:192], T.bt[:, 256:768], ["btz"], ["lz"])
+    copy(T.ew[:, 3:515:4], T.idn[:], ["idn"], ["ew"])
     ts(T.qi[:, 1:2], T.qi[:, 0:1], 15, A.bitwise_and, ["qi0"], ["qi1"])
     quant(T.uq[:], T.us[:], T.ut[:], ["ut"], ["uq"])
     copy(T.qf[:], T.qi[:, 1:2], ["qi1"], ["qf"])
@@ -271,7 +272,10 @@ def rank_program(g, core, T, topo):
     act(T.kq[:], T.kk[:], F.Identity, ["kk", "qf"], ["kq"], bias=T.qf[:])
     act(T.twoc[:], T.kq[:], F.Copy, ["kq"], ["twoc"], "+k", scale=2.0)
     act(T.thr[:], T.kq[:, 0:4], F.Copy, ["kq"], ["thr"], "+k")
-    act(T.thrh[:], T.kq[:, 3:4], F.Identity, ["kq"], ["thrh"], "+k", bias=0.5)
+    act(T.thrh[:], T.kq[:, 0:4], F.Identity, ["kq"], ["thrh"], "+k", bias=0.5)
+    quant(T.xq[:], T.xs[:], T.x0[:, 0:4 * C], ["x0"], ["xq0", "xq1"])
+    for b in range(4):
+        quant(T.eq4[:, 128 * b:128 * b + 128], T.es4[:, 128 * b:128 * b + 128], T.ew[:, 3 - b:515 - b], ["ew"], ["e%d" % b], "+e")
 
     def useg(i):
         return T.u3q[:, 128 * i:128 * i + 128], T.u3s[:, 128 * i:128 * i + 128]
@@ -318,24 +322,26 @@ def rank_program(g, core, T, topo):
         return T.msk[:, C * k:C * k + C]
 
     for t in range(R):
-        x, xk = X[t], XK[t]
+        x, xk = X[t], xkeys(t, 0) + xkeys(t, 1)
         last = t == R - 1
-        quant(T.xq[:], T.xs[:], x[:, 0:4 * C], xk, ["xq"])
         for bank, i in ((0, 0), (1, 1), (2, 2), (3, 1)):
             a, b = useg(i)
-            mm(bank, C, a, b, T.xq[:], T.xs[:], ["u3q", "u3s", "xq"])
-        if t == 0:
-            ts(T.chold[:], T.jm[:], 0.0, A.is_gt, ["jm"], ["chold"])
+            mm(bank, C, a, b, T.xq[:], T.xs[:], ["u3q", "u3s", "xq0", "xq1"])
         op("v", lambda e: e.transpose(T.tt[:, 0:64], T.p0[:, 0:64]), ["#0"], ["tta"])
         op("v", lambda e: e.transpose(T.tt[:, 64:C], T.p0[:, 64:C]), ["#0"], ["ttb"])
 
         def tk(k):
             return "tta" if 16 * k < 64 else "ttb"
 
+        def sign(k):
+            act(mrow(k), T.p1[:, 0:C], F.Sign, ["#1", tk(k)], ["m%d" % k], bias=T.tt[:, 16 * k:16 * k + 1], scale=-1.0)
+
+        shared = 2 * NS
         for i in range(NS + 1):
             if i < NS:
-                k = 2 * i
-                act(mrow(k), T.p1[:, 0:C], F.Sign, ["#1", tk(k)], ["m%d" % k], bias=T.tt[:, 16 * k:16 * k + 1], scale=-1.0)
+                sign(2 * i)
+            if i == 3:
+                sign(shared)
             if i > 0:
                 k = 2 * i - 2
                 act(mrow(k), mrow(k), F.Relu, ["m%d" % k], ["m%d" % k, "gs%d" % k], "+gs%d" % t, scale=-1.0,
@@ -344,12 +350,19 @@ def rank_program(g, core, T, topo):
             ["cnt%d" % (2 * i) for i in range(NS)], bias=-256.0)
         if t == 0:
             act(T.csel[:], T.jm[:], F.Abs, ["jm", "qf"], ["csel"], bias=T.qf[:], scale=-1.0)
-        mine = [k for k in range(NPIV) if k % 2] + [k for k in range(2 * NS, NPIV, 2)]
+            act(T.csel[:], T.csel[:], F.Relu, ["csel"], ["csel"], bias=1024.0, scale=-1024.0)
+        mine = [k for k in range(NPIV) if k % 2] + [shared] + [k for k in range(shared + 2, NPIV, 2)]
         for i in range(len(mine) + 1):
             if i < len(mine):
                 k = mine[i]
                 bank = 2 if k % 2 else 3
-                ts(mrow(k), T["p%d" % bank][:, 0:C], T.tt[:, 16 * k:16 * k + 1], A.is_gt, ["#%d" % bank, tk(k)], ["m%d" % k])
+                if k == shared:
+                    ts(mrow(k), mrow(k), 0.0, A.is_lt, ["m%d" % k], ["m%d" % k])
+                else:
+                    ts(mrow(k), T["p%d" % bank][:, 0:C], T.tt[:, 16 * k:16 * k + 1], A.is_gt, ["#%d" % bank, tk(k)],
+                       ["m%d" % k])
+            elif t == 0:
+                ts(T.chold[:], T.jm[:], 0.0, A.is_gt, ["jm"], ["chold"])
             if i > 0:
                 k = mine[i - 1]
                 scan(T.cnt[:, H * k:H * k + H], T.msk[:, C * k:C * k + H], T.msk[:, C * k + H:C * k + C], -256.0, A.add,
@@ -365,27 +378,26 @@ def rank_program(g, core, T, topo):
         lo["run"]()
         hi["v"]()
         lrow = T.rows[:, Lr + 1:Lr + 1 + C]
-        act(T.lm[:, 3 * C:4 * C], lrow, F.Sign, ["row0", "thrh"], ["lm3"], bias=T.thrh[:], scale=-1.0)
-        if t == 0:
-            act(T.csel[:], T.csel[:], F.Relu, ["csel"], ["csel"], bias=1024.0, scale=-1024.0)
-        for k in range(3):
+        for k in (2, 3):
+            act(T.lm[:, C * k:C * k + C], lrow, F.Sign, ["row0", "thrh"], ["lm%d" % k, "lc%d" % k], "+ld%d" % t,
+                bias=T.thrh[:, k:k + 1], scale=-1.0, accum_out=T.lc[:, H * k + H - 1:H * k + H])
+        for k in range(2):
             ts(T.lm[:, C * k:C * k + C], lrow, T.thr[:, k:k + 1], A.is_le, ["row0", "thr"], ["lm%d" % k], 2.0, A.mult)
-        for k in range(4):
-            scan(T.lc[:, H * k:H * k + H], T.lm[:, C * k:C * k + H], T.lm[:, C * k + H:C * k + C], 0.0 if k == 3 else -320.0,
+        for k in range(2):
+            scan(T.lc[:, H * k:H * k + H], T.lm[:, C * k:C * k + H], T.lm[:, C * k + H:C * k + C], -320.0,
                  A.add, A.add, ["lm%d" % k], ["lc%d" % k], "+lc%d" % t)
         hi["run"]()
         lcs = ["lc%d" % k for k in range(4)]
         lends = T.lc[:, H - 1::H]
         b0 = 0 if t == 0 else 768
-        for j in (2, 3, 0, 1):
+        for j in range(4):
             ts(T.offb[:, 4 * j:4 * j + 4], lends, 2.0, A.mult, lcs, ["offb%d" % j], float(640 + j), A.add)
-        for j in (2, 0, 3, 1):
-            o, i = T.bt[:, b0 + j:b0 + 4 * K:4], x[:, 0:4 * C].indirect(T.offb[:, 4 * j:4 * j + 4])
-            if j >= 2:
-                act(o, i, F.Copy, xk + ["offb%d" % j], ["bt%d_%d" % (t, j)], "+bs%d" % t)
-            else:
-                copy(o, i, xk + ["offb%d" % j], ["bt%d_%d" % (t, j)], "+bv%d" % t)
+        for j in range(4):
+            act(T.bt[:, b0 + j:b0 + 4 * K:4], x[:, 0:4 * C].indirect(T.offb[:, 4 * j:4 * j + 4]), F.Copy,
+                xk + ["offb%d" % j], ["bt%d_%d" % (t, j)], "+bs%d" % t)
         select(0, T.rows[:, Lr:Lr + C], ["row0", "rows0"])
+        select(1, T.rows[:, Lr + 1:Lr + 1 + C], ["row0"])
+        select(2, T.rows[:, Nr:Nr + C], ["row336", "rows0"])
         bq, bs = T["bq%d" % t], T["bs%d" % t]
         quant(bq[:], bs[:], T.bt[:, 512 * t:512 * t + 512], ["btz"] + ["bt%d_%d" % (t, j) for j in range(4)], ["bq%d" % t])
         c0 = K * t
@@ -398,20 +410,20 @@ def rank_program(g, core, T, topo):
             send(T["rq%d" % t][:].bitcast(dt.uint8), src_q, "aq%d" % t, cq, 0, ["bq%d" % t])
             send(T["rs%d" % t][:], src_s, "as%d" % t, cs, 1, ["bq%d" % t])
 
-        select(1, T.rows[:, Lr + 1:Lr + 1 + C], ["row0"])
-        select(2, T.rows[:, Nr:Nr + C], ["row336", "rows0"])
+        tt(sm(2), T.twoc[:], picked(0), A.subtract, ["sel0", "twoc"], ["sm2"])
         ts(sm(0), picked(0), 383.0, A.mult, ["sel0"], ["sm0"], kind="+a%d" % t)
-        tt(sm(2), T.twoc[:], picked(0), A.subtract, ["sel0", "twoc"], ["sm2"], "+a%d" % t)
         ts(sm(1), picked(1), 384.0, A.mult, ["sel1"], ["sm1"], -64.0, A.add, "+a%d" % t)
+        tt(sm(4), sm(2), picked(2), A.subtract, ["sel2", "sm2"], ["sm4"], "+b%d" % t)
+        tt(sm(3), sm(1), sm(0), A.subtract, ["sm0", "sm1"], ["sm3"], "+b%d" % t)
         if last:
             ts(T.offl[:], lends, 0.5, A.mult, lcs, ["offl"], 160.0, A.add)
             if cq is None:
                 send(T.larr[:], T.offl[:], "al", dst, 1, ["offl"])
             else:
                 send(T.rl[:], T.offl[:], "al", cs, 1, ["offl"])
-        tt(sm(4), sm(2), picked(2), A.subtract, ["sel2", "sm2"], ["sm4"], "+b%d" % t)
-        tt(sm(3), sm(1), sm(0), A.subtract, ["sm0", "sm1"], ["sm3"], "+b%d" % t)
         tt(sm(5), sm(3), sm(4), A.max, ["sm3", "sm4"], ["sm5"])
+        if t == 0:
+            quant(T.vq[:], T.vs[:], T.vt[:], ["vt"], ["vq"])
         copy(T.offd[:], sm(5), ["sm5"], ["offd"])
         e0 = (C + K) * t
         copy(T.er[:, e0:e0 + C + K].indirect(T.offd[:]), T.cval[:], ["cval", "offd"], ["er%d" % t])
@@ -421,8 +433,8 @@ def rank_program(g, core, T, topo):
         ts(sm(2), picked(2), 4.0, A.mult, ["sel2"], ["sm2"], 768.0, A.add)
         select(0, T.rows[:, Ar:Ar + C], ["row672", "rows0"])
         select(1, T.rows[:, Ar + 1:Ar + 1 + C], ["row672"])
-        ts(sm(0), picked(0), 1532.0, A.mult, ["sel0"], ["sm0"], kind="+c%d" % t)
-        ts(sm(1), picked(1), 1536.0, A.mult, ["sel1"], ["sm1"], -256.0, A.add, "+c%d" % t)
+        ts(sm(0), picked(0), 1532.0, A.mult, ["sel0"], ["sm0"], 256.0, A.add)
+        ts(sm(1), picked(1), 1536.0, A.mult, ["sel1"], ["sm1"])
         tt(sm(3), sm(1), sm(0), A.subtract, ["sm0", "sm1"], ["sm3"])
         tt(sm(5), sm(3), sm(2), A.max, ["sm3", "sm2"], ["sm5"])
         for j in (2, 3, 0, 1):
@@ -436,49 +448,69 @@ def rank_program(g, core, T, topo):
             act(x[:, 4 * C + b:4 * (C + K):4], T["p%d" % (4 + b)][:, c0:c0 + K], F.Copy, ["#%d" % (4 + b)],
                 ["ar%d_%d" % (t, b)], "+ar%d" % t)
 
-        for j in (2, 0, 3, 1):
-            o, i = T.tb[:, j:4 * C:4], x[:].indirect(T.offt[:, NPIV * j:NPIV * j + NPIV])
+        def gather(h, j, q):
+            o = T.tb[:, 4 * H * h + j:4 * H * (h + 1):4]
+            i = x[:].indirect(T.offt[:, NPIV * j + 10 * h:NPIV * j + 10 * h + 10])
             rd = xk + ["ar%d_%d" % (t, b) for b in range(4)] + ["offt%d" % j]
-            if j >= 2:
-                act(o, i, F.Copy, rd, ["tb%d" % j], "+ts%d" % t)
+            if q == "s":
+                act(o, i, F.Copy, rd, ["tb%d_%d" % (h, j)], "+ts%d_%d" % (t, h))
             else:
-                copy(o, i, rd, ["tb%d" % j], "+tv%d" % t)
-        tbs = ["tb%d" % j for j in range(4)]
-        act(T.tb[:, 4 * C:4 * C + 4], T.tb[:, 0:4], F.Copy, tbs, ["tbw"])
-        quant(T.tq[:], T.ts[:], T.tb[:, 0:4 * C], tbs, ["tq"])
-        if last:
-            ts(T.offe[:], sm(5), 0.25, A.mult, ["sm5"], ["offe"])
-        quant(T.t2q[:], T.t2s[:], T.tb[:, 4:4 * C + 4], tbs + ["tbw"], ["t2q"])
-        if t == 0:
-            quant(T.vq[:], T.vs[:], T.vt[:], ["vt"], ["vq"])
+                copy(o, i, rd, ["tb%d_%d" % (h, j)], "+tv%d_%d" % (t, h))
+
+        def products(h):
+            a, z = RUNS[h]
+            for w, b in ((1, 0), (1, 1), (1, 2), (0, 0), (0, 1), (0, 2), (1, 3), (0, 3)):
+                cols = slice(128 * b, 128 * b + 128)
+                if w:
+                    mm(4 * h + b, z - a, T.wq[:, cols], T.wp[:, cols], T.tq[:, a:z], T.ts[:, a:z], ["wq", "wp", "tq%d" % h],
+                       True, False)
+                else:
+                    mm(4 * h + b, z - a, T.zq[:, cols], T.zp[:, cols], T.t2q[:, a:z], T.t2s[:, a:z],
+                       ["zq", "zp", "t2q%d" % h], False, True)
+
+        def taps(h, rd, more):
+            a, z = RUNS[h]
+            quant(T.tq[:, a:z], T.ts[:, a:z], T.tb[:, 4 * a:4 * z], rd, ["tq%d" % h])
+            quant(T.t2q[:, a:z], T.t2s[:, a:z], T.tb[:, 4 * a + 4:4 * z + 4], rd + more, ["t2q%d" % h])
+
+        tb0, tb1 = ["tb0_%d" % j for j in range(4)], ["tb1_%d" % j for j in range(4)]
+        for j, q in ((2, "s"), (0, "v"), (3, "s"), (1, "v")):
+            gather(0, j, q)
+        for j in (2, 3, 1):
+            gather(1, j, "s")
+        act(T.tb[:, 4 * C:4 * C + 4], T.tb[:, 0:4], F.Copy, tb0, ["tbw"])
         if last:
             act(T.olw[:, C:C + K], T.olw[:, 0:C].indirect(T.larr[:]), F.Identity, ["olw0", "larr"], ["olw1"], bias=float(C))
-            act(T.olr[:], T.olw[:].indirect(T.offe[:]), F.Copy, ["olw0", "olw1", "offe"], ["olr"])
-            dma("y", T.ol[:], T.olr[0:128:16, :], ["olr"], ["o3"])
-        for w, b in ((1, 0), (1, 1), (1, 2), (0, 0), (0, 1), (0, 2), (1, 3), (0, 3)):
-            cols = slice(128 * b, 128 * b + 128)
-            if w:
-                mm(b, C, T.wq[:, cols], T.wp[:, cols], T.tq[:], T.ts[:], ["wq", "wp", "tq"], True, False)
-            else:
-                mm(b, C, T.zq[:, cols], T.zp[:, cols], T.t2q[:], T.t2s[:], ["zq", "zp", "t2q"], False, True)
-        for b in range(4):
-            o, i = X[t + 1][:, b:4 * C:4], T["p%d" % b][:, 0:C]
-            if b % 2 == 0:
-                act(o, i, F.Copy, ["#%d" % b], [XK[t + 1][b]], "+xs%d" % t, scale=0.015625)
-            else:
-                ts(o, i, 0.015625, A.mult, ["#%d" % b], [XK[t + 1][b]], kind="+xv%d" % t)
+        taps(0, tb0, [])
+        products(0)
+        gather(1, 0, "v")
+        taps(1, tb0 + tb1, ["tbw"])
+        products(1)
+        if last:
+            ts(T.offe[:], sm(5), 0.25, A.mult, ["sm5"], ["offe"])
+        for h in range(2):
+            a, z = RUNS[h]
+            nk = xkeys(t + 1, h)
+            for b in range(4):
+                o, i = X[t + 1][:, 4 * a + b:4 * z:4], T["p%d" % (4 * h + b)][:, 0:z - a]
+                if b % 2 == 0:
+                    act(o, i, F.Copy, ["#%d" % (4 * h + b)], [nk[b]], "+xs%d_%d" % (t, h), scale=0.015625)
+                else:
+                    ts(o, i, 0.015625, A.mult, ["#%d" % (4 * h + b)], [nk[b]], kind="+xv%d_%d" % (t, h))
+            quant(T.xq[:, a:z], T.xs[:, a:z], X[t + 1][:, 4 * a:4 * z], nk, ["xq%d" % h])
+            if last:
+                mm(h, z - a, T.vq[:], T.vs[:], T.xq[:, a:z], T.xs[:, a:z], ["vq", "xq%d" % h])
+                dma("y", T.oc[:, 4 * a:4 * z], T.xq[:, a:z].bitcast(dt.uint8), ["xq%d" % h], ["oc%d" % h])
 
+    both = ["xq0", "xq1"]
+    act(T.olr[:], T.olw[:].indirect(T.offe[:]), F.Copy, ["olw0", "olw1", "offe"], ["olr"])
+    dma("s", T.ol[:], T.olr[0:128:16, :], ["olr"], ["o3"])
     for h in range(2):
-        quant(T.xq[:, H * h:H * h + H], T.xs[:, H * h:H * h + H], T.x2[:, 4 * H * h:4 * H * (h + 1)], XK[2],
-              ["xq", "fq0"] if h == 0 else ["fq1"])
-        mm(4 + h, H, T.vq[:], T.vs[:], T.xq[:, H * h:H * h + H], T.xs[:, H * h:H * h + H], ["vq", "fq%d" % h])
-    both = ["fq0", "fq1"]
-    dma("y", T.oc[:], T.xq[:].bitcast(dt.uint8), both, ["o0"])
+        a, z = RUNS[h]
+        copy(T.yo[:, a:z], T["p%d" % h][:, 0:z - a], ["#%d" % h], ["yo%d" % h])
     for k in range(4):
         dma("y" if k < 2 else "s", T.osc[4 * k:4 * k + 4, :], T.xs[32 * k:32 * k + 4, :], both, ["o1_%d" % k])
-    copy(T.yo[:, 0:H], T.p4[:, 0:H], ["#4"], ["yo0"], "+y")
-    copy(T.yo[:, H:C], T.p5[:, 0:H], ["#5"], ["yo1"], "+y")
     dma("y", T.y[:], T.yo[:], ["yo0", "yo1"], ["o2"])
-    op("y", None, ["o0", "o2", "o3"] + ["o1_%d" % k for k in range(4)], [])
+    op("y", None, ["oc0", "oc1", "o2", "o3"] + ["o1_%d" % k for k in range(4)], [])
     emit(g, T, ops)
     g.wait_ge(T.sem.sent, sent[0])

@@ -5,7 +5,14 @@ Q4, U8, BF, FP, I32, U16 = "float8_e4m3fn_x4", "uint8", "bfloat16", "float32", "
 NPIV = C // 16
 NS = 7
 H = C // 2
-RUNS = ((0, H - 2), (H - 2, C))
+CUTS = (10, 10)
+EARLY = 128
+EW = 3 * C
+TINY = 2.0 ** -40
+LW = C - K + 16
+SPLIT = 4
+BQ = ("svsv", "ssss")
+AQ = ("ssvv", "ssss")
 
 
 def sb(n, t):
@@ -13,7 +20,7 @@ def sb(n, t):
 
 
 SCRATCH = {
-    "ut": sb(512, BF), "vt": sb(512, BF), "uq": sb(128, Q4), "us": sb(128, U8), "u3q": sb(384, Q4), "u3s": sb(384, U8),
+    "ut": sb(512, BF), "vt": sb(512, BF), "uq": sb(128, Q4), "us": sb(128, U8), "u2q": sb(256, Q4), "u2s": sb(256, U8),
     "vq": sb(128, Q4), "vs": sb(128, U8),
     "wq": sb(512, Q4), "wp": sb(512, U8), "zq": sb(512, Q4), "zp": sb(512, U8),
     "x0": sb(4 * (C + K), BF), "x1": sb(4 * (C + K), BF), "x2": sb(4 * C, BF),
@@ -23,22 +30,23 @@ SCRATCH = {
     "yb": sb(2 * C, BF), "yr": sb(2 * C, BF), "wr": sb(2 * C, BF), "eq": sb(2 * C, BF), "vr": sb(2 * C, BF),
     "mx": sb(2 * H, BF), "nn": sb(1, FP),
     "lm": sb(4 * C, BF), "lc": sb(4 * H, FP),
-    "sel": sb(3 * C, BF), "sm": sb(6 * NPIV, FP), "er": sb(2 * (C + K), BF),
-    "offb": sb(16, U16), "offt": sb(4 * NPIV, U16), "offd": sb(NPIV, U16), "offe": sb(NPIV, U16), "offu": sb(24, U16),
+    "sel": sb(C, BF), "sel5": sb(5 * C + 64, BF), "sel3": sb(3 * C + 32, BF), "co5": sb(5 * NPIV, FP), "co3": sb(3 * NPIV, FP),
+    "al5": sb(5 * NPIV, FP), "al3": sb(3 * NPIV, FP), "sm": sb(2 * NPIV, FP), "er": sb(2 * EW, BF),
+    "offb": sb(16, U16), "offt": sb(4 * NPIV, U16), "offd": sb(NPIV, U16), "offe": sb(NPIV, U16), "offu": sb(16, U16),
     "offl": sb(4, U16), "larr": sb(4, U16), "rl": sb(4, U16),
     "bt": sb(1024, BF), "bq0": sb(128, Q4), "bs0": sb(128, U8), "bq1": sb(128, Q4), "bs1": sb(128, U8),
     "lq": sb(256, Q4), "ls": sb(256, U8),
     "rq0": sb(K, Q4), "rs0": sb(K, U8), "rq1": sb(K, Q4), "rs1": sb(K, U8),
     "tb": sb(4 * C + 8, BF), "tq": sb(C, Q4), "ts": sb(C, U8), "t2q": sb(C, Q4), "t2s": sb(C, U8),
-    "ew": sb(520, BF), "idn": sb(128, BF), "eq4": sb(512, Q4), "es4": sb(512, U8),
-    "iu": sb(24, I32), "qi": sb(2, I32), "qf": sb(1, FP), "kk": sb(NPIV, FP), "kq": sb(NPIV, FP), "twoc": sb(NPIV, FP),
+    "ew": sb(520, BF), "eq4": sb(512, Q4), "es4": sb(512, U8),
+    "iu": sb(16, I32), "qi": sb(2, I32), "qf": sb(1, FP), "kk": sb(NPIV, FP), "kq": sb(NPIV, FP), "rc": sb(NPIV, FP),
     "thr": sb(4, BF), "thrh": sb(4, FP), "jm": sb(C, BF), "csel": sb(C, BF), "chold": sb(C, BF), "cval": sb(C, BF),
     "olw": sb(C + K, FP), "olr": sb(C, FP), "yo": sb(C, FP),
 }
 for _b in range(8):
     SCRATCH["p%d" % _b] = ("psum", [128, 512], FP)
 
-POOLS = {"v": 52, "s": 30, "t": 24, "g": 10, "d": 20}
+POOLS = {"v": 54, "s": 30, "t": 24, "g": 14, "d": 22}
 SEMAPHORES = ["aq0", "aq1", "as0", "as1", "al", "sent"] + ["%s%d" % (k, i) for k in POOLS for i in range(POOLS[k])]
 
 
@@ -196,6 +204,12 @@ def rank_program(g, core, T, topo):
     def act(out, in_, f, rd, wr, kind="", **kw):
         op("s", lambda e: e.activation(out, in_, f, **kw), rd, wr, kind)
 
+    def move(q, out, in_, rd, wr, kind):
+        if q == "s":
+            act(out, in_, F.Copy, rd, wr, kind + q)
+        else:
+            copy(out, in_, rd, wr, kind + q)
+
     def fill(ap, c, wr):
         op("v", lambda e: e.memset(ap, c), [], wr)
 
@@ -205,6 +219,9 @@ def rank_program(g, core, T, topo):
     def mm(bank, n, lq, ls, rq, rs, rd, start=True, stop=True):
         op("t", lambda e: e.matmul_mx(T["p%d" % bank][:, 0:n], lq, ls, rq, rs, start, stop), rd, ["#%d" % bank],
            "" if start else "acc")
+
+    def turn(out, in_, rd, wr):
+        op("v", lambda e: e.transpose(out, in_), rd, wr)
 
     def iota(out, pattern, base, cm, wr, small=False):
         if small:
@@ -237,48 +254,68 @@ def rank_program(g, core, T, topo):
     Lr, Nr, Ar = 0, 336, 672
 
     def xkeys(t, h):
-        return ["x0"] if t == 0 else ["x%d_%d_%d" % (t, h, b) for b in range(4)]
+        return ["x0_%d" % h] if t == 0 else ["x%d_%d_%d" % (t, h, b) for b in range(4)]
 
+    def early(step):
+        if step == 0:
+            mm(0, EARLY, T.uq[:], T.us[:], T.xq[:, 0:EARLY], T.xs[:, 0:EARLY], ["uq", "xq0"])
+        else:
+            turn(T.tt[:, 0:EARLY], T.p0[:, 0:EARLY], ["#0"], ["tta"])
+
+    x0 = 4 * (H - 2)
     dma("y", T.ut[:], T.u[:], [], ["ut"])
-    dma("s", T.x0[:, 0:4 * C], T.x[:], [], ["x0"])
-    dma("y", T.wq[:].bitcast(dt.uint8), T.wc[:], ["x0"], ["wq"])
+    dma("s", T.x0[:, 0:x0], T.x[:, 0:x0], [], ["x0_0"])
+    dma("s", T.x0[:, x0:4 * C], T.x[:, x0:4 * C], [], ["x0_1"])
+    dma("y", T.wq[:].bitcast(dt.uint8), T.wc[:], ["x0_0", "x0_1"], ["wq"])
     dma("y", T.zq[:].bitcast(dt.uint8), T.zc[:], [], ["zq"])
     dma("y", T.wp[:], T.ws[:], [], ["wp"])
     dma("y", T.zp[:], T.zs[:], [], ["zp"])
     dma("y", T.vt[:], T.v[:], [], ["vt"])
 
-    iota(T.iu[:, 0:8], [[16, 8]], 0, 0, ["iu0"])
-    iota(T.iu[:, 8:24], [[16, 2], [32, 4], [0, 2]], 0, 0, ["iu1"])
-    fill(T.idn[:], 1.0, ["idn"])
-    op("g", lambda e: e.affine_select(T.idn[:], T.idn[:], [[-1, 128]], A.is_equal, 0.0, 0, 1), ["idn"], ["idn"])
+    iota(T.iu[:], [[16, 2], [32, 4], [0, 2]], 0, 0, ["iu"])
     iota(T.qi[:, 0:1], [[0, 1]], 0, 1, ["qi0"])
     iota(T.kk[:], [[16, NPIV]], 0, 0, ["kk"], True)
     iota(T.jm[:], [[0, NPIV], [1, 16]], 0, 0, ["jm"], True)
+    iota(T.zz[:], [[0, 2 * C]], 0, 0, ["zz0", "zz1"], True)
+    iota(T.bt[:, 256:768], [[0, 512]], 0, 0, ["btz"], True)
     iota(T.cval[:], [[1, C]], -192, 0, ["cval"], True)
+    iota(T.er[:, 0:C], [[0, C]], 1, 0, ["er0"], True)
+    iota(T.ew[:], [[0, 520]], 1, 0, ["ew"], True)
+    op("g", lambda e: e.affine_select(T.ew[:], T.ew[:], [[-1, 520]], A.is_equal, 0.0, 3, 4), ["ew"], ["ew"])
+    iota(T.er[:, EW:EW + C], [[0, C]], 1, 0, ["er1"], True)
     iota(T.olw[:, 0:C], [[1, C]], 0, 0, ["olw0"], True)
-    fill(T.ew[:], 0.0, ["ew"])
-    fill(T.bt[:, 256:768], 0.0, ["btz"])
-    fill(T.zz[:], 0.0, ["zz0", "zz1"])
-    fill(T.rows[:, 0::336], 0.0, ["rows0"])
-    fill(T.er[:], 128.0, ["er0", "er1"])
-    copy(T.offu[:], T.iu[:], ["iu0", "iu1"], ["offu"])
-    quant(T.lq[:, 64:192], T.ls[:, 64:192], T.bt[:, 256:768], ["btz"], ["lz"])
-    copy(T.ew[:, 3:515:4], T.idn[:], ["idn"], ["ew"])
+    fill(T.rows[:, Lr:Ar:Nr], 0.0, ["rows0"])
+    fill(T.rows[:, Ar:Ar + 1], 1.0, ["rows1"])
+    fill(T.co5[:, 0::5], 0.0, ["co50"])
+    fill(T.co5[:, 3::5], -0.5, ["co53"])
+    fill(T.co5[:, 4::5], 0.0, ["co54"])
+    copy(T.offu[:], T.iu[:], ["iu"], ["offu"])
     ts(T.qi[:, 1:2], T.qi[:, 0:1], 15, A.bitwise_and, ["qi0"], ["qi1"])
-    quant(T.uq[:], T.us[:], T.ut[:], ["ut"], ["uq"])
+    fill(T.sel5[:, 139::80], 0.0, ["s54"])
+    fill(T.co3[:, 0::3], 0.0, ["co30"])
     copy(T.qf[:], T.qi[:, 1:2], ["qi1"], ["qf"])
-    copy(T.u3q[:].bitcast(dt.uint32), T.uq[:].bitcast(dt.uint32).indirect(T.offu[:]), ["uq", "offu"], ["u3q"])
-    act(T.u3s[:], T.us[:].indirect(T.offu[:]), F.Copy, ["uq", "offu"], ["u3s"])
+    fill(T.co3[:, 1::3], -(1.0 + 1.0 / 512), ["co31"])
+    fill(T.co3[:, 2::3], 1.0, ["co32"])
+    fill(T.sel3[:, 77::48], 386.0 / 512, ["s32"])
     act(T.kq[:], T.kk[:], F.Identity, ["kk", "qf"], ["kq"], bias=T.qf[:])
-    act(T.twoc[:], T.kq[:], F.Copy, ["kq"], ["twoc"], "+k", scale=2.0)
+    act(T.co5[:, 2::5], T.kq[:], F.Identity, ["kq"], ["co52"], bias=float(-C), scale=-1.0)
     act(T.thr[:], T.kq[:, 0:4], F.Copy, ["kq"], ["thr"], "+k")
     act(T.thrh[:], T.kq[:, 0:4], F.Identity, ["kq"], ["thrh"], "+k", bias=0.5)
-    quant(T.xq[:], T.xs[:], T.x0[:, 0:4 * C], ["x0"], ["xq0", "xq1"])
-    for b in range(4):
-        quant(T.eq4[:, 128 * b:128 * b + 128], T.es4[:, 128 * b:128 * b + 128], T.ew[:, 3 - b:515 - b], ["ew"], ["e%d" % b], "+e")
+    act(T.sel5[:, 123::80], T.kq[:], F.Identity, ["kq"], ["s53"], "+k", bias=float(-H))
+    op("v", lambda e: e.reciprocal(T.rc[:], T.co5[:, 2::5]), ["co52"], ["rc"])
+    ts(T.chold[:], T.jm[:], 0.0, A.is_gt, ["jm"], ["chold"])
+    act(T.co5[:, 1::5], T.rc[:], F.Identity, ["rc"], ["co51"], bias=-1.0)
+    quant(T.uq[:], T.us[:], T.ut[:], ["ut"], ["uq"])
+    quant(T.xq[:, 0:H - 2], T.xs[:, 0:H - 2], T.x0[:, 0:x0], ["x0_0"], ["xq0"])
+    copy(T.u2q[:].bitcast(dt.uint32), T.uq[:].bitcast(dt.uint32).indirect(T.offu[:]), ["uq", "offu"], ["u2q"])
+    act(T.u2s[:], T.us[:].indirect(T.offu[:]), F.Copy, ["uq", "offu"], ["u2s"])
+    act(T.csel[:], T.jm[:], F.Abs, ["jm", "qf"], ["csel"], bias=T.qf[:], scale=-1.0)
+    early(0)
+    quant(T.xq[:, H - 2:C], T.xs[:, H - 2:C], T.x0[:, x0:4 * C], ["x0_1"], ["xq1"])
+    early(1)
 
     def useg(i):
-        return T.u3q[:, 128 * i:128 * i + 128], T.u3s[:, 128 * i:128 * i + 128]
+        return T.u2q[:, 128 * i:128 * i + 128], T.u2s[:, 128 * i:128 * i + 128]
 
     ends = T.cnt[:, H - 1::H]
     cnts = ["cnt%d" % k for k in range(NPIV)]
@@ -296,7 +333,7 @@ def rank_program(g, core, T, topo):
             "c": lambda: ts(c, ends, float(limit), A.is_ge, cnts, [k("cut")], -512.0, A.mult),
             "z": lambda: tt(T.zz[:, C * s:C * s + C:16], ends, c, A.min, cnts + [k("cut")], [k("zz")]),
             "spread": lambda: scan(w(T.yb), T.chold[:], w(T.zz), 0.0, A.mult, A.add, ["chold", k("zz")], [k("yb")]),
-            "turn": lambda: op("v", lambda e: e.transpose(w(T.yr), w(T.yb)), [k("yb")], [k("yr")]),
+            "turn": lambda: turn(w(T.yr), w(T.yb), [k("yb")], [k("yr")]),
             "out": lambda: act(w(T.wr), w(T.yr), F.Relu, [k("yr")], [k("wr")], bias=-1.0, scale=-1.0 / 256),
             "top": lambda: scan(w(T.mx, H), T.yr[:, C * s:C * s + H], T.yr[:, C * s + H:C * s + C], -1024.0, A.max, A.max,
                                 [k("yr")], [k("mx")]),
@@ -309,11 +346,11 @@ def rank_program(g, core, T, topo):
 
     lo, hi = cut(0, 0, Lr), cut(1, -192, Nr)
 
-    def select(slot, row, rd, kind=""):
-        scan(T.sel[:, C * slot:C * slot + C], T.csel[:], row, 0.0, A.add, A.min, ["csel"] + rd, ["sel%d" % slot], kind)
+    def select(out, row, rd, wr):
+        scan(out, T.csel[:], row, 0.0, A.add, A.min, ["csel"] + rd, wr)
 
-    def picked(slot):
-        return T.sel[:, C * slot + 15:C * slot + C:16]
+    def turns(buf, n, r):
+        return buf[:, 16 * r:16 * r + n * (C - 1) + 1:n]
 
     def sm(i):
         return T.sm[:, NPIV * i:NPIV * i + NPIV]
@@ -324,17 +361,18 @@ def rank_program(g, core, T, topo):
     for t in range(R):
         x, xk = X[t], xkeys(t, 0) + xkeys(t, 1)
         last = t == R - 1
-        for bank, i in ((0, 0), (1, 1), (2, 2), (3, 1)):
+        both = ["xq0", "xq1"]
+        mm(1, C - EARLY, T.uq[:], T.us[:], T.xq[:, EARLY:C], T.xs[:, EARLY:C], ["uq"] + both)
+        for bank, i in ((2, 0), (3, 1), (4, 0)):
             a, b = useg(i)
-            mm(bank, C, a, b, T.xq[:], T.xs[:], ["u3q", "u3s", "xq0", "xq1"])
-        op("v", lambda e: e.transpose(T.tt[:, 0:64], T.p0[:, 0:64]), ["#0"], ["tta"])
-        op("v", lambda e: e.transpose(T.tt[:, 64:C], T.p0[:, 64:C]), ["#0"], ["ttb"])
+            mm(bank, C, a, b, T.xq[:], T.xs[:], ["u2q", "u2s"] + both)
+        turn(T.tt[:, EARLY:C], T.p1[:, 0:C - EARLY], ["#1"], ["ttb"])
 
         def tk(k):
-            return "tta" if 16 * k < 64 else "ttb"
+            return "tta" if 16 * k < EARLY else "ttb"
 
         def sign(k):
-            act(mrow(k), T.p1[:, 0:C], F.Sign, ["#1", tk(k)], ["m%d" % k], bias=T.tt[:, 16 * k:16 * k + 1], scale=-1.0)
+            act(mrow(k), T.p2[:, 0:C], F.Sign, ["#2", tk(k)], ["m%d" % k], bias=T.tt[:, 16 * k:16 * k + 1], scale=-1.0)
 
         shared = 2 * NS
         for i in range(NS + 1):
@@ -348,117 +386,178 @@ def rank_program(g, core, T, topo):
                     accum_out=T.gsum[:, i - 1:i])
         act(T.cnt[:, H - 1:2 * H * NS:2 * H], T.gsum[:], F.Identity, ["gs%d" % (2 * i) for i in range(NS)],
             ["cnt%d" % (2 * i) for i in range(NS)], bias=-256.0)
-        if t == 0:
-            act(T.csel[:], T.jm[:], F.Abs, ["jm", "qf"], ["csel"], bias=T.qf[:], scale=-1.0)
-            act(T.csel[:], T.csel[:], F.Relu, ["csel"], ["csel"], bias=1024.0, scale=-1024.0)
         mine = [k for k in range(NPIV) if k % 2] + [shared] + [k for k in range(shared + 2, NPIV, 2)]
         for i in range(len(mine) + 1):
             if i < len(mine):
                 k = mine[i]
-                bank = 2 if k % 2 else 3
+                bank = 3 if k % 2 else 4
                 if k == shared:
                     ts(mrow(k), mrow(k), 0.0, A.is_lt, ["m%d" % k], ["m%d" % k])
                 else:
                     ts(mrow(k), T["p%d" % bank][:, 0:C], T.tt[:, 16 * k:16 * k + 1], A.is_gt, ["#%d" % bank, tk(k)],
                        ["m%d" % k])
-            elif t == 0:
-                ts(T.chold[:], T.jm[:], 0.0, A.is_gt, ["jm"], ["chold"])
             if i > 0:
                 k = mine[i - 1]
                 scan(T.cnt[:, H * k:H * k + H], T.msk[:, C * k:C * k + H], T.msk[:, C * k + H:C * k + C], -256.0, A.add,
                      A.add, ["m%d" % k], ["cnt%d" % k], "+cnt%d" % t)
 
-        for step in ("c", "z", "spread", "turn", "out", "top"):
-            lo[step]()
-            hi[step]()
-        lo["eq"]()
-        hi["n"]()
-        lo["v"]()
-        hi["eq"]()
-        lo["run"]()
-        hi["v"]()
-        lrow = T.rows[:, Lr + 1:Lr + 1 + C]
-        for k in (2, 3):
-            act(T.lm[:, C * k:C * k + C], lrow, F.Sign, ["row0", "thrh"], ["lm%d" % k, "lc%d" % k], "+ld%d" % t,
-                bias=T.thrh[:, k:k + 1], scale=-1.0, accum_out=T.lc[:, H * k + H - 1:H * k + H])
-        for k in range(2):
-            ts(T.lm[:, C * k:C * k + C], lrow, T.thr[:, k:k + 1], A.is_le, ["row0", "thr"], ["lm%d" % k], 2.0, A.mult)
-        for k in range(2):
-            scan(T.lc[:, H * k:H * k + H], T.lm[:, C * k:C * k + H], T.lm[:, C * k + H:C * k + C], -320.0,
-                 A.add, A.add, ["lm%d" % k], ["lc%d" % k], "+lc%d" % t)
-        hi["run"]()
+        if t == 0:
+            act(T.csel[:], T.csel[:], F.Relu, ["csel"], ["csel"], bias=1024.0, scale=-1024.0)
+            act(T.cval[:], T.cval[:], F.Copy, ["cval"], ["cval"], scale=TINY)
         lcs = ["lc%d" % k for k in range(4)]
         lends = T.lc[:, H - 1::H]
-        b0 = 0 if t == 0 else 768
-        for j in range(4):
-            ts(T.offb[:, 4 * j:4 * j + 4], lends, 2.0, A.mult, lcs, ["offb%d" % j], float(640 + j), A.add)
-        for j in range(4):
-            act(T.bt[:, b0 + j:b0 + 4 * K:4], x[:, 0:4 * C].indirect(T.offb[:, 4 * j:4 * j + 4]), F.Copy,
-                xk + ["offb%d" % j], ["bt%d_%d" % (t, j)], "+bs%d" % t)
-        select(0, T.rows[:, Lr:Lr + C], ["row0", "rows0"])
-        select(1, T.rows[:, Lr + 1:Lr + 1 + C], ["row0"])
-        select(2, T.rows[:, Nr:Nr + C], ["row336", "rows0"])
+        b0, c0, e0 = 768 * t, K * t, EW * t
+        er = T.er[:, e0:e0 + C]
         bq, bs = T["bq%d" % t], T["bs%d" % t]
-        quant(bq[:], bs[:], T.bt[:, 512 * t:512 * t + 512], ["btz"] + ["bt%d_%d" % (t, j) for j in range(4)], ["bq%d" % t])
-        c0 = K * t
-        lq, ls = land(T, t)
-        src_q, src_s = bq[:, c0:c0 + K].bitcast(dt.uint8), bs[:, c0:c0 + K]
-        if cq is None:
-            send(lq, src_q, "aq%d" % t, dst, 0, ["bq%d" % t])
-            send(ls, src_s, "as%d" % t, dst, 1, ["bq%d" % t])
-        else:
-            send(T["rq%d" % t][:].bitcast(dt.uint8), src_q, "aq%d" % t, cq, 0, ["bq%d" % t])
-            send(T["rs%d" % t][:], src_s, "as%d" % t, cs, 1, ["bq%d" % t])
 
-        tt(sm(2), T.twoc[:], picked(0), A.subtract, ["sel0", "twoc"], ["sm2"])
-        ts(sm(0), picked(0), 383.0, A.mult, ["sel0"], ["sm0"], kind="+a%d" % t)
-        ts(sm(1), picked(1), 384.0, A.mult, ["sel1"], ["sm1"], -64.0, A.add, "+a%d" % t)
-        tt(sm(4), sm(2), picked(2), A.subtract, ["sel2", "sm2"], ["sm4"], "+b%d" % t)
-        tt(sm(3), sm(1), sm(0), A.subtract, ["sm0", "sm1"], ["sm3"], "+b%d" % t)
-        if last:
+        def count_s(k):
+            m = min(16 * k, C - LW - 16 * k)
+            act(T.lm[:, C * k + m:C * k + C - m], T.rows[:, Lr + 1 + m:Lr + 1 + C - m], F.Sign, ["row0", "thrh"],
+                ["lm%d" % k, "lc%d" % k], "+ld%d" % t, bias=T.thrh[:, k:k + 1], scale=-1.0,
+                accum_out=T.lc[:, H * k + H - 1:H * k + H])
+
+        def mask_v(k):
+            ts(T.lm[:, C * k:C * k + LW], T.rows[:, Lr + 1 + 16 * k:Lr + 1 + 16 * k + LW], T.thr[:, k:k + 1], A.is_le,
+               ["row0", "thr"], ["lm%d" % k], 2.0, A.mult)
+
+        def count_v(k):
+            scan(T.lc[:, H * k + H - LW // 2:H * k + H], T.lm[:, C * k:C * k + LW // 2], T.lm[:, C * k + LW // 2:C * k + LW],
+                 float(32 * k - C), A.add, A.add, ["lm%d" % k], ["lc%d" % k], "+lc%d" % t)
+
+        def border_offsets():
+            for j in (0, 2, 1, 3):
+                ts(T.offb[:, 4 * j:4 * j + 4], lends, 2.0, A.mult, lcs, ["offb%d" % j], float(640 + j), A.add)
+
+        def border_gathers():
+            for j in range(4):
+                move(BQ[t][j], T.bt[:, b0 + j:b0 + 4 * K:4], x[:, 0:4 * C].indirect(T.offb[:, 4 * j:4 * j + 4]),
+                     xk + ["offb%d" % j], ["bt%d_%d" % (t, j)], "+b%d" % t)
+
+        def border_out():
+            quant(bq[:], bs[:], T.bt[:, 512 * t:512 * t + 512], ["btz"] + ["bt%d_%d" % (t, j) for j in range(4)], ["bq%d" % t])
+            lq, ls = land(T, t)
+            src_q, src_s = bq[:, c0:c0 + K].bitcast(dt.uint8), bs[:, c0:c0 + K]
+            if cq is None:
+                send(lq, src_q, "aq%d" % t, dst, 0, ["bq%d" % t])
+                send(ls, src_s, "as%d" % t, dst, 1, ["bq%d" % t])
+            else:
+                send(T["rq%d" % t][:].bitcast(dt.uint8), src_q, "aq%d" % t, cq, 0, ["bq%d" % t])
+                send(T["rs%d" % t][:], src_s, "as%d" % t, cs, 1, ["bq%d" % t])
+
+        def list_out():
             ts(T.offl[:], lends, 0.5, A.mult, lcs, ["offl"], 160.0, A.add)
             if cq is None:
                 send(T.larr[:], T.offl[:], "al", dst, 1, ["offl"])
             else:
                 send(T.rl[:], T.offl[:], "al", cs, 1, ["offl"])
-        tt(sm(5), sm(3), sm(4), A.max, ["sm3", "sm4"], ["sm5"])
+
+        def pick(r):
+            row, a, key = ((Lr, 0, "row0"), (Lr, 1, "row0"), (Nr, 0, "row336"))[r]
+            select(turns(T.sel5, 5, r), T.rows[:, row + a:row + a + C], [key, "rows0"], ["s5%d" % r])
+
+        def places():
+            scan(T.al5[:], T.co5[:], T.sel5[:, 75::16], 0.0, A.mult, A.add,
+                 ["s5%d" % i for i in range(5)] + ["co5%d" % i for i in range(5)], ["al5"])
+
+        def place_offsets():
+            ts(T.offd[:], T.al5[:, 3::5], 2.0, A.mult, ["al5"], ["offd"], C + 0.25, A.add)
+
+        def scatter(a, z):
+            copy(T.er[:, e0:e0 + EW].indirect(T.offd[:, a:z]), T.cval[:, 16 * a:16 * z], ["cval", "offd"], ["er%d" % t])
+
+        def unit(b):
+            quant(T.eq4[:, 128 * b:128 * b + 128], T.es4[:, 128 * b:128 * b + 128], T.ew[:, 3 - b:515 - b], ["ew"], ["e%d" % b])
+
+        for step in ("c", "z", "spread", "turn", "out", "top"):
+            lo[step]()
+            hi[step]()
+        if t == 0:
+            lo["eq"]()
+            hi["n"]()
+            lo["v"]()
+            hi["eq"]()
+            lo["run"]()
+            hi["v"]()
+            count_s(1)
+            count_s(2)
+            mask_v(0)
+            mask_v(3)
+            count_v(0)
+            count_v(3)
+            hi["run"]()
+            border_offsets()
+            border_gathers()
+            pick(0)
+            border_out()
+            pick(1)
+            pick(2)
+            quant(T.lq[:, 64:192], T.ls[:, 64:192], T.bt[:, 256:768], ["btz"], ["lz"])
+            places()
+            unit(0)
+            place_offsets()
+            unit(1)
+            scatter(0, NPIV)
+            unit(2)
+        else:
+            lo["eq"]()
+            hi["n"]()
+            hi["eq"]()
+            lo["v"]()
+            hi["v"]()
+            lo["run"]()
+            hi["run"]()
+            count_s(1)
+            count_s(2)
+            mask_v(0)
+            mask_v(3)
+            pick(0)
+            count_v(0)
+            count_v(3)
+            pick(1)
+            pick(2)
+            border_offsets()
+            border_gathers()
+            places()
+            place_offsets()
+            scatter(0, SPLIT)
+            border_out()
+            scatter(SPLIT, NPIV)
+            list_out()
+        scan(T.rows[:, Ar + 1:Ar + 1 + C], er, er, 1.0, A.add, A.max, ["er%d" % t], ["row672"])
+        select(T.sel[:], er, ["er%d" % t], ["sel"])
+        select(turns(T.sel3, 3, 0), T.rows[:, Ar + 1:Ar + 1 + C], ["row672"], ["s30"])
+        select(turns(T.sel3, 3, 1), T.rows[:, Ar:Ar + C], ["row672", "rows1"], ["s31"])
+        ts(sm(0), T.sel[:, 15::16], -1.0 / (512 * TINY), A.mult, ["sel"], ["sm0"], -0.25, A.max)
+        scan(T.al3[:], T.co3[:], T.sel3[:, 45::16], 0.0, A.mult, A.add,
+             ["s30", "s31", "s32", "co30", "co31", "co32"], ["al3"])
+        if t == 0:
+            unit(3)
+        tt(sm(1), T.al3[:, 2::3], sm(0), A.min, ["al3", "sm0"], ["sm1"])
         if t == 0:
             quant(T.vq[:], T.vs[:], T.vt[:], ["vt"], ["vq"])
-        copy(T.offd[:], sm(5), ["sm5"], ["offd"])
-        e0 = (C + K) * t
-        copy(T.er[:, e0:e0 + C + K].indirect(T.offd[:]), T.cval[:], ["cval", "offd"], ["er%d" % t])
-        ts(T.eq[:, 0:C], T.er[:, e0:e0 + C], 127.5, A.is_gt, ["er%d" % t], ["eq0"])
-        select(2, T.er[:, e0:e0 + C], ["er%d" % t])
-        scan(T.rows[:, Ar + 1:Ar + 1 + C], T.eq[:, 0:C], T.eq[:, 0:C], 0.0, A.add, A.max, ["eq0"], ["row672"])
-        ts(sm(2), picked(2), 4.0, A.mult, ["sel2"], ["sm2"], 768.0, A.add)
-        select(0, T.rows[:, Ar:Ar + C], ["row672", "rows0"])
-        select(1, T.rows[:, Ar + 1:Ar + 1 + C], ["row672"])
-        ts(sm(0), picked(0), 1532.0, A.mult, ["sel0"], ["sm0"], 256.0, A.add)
-        ts(sm(1), picked(1), 1536.0, A.mult, ["sel1"], ["sm1"])
-        tt(sm(3), sm(1), sm(0), A.subtract, ["sm0", "sm1"], ["sm3"])
-        tt(sm(5), sm(3), sm(2), A.max, ["sm3", "sm2"], ["sm5"])
-        for j in (2, 3, 0, 1):
-            ts(T.offt[:, NPIV * j:NPIV * j + NPIV], sm(5), float(j), A.add, ["sm5"], ["offt%d" % j])
+        for j in (2, 0, 3, 1):
+            ts(T.offt[:, NPIV * j:NPIV * j + NPIV], sm(1), -2048.0, A.mult, ["sm1"], ["offt%d" % j], float(768 + j), A.add)
+        if last:
+            ts(T.offe[:], sm(1), -512.0, A.mult, ["sm1"], ["offe"], 192.0, A.add)
 
         m0 = 128 * t
         for b in range(4):
             mm(4 + b, 128, T.eq4[:, 128 * b:128 * b + 128], T.es4[:, 128 * b:128 * b + 128], T.lq[:, m0:m0 + 128],
                T.ls[:, m0:m0 + 128], ["e%d" % b, "lz", "lq%d" % t, "ls%d" % t])
         for b in range(4):
-            act(x[:, 4 * C + b:4 * (C + K):4], T["p%d" % (4 + b)][:, c0:c0 + K], F.Copy, ["#%d" % (4 + b)],
-                ["ar%d_%d" % (t, b)], "+ar%d" % t)
+            move(AQ[t][b], x[:, 4 * C + b:4 * (C + K):4], T["p%d" % (4 + b)][:, c0:c0 + K], ["#%d" % (4 + b)],
+                 ["ar%d_%d" % (t, b)], "+ar%d" % t)
+
+        run = (0, 16 * CUTS[t] - 2), (16 * CUTS[t] - 2, C)
+        slots = ((0, CUTS[t]), (CUTS[t], NPIV))
 
         def gather(h, j, q):
-            o = T.tb[:, 4 * H * h + j:4 * H * (h + 1):4]
-            i = x[:].indirect(T.offt[:, NPIV * j + 10 * h:NPIV * j + 10 * h + 10])
-            rd = xk + ["ar%d_%d" % (t, b) for b in range(4)] + ["offt%d" % j]
-            if q == "s":
-                act(o, i, F.Copy, rd, ["tb%d_%d" % (h, j)], "+ts%d_%d" % (t, h))
-            else:
-                copy(o, i, rd, ["tb%d_%d" % (h, j)], "+tv%d_%d" % (t, h))
+            a, z = slots[h]
+            move(q, T.tb[:, 64 * a + j:64 * z:4], x[:].indirect(T.offt[:, NPIV * j + a:NPIV * j + z]),
+                 xk + ["ar%d_%d" % (t, b) for b in range(4)] + ["offt%d" % j], ["tb%d_%d" % (h, j)], "+t%d_%d" % (t, h))
 
         def products(h):
-            a, z = RUNS[h]
+            a, z = run[h]
             for w, b in ((1, 0), (1, 1), (1, 2), (0, 0), (0, 1), (0, 2), (1, 3), (0, 3)):
                 cols = slice(128 * b, 128 * b + 128)
                 if w:
@@ -469,7 +568,7 @@ def rank_program(g, core, T, topo):
                        ["zq", "zp", "t2q%d" % h], False, True)
 
         def taps(h, rd, more):
-            a, z = RUNS[h]
+            a, z = run[h]
             quant(T.tq[:, a:z], T.ts[:, a:z], T.tb[:, 4 * a:4 * z], rd, ["tq%d" % h])
             quant(T.t2q[:, a:z], T.t2s[:, a:z], T.tb[:, 4 * a + 4:4 * z + 4], rd + more, ["t2q%d" % h])
 
@@ -486,10 +585,8 @@ def rank_program(g, core, T, topo):
         gather(1, 0, "v")
         taps(1, tb0 + tb1, ["tbw"])
         products(1)
-        if last:
-            ts(T.offe[:], sm(5), 0.25, A.mult, ["sm5"], ["offe"])
         for h in range(2):
-            a, z = RUNS[h]
+            a, z = run[h]
             nk = xkeys(t + 1, h)
             for b in range(4):
                 o, i = X[t + 1][:, 4 * a + b:4 * z:4], T["p%d" % (4 * h + b)][:, 0:z - a]
@@ -497,20 +594,26 @@ def rank_program(g, core, T, topo):
                     act(o, i, F.Copy, ["#%d" % (4 * h + b)], [nk[b]], "+xs%d_%d" % (t, h), scale=0.015625)
                 else:
                     ts(o, i, 0.015625, A.mult, ["#%d" % (4 * h + b)], [nk[b]], kind="+xv%d_%d" % (t, h))
+            if h == 1 and not last:
+                early(1)
             quant(T.xq[:, a:z], T.xs[:, a:z], X[t + 1][:, 4 * a:4 * z], nk, ["xq%d" % h])
+            if h == 0 and not last:
+                early(0)
             if last:
+                if h == 0:
+                    act(T.olr[:], T.olw[:].indirect(T.offe[:]), F.Copy, ["olw0", "olw1", "offe"], ["olr"])
+                    dma("y", T.ol[:], T.olr[0:128:16, :], ["olr"], ["o3"])
+                else:
+                    act(T.yo[:, 0:a], T.p0[:, 0:a], F.Copy, ["#0"], ["yo0"])
+                    dma("s", T.y[:, 0:a], T.yo[:, 0:a], ["yo0"], ["o2_0"])
                 mm(h, z - a, T.vq[:], T.vs[:], T.xq[:, a:z], T.xs[:, a:z], ["vq", "xq%d" % h])
                 dma("y", T.oc[:, 4 * a:4 * z], T.xq[:, a:z].bitcast(dt.uint8), ["xq%d" % h], ["oc%d" % h])
 
-    both = ["xq0", "xq1"]
-    act(T.olr[:], T.olw[:].indirect(T.offe[:]), F.Copy, ["olw0", "olw1", "offe"], ["olr"])
-    dma("s", T.ol[:], T.olr[0:128:16, :], ["olr"], ["o3"])
-    for h in range(2):
-        a, z = RUNS[h]
-        copy(T.yo[:, a:z], T["p%d" % h][:, 0:z - a], ["#%d" % h], ["yo%d" % h])
+    a = run[1][0]
+    copy(T.yo[:, a:C], T.p1[:, 0:C - a], ["#1"], ["yo1"])
     for k in range(4):
         dma("y" if k < 2 else "s", T.osc[4 * k:4 * k + 4, :], T.xs[32 * k:32 * k + 4, :], both, ["o1_%d" % k])
-    dma("y", T.y[:], T.yo[:], ["yo0", "yo1"], ["o2"])
-    op("y", None, ["oc0", "oc1", "o2", "o3"] + ["o1_%d" % k for k in range(4)], [])
+    dma("y", T.y[:, a:C], T.yo[:, a:C], ["yo1"], ["o2_1"])
+    op("y", None, ["oc0", "oc1", "o2_0", "o2_1", "o3"] + ["o1_%d" % k for k in range(4)], [])
     emit(g, T, ops)
     g.wait_ge(T.sem.sent, sent[0])

@@ -1,18 +1,41 @@
 from concourse.mybir import dt, AluOpType as A, ActivationFunctionType as F
 
 C, K, R = 320, 64, 2
-Q4, U8, BF, FP, I32, U16 = "float8_e4m3fn_x4", "uint8", "bfloat16", "float32", "int32", "uint16"
+Q4, U8, BF, FP, I32, U16, HF = "float8_e4m3fn_x4", "uint8", "bfloat16", "float32", "int32", "uint16", "float16"
 NPIV = C // 16
-NS = 7
+NG = NPIV // 2
 H = C // 2
-CUTS = (10, 10)
 EARLY = 128
-EW = 3 * C
+CUT = 10
+FIRST = 16 * CUT - 2
+SW = C + 2
+CW = 8 * (H + 1) + 8
+RW = 336
+EW = 3 * C + 16
 TINY = 2.0 ** -40
 LW = C - K + 16
-SPLIT = 4
-BQ = ("svsv", "ssss")
-AQ = ("ssvv", "ssss")
+
+CFG = [
+    [dict(bq="svsv", aq="ssvv", split=0), dict(bq="ssss", aq="ssss", split=6)],
+    [dict(bq="svsv", aq="ssvv", split=0), dict(bq="svsv", aq="ssvv", split=0)],
+]
+DIGITS = "0123456789abcdefghijklmnopqrstuvwxyzABCDEFGHIJKLMNOPQRSTUVWXYZ"
+ORDER = [
+    "000102030405060C0d0e0g070F0E0f0i0G0D0h0O0I0H0J0Y0l0N0m120L0k0Z1110140T0n0P08130V0Q1J151b0W091i161f0a1g1k0o0b1a1d1h191x0c171B1s0j1A1l"
+    "1z1q1y0q1r0r1w0s1e0p181j1m1v1n1D0t1o1c1t1C1u1E0u0v1p1G0w0x0X0y1F0K0z1I1H0A0M1O1L1P1Q1M0B1R1S1N1T1U1W1V1Y1X201Z220R210S2423262527282a"
+    "292c2b2d2g2h2e1K2f2j2k2m2A2l2n2o2B2i2s2p2q2r2C2t2w2v2u0U2D2x2E2N2y2F2z2G2H2I2J2K2L2M2R2Q2P2O2V2S2T2Z2U2W2X2Y3233313035383739343i3c36"
+    "3a3f3g3h3j3v3d3k3b3w3e3t3n3l3u3r3o3x3q3s3y3m3A3p3B3D3F3z3K3E3C3H3N3L3I3R3M3J3P3O3G3T3Q453S3W4443473V4841464a3X40494c3U3Y4b3Z4d424f4e"
+    "4h4g4l4m4i4n4o4j4p4q4k4r4s4t4v4x4u4w4z4y4B4A4D4C4E4F4H4G4J4I4K4O4N4L4M4R4Q4T5b4S4U4V5a594Z4W4P5c534Y4X57505d51525e545f55565I585s5v5g"
+    "5u5w5h5t5z5j5y5i5x5k5l5m5n5q5o5p5A5D5C5B5G5J5H5F5K5r5T5N5E5R5Q5S5U5M665V5L69675O5P5Y645W65615X68605Z6c626e636d6a6b6f6g6i6h6j6k6l6p6n"
+    "6m6q6r6o6s",
+    "000102030405060C0d0e0g070E0F0f0D0i0V0h0G0I0O0J0P0Q0Y0S0l0H0m0K120k0Z1110140n0813151b0W09161g1c0a181d1i0o1e0b171h1v1a0c1k1l1f0j1w1o1C"
+    "1u1D1m0q1z1q0r0s1y1r0p1A191p1x0t1j1t1B1E1s0u0v1n1G0w0U0T0x0X1J1F0y1I0z1H0L0A1O1L1P1Q1M1S0B1N1U1R1W1Y1T0R1X22201V1K26241Z28212a2c2325"
+    "2e2g2h0M272j2l2m2b2k2n2o2A2p2s2r2q292t2w2v2u2d2x2f2B2y2z2C2i2D0N2E2F2G2H2V2J2T2I2S2K2U2L2W2Z2X2M2Y2O2P2R2Q30313233342N383736393i3c35"
+    "3b3f3e3j3g3v3k3a3u3d3h3m3t3l3w3n3q3x3p3o3A3r3z3s3y3D3K3B3F3E3C3J3O3L3G3R3N3I3P3M3H3T3Q44463X4c3U45404b3V4a3Z3S3W483Y474249434d414f4e"
+    "4h4g4l4i4m4n4j4p4k4r4o4t4v4q4u4x4z4s4B4D4w4F4H4J4y4A4L4O4N4E4C4S4Q4T4G4R4U4V4K594Y4Z4X4W4I525351504M5a545b57554P565c585d5e5f5g5i5h5j"
+    "5k5t5s5u5x5r5l5w5y5o5n5v5p5m5B5A5C5z5F5I5E5J5S5Q5H5K5D5q5M5N5G685P5T5L5U5O5R636164655V665X5Y675W5Z6c6b60626d696a6e6f6h6g6i6j6k6p6m6l"
+    "6o6q6n6r",
+]
 
 
 def sb(n, t):
@@ -24,29 +47,30 @@ SCRATCH = {
     "vq": sb(128, Q4), "vs": sb(128, U8),
     "wq": sb(512, Q4), "wp": sb(512, U8), "zq": sb(512, Q4), "zp": sb(512, U8),
     "x0": sb(4 * (C + K), BF), "x1": sb(4 * (C + K), BF), "x2": sb(4 * C, BF),
-    "xq": sb(C, Q4), "xs": sb(C, U8),
-    "tt": sb(C, FP), "msk": sb(NPIV * C, BF), "cnt": sb(NPIV * H, BF), "gsum": sb(NS, FP),
-    "zz": sb(2 * C, BF), "rows": sb(3 * 336, BF), "cut": sb(2 * NPIV, BF),
-    "yb": sb(2 * C, BF), "yr": sb(2 * C, BF), "wr": sb(2 * C, BF), "eq": sb(2 * C, BF), "vr": sb(2 * C, BF),
-    "mx": sb(2 * H, BF), "nn": sb(1, FP),
+    "xq": sb(C + R * K, Q4), "xs": sb(C + R * K, U8),
+    "tt": sb(C, FP), "msk": sb(NPIV * SW, BF), "cum": sb(2 * CW, HF), "cnt": sb(NPIV, BF), "gsum": sb(NPIV, FP),
+    "zr": sb(RW, BF), "zz": sb(C, BF), "yb": sb(C, BF), "yr": sb(C, BF),
+    "zf": sb(2 * C, HF), "ybf": sb(2 * C, HF), "yrf": sb(2 * C, HF), "mxf": sb(2 * H, HF), "mx": sb(2 * H, BF),
+    "sg": sb(2 * C, BF), "sn": sb(8, FP), "se": sb(8, BF), "cut": sb(2 * NPIV, BF),
+    "wr": sb(2 * RW, BF), "eq": sb(2 * RW, BF), "vr": sb(2 * RW, BF), "rows": sb(3 * RW, BF),
     "lm": sb(4 * C, BF), "lc": sb(4 * H, FP),
     "sel": sb(C, BF), "sel5": sb(5 * C + 64, BF), "sel3": sb(3 * C + 32, BF), "co5": sb(5 * NPIV, FP), "co3": sb(3 * NPIV, FP),
     "al5": sb(5 * NPIV, FP), "al3": sb(3 * NPIV, FP), "sm": sb(2 * NPIV, FP), "er": sb(2 * EW, BF),
     "offb": sb(16, U16), "offt": sb(4 * NPIV, U16), "offd": sb(NPIV, U16), "offe": sb(NPIV, U16), "offu": sb(16, U16),
-    "offl": sb(4, U16), "larr": sb(4, U16), "rl": sb(4, U16),
-    "bt": sb(1024, BF), "bq0": sb(128, Q4), "bs0": sb(128, U8), "bq1": sb(128, Q4), "bs1": sb(128, U8),
-    "lq": sb(256, Q4), "ls": sb(256, U8),
+    "offl": sb(4, U16), "larr": sb(4, U16), "rl": sb(4, U16), "offw": sb(2, U16),
+    "bt": sb(768, BF), "bq0": sb(128, Q4), "bs0": sb(128, U8), "bq1": sb(128, Q4), "bs1": sb(128, U8),
     "rq0": sb(K, Q4), "rs0": sb(K, U8), "rq1": sb(K, Q4), "rs1": sb(K, U8),
     "tb": sb(4 * C + 8, BF), "tq": sb(C, Q4), "ts": sb(C, U8), "t2q": sb(C, Q4), "t2s": sb(C, U8),
-    "ew": sb(520, BF), "eq4": sb(512, Q4), "es4": sb(512, U8),
+    "ew": sb(2 * C, BF), "eq4": sb(512, Q4), "es4": sb(512, U8), "j16": sb(16, BF), "oh": sb(16, BF),
     "iu": sb(16, I32), "qi": sb(2, I32), "qf": sb(1, FP), "kk": sb(NPIV, FP), "kq": sb(NPIV, FP), "rc": sb(NPIV, FP),
-    "thr": sb(4, BF), "thrh": sb(4, FP), "jm": sb(C, BF), "csel": sb(C, BF), "chold": sb(C, BF), "cval": sb(C, BF),
+    "thr": sb(4, BF), "thrh": sb(4, FP), "thr2": sb(4, BF), "thrh2": sb(4, FP),
+    "jm": sb(C, BF), "csel": sb(C, BF), "chold": sb(C, BF), "cval": sb(C, BF),
     "olw": sb(C + K, FP), "olr": sb(C, FP), "yo": sb(C, FP),
 }
 for _b in range(8):
     SCRATCH["p%d" % _b] = ("psum", [128, 512], FP)
 
-POOLS = {"v": 54, "s": 30, "t": 24, "g": 14, "d": 22}
+POOLS = {"v": 46, "s": 28, "t": 20, "g": 30, "d": 20}
 SEMAPHORES = ["aq0", "aq1", "as0", "as1", "al", "sent"] + ["%s%d" % (k, i) for k in POOLS for i in range(POOLS[k])]
 
 
@@ -75,8 +99,8 @@ def halves(topo, src, dst):
 
 
 def land(T, t):
-    a = 0 if t == 0 else 192
-    return T.lq[:, a:a + K].bitcast(dt.uint8), T.ls[:, a:a + K]
+    a = C + K * t
+    return T.xq[:, a:a + K].bitcast(dt.uint8), T.xs[:, a:a + K]
 
 
 def hand_on(g, core, T, topo):
@@ -172,11 +196,8 @@ def emit(g, T, ops):
         ins.then_inc(T.sem[mark[end][0]], step)
 
 
-def rank_program(g, core, T, topo):
+def plan(core, T, topo, cfg):
     rank = T.rank_of(core)
-    if rank is None:
-        hand_on(g, core, T, topo)
-        return
     n_ranks = len(T.cores)
     ops = []
 
@@ -210,9 +231,6 @@ def rank_program(g, core, T, topo):
         else:
             copy(out, in_, rd, wr, kind + q)
 
-    def fill(ap, c, wr):
-        op("v", lambda e: e.memset(ap, c), [], wr)
-
     def quant(q, s, in_, rd, wr, kind=""):
         op("v", lambda e: e.quantize_mx(q, s, in_), rd, wr, kind)
 
@@ -223,7 +241,7 @@ def rank_program(g, core, T, topo):
     def turn(out, in_, rd, wr):
         op("v", lambda e: e.transpose(out, in_), rd, wr)
 
-    def iota(out, pattern, base, cm, wr, small=False):
+    def iota(out, pattern, base, cm, wr, small=True):
         if small:
             op("g", lambda e: e.iota(out, pattern, base, cm, allow_small_or_imprecise_dtypes=True), [], wr)
         else:
@@ -251,100 +269,146 @@ def rank_program(g, core, T, topo):
     op("x", ("al", ns), [], ["larr"])
 
     X = [T.x0, T.x1, T.x2]
-    Lr, Nr, Ar = 0, 336, 672
+    Lr, Nr, Ar = 0, RW, 2 * RW
 
     def xkeys(t, h):
         return ["x0_%d" % h] if t == 0 else ["x%d_%d_%d" % (t, h, b) for b in range(4)]
 
-    def early(step):
-        if step == 0:
-            mm(0, EARLY, T.uq[:], T.us[:], T.xq[:, 0:EARLY], T.xs[:, 0:EARLY], ["uq", "xq0"])
-        else:
-            turn(T.tt[:, 0:EARLY], T.p0[:, 0:EARLY], ["#0"], ["tta"])
-
-    x0 = 4 * (H - 2)
-    dma("y", T.ut[:], T.u[:], [], ["ut"])
-    dma("s", T.x0[:, 0:x0], T.x[:, 0:x0], [], ["x0_0"])
-    dma("s", T.x0[:, x0:4 * C], T.x[:, x0:4 * C], [], ["x0_1"])
-    dma("y", T.wq[:].bitcast(dt.uint8), T.wc[:], ["x0_0", "x0_1"], ["wq"])
-    dma("y", T.zq[:].bitcast(dt.uint8), T.zc[:], [], ["zq"])
-    dma("y", T.wp[:], T.ws[:], [], ["wp"])
-    dma("y", T.zp[:], T.zs[:], [], ["zp"])
-    dma("y", T.vt[:], T.v[:], [], ["vt"])
-
-    iota(T.iu[:], [[16, 2], [32, 4], [0, 2]], 0, 0, ["iu"])
-    iota(T.qi[:, 0:1], [[0, 1]], 0, 1, ["qi0"])
-    iota(T.kk[:], [[16, NPIV]], 0, 0, ["kk"], True)
-    iota(T.jm[:], [[0, NPIV], [1, 16]], 0, 0, ["jm"], True)
-    iota(T.zz[:], [[0, 2 * C]], 0, 0, ["zz0", "zz1"], True)
-    iota(T.bt[:, 256:768], [[0, 512]], 0, 0, ["btz"], True)
-    iota(T.cval[:], [[1, C]], -192, 0, ["cval"], True)
-    iota(T.er[:, 0:C], [[0, C]], 1, 0, ["er0"], True)
-    iota(T.ew[:], [[0, 520]], 1, 0, ["ew"], True)
-    op("g", lambda e: e.affine_select(T.ew[:], T.ew[:], [[-1, 520]], A.is_equal, 0.0, 3, 4), ["ew"], ["ew"])
-    iota(T.er[:, EW:EW + C], [[0, C]], 1, 0, ["er1"], True)
-    iota(T.olw[:, 0:C], [[1, C]], 0, 0, ["olw0"], True)
-    fill(T.rows[:, Lr:Ar:Nr], 0.0, ["rows0"])
-    fill(T.rows[:, Ar:Ar + 1], 1.0, ["rows1"])
-    fill(T.co5[:, 0::5], 0.0, ["co50"])
-    fill(T.co5[:, 3::5], -0.5, ["co53"])
-    fill(T.co5[:, 4::5], 0.0, ["co54"])
-    copy(T.offu[:], T.iu[:], ["iu"], ["offu"])
-    ts(T.qi[:, 1:2], T.qi[:, 0:1], 15, A.bitwise_and, ["qi0"], ["qi1"])
-    fill(T.sel5[:, 139::80], 0.0, ["s54"])
-    fill(T.co3[:, 0::3], 0.0, ["co30"])
-    copy(T.qf[:], T.qi[:, 1:2], ["qi1"], ["qf"])
-    fill(T.co3[:, 1::3], -(1.0 + 1.0 / 512), ["co31"])
-    fill(T.co3[:, 2::3], 1.0, ["co32"])
-    fill(T.sel3[:, 77::48], 386.0 / 512, ["s32"])
-    act(T.kq[:], T.kk[:], F.Identity, ["kk", "qf"], ["kq"], bias=T.qf[:])
-    act(T.co5[:, 2::5], T.kq[:], F.Identity, ["kq"], ["co52"], bias=float(-C), scale=-1.0)
-    act(T.thr[:], T.kq[:, 0:4], F.Copy, ["kq"], ["thr"], "+k")
-    act(T.thrh[:], T.kq[:, 0:4], F.Identity, ["kq"], ["thrh"], "+k", bias=0.5)
-    act(T.sel5[:, 123::80], T.kq[:], F.Identity, ["kq"], ["s53"], "+k", bias=float(-H))
-    op("v", lambda e: e.reciprocal(T.rc[:], T.co5[:, 2::5]), ["co52"], ["rc"])
-    ts(T.chold[:], T.jm[:], 0.0, A.is_gt, ["jm"], ["chold"])
-    act(T.co5[:, 1::5], T.rc[:], F.Identity, ["rc"], ["co51"], bias=-1.0)
-    quant(T.uq[:], T.us[:], T.ut[:], ["ut"], ["uq"])
-    quant(T.xq[:, 0:H - 2], T.xs[:, 0:H - 2], T.x0[:, 0:x0], ["x0_0"], ["xq0"])
-    copy(T.u2q[:].bitcast(dt.uint32), T.uq[:].bitcast(dt.uint32).indirect(T.offu[:]), ["uq", "offu"], ["u2q"])
-    act(T.u2s[:], T.us[:].indirect(T.offu[:]), F.Copy, ["uq", "offu"], ["u2s"])
-    act(T.csel[:], T.jm[:], F.Abs, ["jm", "qf"], ["csel"], bias=T.qf[:], scale=-1.0)
-    early(0)
-    quant(T.xq[:, H - 2:C], T.xs[:, H - 2:C], T.x0[:, x0:4 * C], ["x0_1"], ["xq1"])
-    early(1)
-
     def useg(i):
         return T.u2q[:, 128 * i:128 * i + 128], T.u2s[:, 128 * i:128 * i + 128]
 
-    ends = T.cnt[:, H - 1::H]
-    cnts = ["cnt%d" % k for k in range(NPIV)]
+    def tk(k):
+        return "tta" if 16 * k < EARLY else "ttb"
 
-    def cut(s, limit, row):
+    def mrow(k, a, z):
+        s = SW * (k // 2 + NG * (k % 2))
+        return T.msk[:, s + a:s + z]
+
+    def sign(t, k, bank, a, z, wr):
+        i = k // 2 + (NG if z < C else 0)
+        act(mrow(k, a, z), T["p%d" % bank][:, a:z], F.Sign, ["#%d" % bank, tk(k), "gz"], wr, "+sg%d_%d" % (t, z == C),
+            bias=T.tt[:, 16 * k:16 * k + 1], scale=-1.0, accum_out=T.gsum[:, i:i + 1])
+
+    def above(t, k, bank, a, z, wr):
+        ts(mrow(k, a, z), T["p%d" % bank][:, a:z], T.tt[:, 16 * k:16 * k + 1], A.is_gt, ["#%d" % bank, tk(k)], wr, -2.0, A.mult,
+           "+cm%d_%d" % (t, k // NG) if z == C else "+ce%d" % t)
+
+    def early(t):
+        mm(0, EARLY, T.uq[:], T.us[:], T.xq[:, 0:EARLY], T.xs[:, 0:EARLY], ["uq", "xq0"])
+        turn(T.tt[:, 0:EARLY], T.p0[:, 0:EARLY], ["#0"], ["tta"])
+        for bank, i, call in ((1, 0, sign), (2, 1, above)):
+            q, s = useg(i)
+            mm(bank, FIRST, q, s, T.xq[:, 0:FIRST], T.xs[:, 0:FIRST], ["u2q", "u2s", "xq0"])
+            for k in range(i, EARLY // 16, 2):
+                call(t, k, bank, 0, FIRST, ["n%d" % k])
+
+    def rest(t, k, call, bank):
+        if 16 * k < EARLY:
+            call(t, k, bank, FIRST, C, ["m%d" % k])
+        else:
+            call(t, k, bank, 0, C, ["m%d" % k, "n%d" % k])
+
+    x0 = 4 * FIRST
+    dma("y", T.ut[:], T.u[:], [], ["ut"])
+    dma("s", T.x0[:, 0:x0], T.x[:, 0:x0], [], ["x0_0"])
+    dma("y", T.x0[:, x0:4 * C], T.x[:, x0:4 * C], [], ["x0_1"])
+    dma("y", T.wq[:].bitcast(dt.uint8), T.wc[:], ["x0_0", "x0_1"], ["wq"])
+    dma("y", T.zq[:].bitcast(dt.uint8), T.zc[:], ["x0_1"], ["zq"])
+    dma("y", T.wp[:], T.ws[:], ["x0_1"], ["wp"])
+    dma("y", T.zp[:], T.zs[:], ["x0_1"], ["zp"])
+    dma("y", T.vt[:], T.v[:], ["x0_1"], ["vt"])
+
+    iota(T.qi[:, 0:1], [[0, 1]], 0, 1, ["qi0"], False)
+    iota(T.j16[:], [[1, 16]], 0, 0, ["j16"])
+    iota(T.iu[:], [[16, 2], [32, 4], [0, 2]], 0, 0, ["iu"], False)
+    iota(T.kk[:], [[16, NPIV]], 0, 0, ["kk"])
+    iota(T.jm[:], [[0, NPIV], [1, 16]], 0, 0, ["jm"])
+    iota(T.gsum[:, NG:NPIV], [[0, NG]], 0, 0, ["gz"])
+    iota(T.zr[:], [[0, RW]], 0, 0, ["zr"])
+    iota(T.zz[:], [[0, C]], 0, 0, ["zz2"])
+    iota(T.msk[:, C::SW], [[0, NPIV]], C, 0, ["pad0"])
+    iota(T.msk[:, C + 1::SW], [[0, NPIV]], 0, 0, ["pad1"])
+    iota(T.er[:, 16:16 + C], [[0, C]], 1, 0, ["er0"])
+    op("g", lambda e: e.affine_select(T.chold[:], T.er[:, 16:16 + C], [[0, NPIV], [1, 16]], A.is_gt, 0.0, 0, 0), ["er0"], ["chold"])
+    iota(T.bt[:, 256:512], [[0, 256]], 0, 0, ["btz"])
+    iota(T.eq[:, C::RW], [[2 * K - C, 2]], -K, 0, ["eqp"])
+    iota(T.vr[:, 0::RW], [[0, 2]], -1024, 0, ["vrp"])
+    iota(T.wr[:, 0::RW], [[0, 2]], 0, 0, ["wrp"])
+    iota(T.cval[:], [[1, C]], -192, 0, ["cval"])
+    iota(T.co5[:, 0::5], [[0, NPIV]], 0, 0, ["co50"])
+    iota(T.co5[:, 4::5], [[0, NPIV]], 0, 0, ["co54"])
+    iota(T.sel5[:, 139::80], [[0, NPIV]], 0, 0, ["s54"])
+    iota(T.rows[:, Ar:Ar + 1], [[0, 1]], 1, 0, ["erz"])
+    iota(T.co3[:, 0::3], [[0, NPIV]], 0, 0, ["co30"])
+    iota(T.co3[:, 2::3], [[0, NPIV]], 1, 0, ["co32"])
+    iota(T.er[:, EW + 16:EW + 16 + C], [[0, C]], 1, 0, ["er1"])
+    iota(T.olw[:, 0:C], [[1, C]], 0, 0, ["olw0"])
+    op("v", lambda e: e.memset(T.ew[:], 0.0), [], ["ew"])
+    copy(T.zf[:], T.ew[:], ["ew"], ["zz0", "zz1"])
+    ts(T.qi[:, 1:2], T.qi[:, 0:1], 15, A.bitwise_and, ["qi0"], ["qi1"])
+    ts(T.offw[:, 0:1], T.qi[:, 0:1], 4.0, A.mult, ["qi0"], ["offw"], 3.0, A.add)
+    copy(T.qf[:], T.qi[:, 1:2], ["qi1"], ["qf"])
+    copy(T.offu[:], T.iu[:], ["iu"], ["offu"])
+    ts(T.oh[:], T.j16[:], T.qf[:], A.is_equal, ["j16", "qf"], ["oh"])
+    copy(T.ew[:].indirect(T.offw[:, 0:1]), T.oh[:], ["oh", "offw"], ["ew"])
+    for b in range(4):
+        quant(T.eq4[:, 128 * b:128 * b + 128], T.es4[:, 128 * b:128 * b + 128], T.ew[:, 3 - b:515 - b], ["ew"], ["e%d" % b])
+    act(T.kq[:], T.kk[:], F.Identity, ["kk", "qf"], ["kq"], bias=T.qf[:])
+    act(T.co5[:, 2::5], T.kq[:], F.Identity, ["kq"], ["co52"], bias=float(-C), scale=-1.0)
+    act(T.thr[:], T.kq[:, 0:4], F.Copy, ["kq"], ["thr"])
+    act(T.thrh[:], T.kq[:, 0:4], F.Identity, ["kq"], ["thrh"], bias=0.5)
+    act(T.sel5[:, 123::80], T.kq[:], F.Identity, ["kq"], ["s53"], bias=float(-H))
+    act(T.co5[:, 3::5], T.kk[:], F.Identity, ["kk"], ["co53"], bias=-0.5, scale=0.0)
+    act(T.co3[:, 1::3], T.kk[:], F.Identity, ["kk"], ["co31"], bias=-(1.0 + 1.0 / 512), scale=0.0)
+    act(T.sel3[:, 77::48], T.kk[:], F.Identity, ["kk"], ["s32"], bias=386.0 / 512, scale=0.0)
+    op("v", lambda e: e.reciprocal(T.rc[:], T.co5[:, 2::5]), ["co52"], ["rc"])
+    act(T.co5[:, 1::5], T.rc[:], F.Identity, ["rc"], ["co51"], bias=-1.0)
+    quant(T.uq[:], T.us[:], T.ut[:], ["ut"], ["uq"])
+    quant(T.xq[:, 0:FIRST], T.xs[:, 0:FIRST], T.x0[:, 0:x0], ["x0_0"], ["xq0"])
+    copy(T.u2q[:].bitcast(dt.uint32), T.uq[:].bitcast(dt.uint32).indirect(T.offu[:]), ["uq", "offu"], ["u2q"])
+    act(T.u2s[:], T.us[:].indirect(T.offu[:]), F.Copy, ["uq", "offu"], ["u2s"])
+    act(T.csel[:], T.jm[:], F.Abs, ["jm", "qf"], ["csel"], bias=T.qf[:], scale=-1.0)
+    quant(T.xq[:, FIRST:C], T.xs[:, FIRST:C], T.x0[:, x0:4 * C], ["x0_1"], ["xq1"])
+    early(0)
+
+    ends = T.cnt[:]
+    cnts = ["cnt0", "cnt1", "cnt11"]
+
+    def cut(s, at, start, row):
         def k(name):
             return "%s%d" % (name, s)
 
         def w(buf, n=C):
             return buf[:, n * s:n * s + n]
 
-        c, top = w(T.cut, NPIV), T.mx[:, H * s + H - 1:H * s + H]
-        first = (T.nn[:], "nn") if limit else (top, k("mx"))
+        def key(i):
+            return T.se[:, 4 * s + i:4 * s + i + 1]
+
+        c, top, bot, a = w(T.cut, NPIV), T.mxf[:, H * s + H - 1:H * s + H], T.mx[:, H * s + H - 1:H * s + H], RW * s
+        y0, y1, n = T.yrf[:, C * s:C * s + H], T.yrf[:, C * s + H:C * s + C], T.sn[:, 4 * s:4 * s + 1]
         return {
-            "c": lambda: ts(c, ends, float(limit), A.is_ge, cnts, [k("cut")], -512.0, A.mult),
-            "z": lambda: tt(T.zz[:, C * s:C * s + C:16], ends, c, A.min, cnts + [k("cut")], [k("zz")]),
-            "spread": lambda: scan(w(T.yb), T.chold[:], w(T.zz), 0.0, A.mult, A.add, ["chold", k("zz")], [k("yb")]),
-            "turn": lambda: turn(w(T.yr), w(T.yb), [k("yb")], [k("yr")]),
-            "out": lambda: act(w(T.wr), w(T.yr), F.Relu, [k("yr")], [k("wr")], bias=-1.0, scale=-1.0 / 256),
-            "top": lambda: scan(w(T.mx, H), T.yr[:, C * s:C * s + H], T.yr[:, C * s + H:C * s + C], -1024.0, A.max, A.max,
-                                [k("yr")], [k("mx")]),
-            "eq": lambda: ts(w(T.eq), w(T.yr), top, A.is_equal, [k("yr"), k("mx")], [k("eq")]),
-            "n": lambda: ts(T.nn[:], top, float(-limit), A.add, [k("mx")], ["nn"]),
-            "v": lambda: scan(w(T.vr), w(T.eq), w(T.wr), first[0], A.add, A.add, [k("eq"), k("wr"), first[1]], [k("vr")]),
-            "run": lambda: scan(T.rows[:, row + 1:row + 1 + C], w(T.wr), w(T.vr), 0.0, A.add, A.max, [k("wr"), k("vr")],
-                                ["row%d" % row]),
+            "c": lambda: ts(c, ends, float(at), A.is_le, cnts, [k("cut")], 1024.0, A.mult),
+            "z": lambda: tt(T.zf[:, C * s:C * s + C:16], ends, c, A.add, cnts + [k("cut")], [k("zz")]),
+            "spread": lambda: scan(w(T.ybf), T.chold[:], w(T.zf), 0.0, A.mult, A.add, ["chold", k("zz")], [k("yb")]),
+            "turn": lambda: turn(w(T.yrf), w(T.ybf), [k("yb")], [k("yr")]),
+            "n": lambda: act(w(T.sg), T.yr[:], F.Sign, ["yr2"], [k("sn")], bias=-at - 0.5, accum_out=n),
+            "top": lambda: scan(w(T.mxf, H), y0, y1, -2048.0, A.max, A.max, [k("yr")], [k("mx")]),
+            "bot": lambda: scan(w(T.mx, H), y0, y1, 2048.0, A.min, A.min, [k("yr")], [k("mn")]),
+            "d": lambda: ts(key(0), top, 1024.0, A.subtract, [k("mx")], [k("dd")]),
+            "a": lambda: ts(key(1), n, float(-at), A.is_ge, [k("sn"), k("mn")], [k("aa")], bot, A.mult),
+            "e": lambda: ts(key(2), n, float(-at), A.is_lt, [k("sn"), k("dd")], [k("ee")], key(0), A.mult),
+            "with": lambda: ts(T.eq[:, a:a + C], T.yr[:], key(1), A.subtract, ["yr2", k("aa"), k("ee")], [k("eq")],
+                               key(2), A.is_le),
+            "past": lambda: ts(T.wr[:, a + 1:a + 1 + C], T.yr[:], key(1), A.subtract, ["yr2", k("aa"), k("ee")], [k("wr")],
+                               key(2), A.is_lt),
+            "v": lambda: scan(T.vr[:, a + 1:a + 2 + C], T.eq[:, a:a + C + 1], T.zr[:, 0:C + 1], float(start), A.add, A.add,
+                              [k("eq"), "eqp", "zr"], [k("vr")]),
+            "run": lambda: scan(T.rows[:, row:row + 1 + C], T.wr[:, a:a + 1 + C], T.vr[:, a:a + 1 + C],
+                                T.vr[:, a + 1 + C:a + 2 + C], A.add, A.max, [k("wr"), k("vr"), "wrp", "vrp"], ["row%d" % row]),
         }
 
-    lo, hi = cut(0, 0, Lr), cut(1, -192, Nr)
+    lo, hi = cut(0, -192, -192, Lr), cut(1, 192, -128, Nr)
+    il, ih = T.vr[:, C + 1:C + 2], T.vr[:, RW + C + 1:RW + C + 2]
 
     def select(out, row, rd, wr):
         scan(out, T.csel[:], row, 0.0, A.add, A.min, ["csel"] + rd, wr)
@@ -355,183 +419,112 @@ def rank_program(g, core, T, topo):
     def sm(i):
         return T.sm[:, NPIV * i:NPIV * i + NPIV]
 
-    def mrow(k):
-        return T.msk[:, C * k:C * k + C]
-
     for t in range(R):
-        x, xk = X[t], xkeys(t, 0) + xkeys(t, 1)
+        x, xk, cf = X[t], xkeys(t, 0) + xkeys(t, 1), cfg[t]
         last = t == R - 1
         both = ["xq0", "xq1"]
-        mm(1, C - EARLY, T.uq[:], T.us[:], T.xq[:, EARLY:C], T.xs[:, EARLY:C], ["uq"] + both)
-        for bank, i in ((2, 0), (3, 1), (4, 0)):
-            a, b = useg(i)
-            mm(bank, C, a, b, T.xq[:], T.xs[:], ["u2q", "u2s"] + both)
-        turn(T.tt[:, EARLY:C], T.p1[:, 0:C - EARLY], ["#1"], ["ttb"])
+        for bank, i in ((4, 1), (5, 0), (6, None)):
+            if i is None:
+                mm(bank, C - EARLY, T.uq[:], T.us[:], T.xq[:, EARLY:C], T.xs[:, EARLY:C], ["uq"] + both)
+            else:
+                a, b = useg(i)
+                mm(bank, C, a, b, T.xq[:, 0:C], T.xs[:, 0:C], ["u2q", "u2s"] + both)
 
-        def tk(k):
-            return "tta" if 16 * k < EARLY else "ttb"
-
-        def sign(k):
-            act(mrow(k), T.p2[:, 0:C], F.Sign, ["#2", tk(k)], ["m%d" % k], bias=T.tt[:, 16 * k:16 * k + 1], scale=-1.0)
-
-        shared = 2 * NS
-        for i in range(NS + 1):
-            if i < NS:
-                sign(2 * i)
-            if i == 3:
-                sign(shared)
-            if i > 0:
-                k = 2 * i - 2
-                act(mrow(k), mrow(k), F.Relu, ["m%d" % k], ["m%d" % k, "gs%d" % k], "+gs%d" % t, scale=-1.0,
-                    accum_out=T.gsum[:, i - 1:i])
-        act(T.cnt[:, H - 1:2 * H * NS:2 * H], T.gsum[:], F.Identity, ["gs%d" % (2 * i) for i in range(NS)],
-            ["cnt%d" % (2 * i) for i in range(NS)], bias=-256.0)
-        mine = [k for k in range(NPIV) if k % 2] + [shared] + [k for k in range(shared + 2, NPIV, 2)]
-        for i in range(len(mine) + 1):
-            if i < len(mine):
-                k = mine[i]
-                bank = 3 if k % 2 else 4
-                if k == shared:
-                    ts(mrow(k), mrow(k), 0.0, A.is_lt, ["m%d" % k], ["m%d" % k])
-                else:
-                    ts(mrow(k), T["p%d" % bank][:, 0:C], T.tt[:, 16 * k:16 * k + 1], A.is_gt, ["#%d" % bank, tk(k)],
-                       ["m%d" % k])
-            if i > 0:
-                k = mine[i - 1]
-                scan(T.cnt[:, H * k:H * k + H], T.msk[:, C * k:C * k + H], T.msk[:, C * k + H:C * k + C], -256.0, A.add,
-                     A.add, ["m%d" % k], ["cnt%d" % k], "+cnt%d" % t)
+        rest(t, 1, above, 4)
+        turn(T.tt[:, EARLY:C], T.p6[:, 0:C - EARLY], ["#6"], ["ttb"])
+        for k in range(0, NPIV, 2):
+            rest(t, k, sign, 5)
+        for k in range(3, NPIV, 2):
+            rest(t, k, above, 4)
+        for i in range(2):
+            ks, s0, n = range(1 + NG * i, NG + NG * i, 2), NG + NG // 2 * i, NG // 2 * (H + 1)
+            scan(T.cum[:, CW * i:CW * i + n + 1], T.msk[:, SW * s0 - 2:SW * s0 + 2 * n:2], T.msk[:, SW * s0 - 1:SW * s0 + 2 * n:2],
+                 0.0, A.add, A.add, ["pad0", "pad1"] + ["m%d" % k for k in ks] + ["n%d" % k for k in ks], ["cum%d" % i])
+            tt(T.cnt[:, ks[0]:NG + NG * i:2], T.cum[:, CW * i + H + 1:CW * i + n + 1:H + 1], T.cum[:, CW * i:CW * i + n:H + 1],
+               A.subtract, ["cum%d" % i], ["cnt%d" % ks[0]])
+        tt(T.cnt[:, 0:NPIV:2], T.gsum[:, 0:NG], T.gsum[:, NG:NPIV], A.add,
+           ["gz"] + [p + str(k) for k in range(0, NPIV, 2) for p in "mn"], ["cnt0"])
 
         if t == 0:
             act(T.csel[:], T.csel[:], F.Relu, ["csel"], ["csel"], bias=1024.0, scale=-1024.0)
             act(T.cval[:], T.cval[:], F.Copy, ["cval"], ["cval"], scale=TINY)
         lcs = ["lc%d" % k for k in range(4)]
         lends = T.lc[:, H - 1::H]
-        b0, c0, e0 = 768 * t, K * t, EW * t
+        b0, c0, e0 = 512 * t, K * t, EW * t + 16
         er = T.er[:, e0:e0 + C]
         bq, bs = T["bq%d" % t], T["bs%d" % t]
 
         def count_s(k):
             m = min(16 * k, C - LW - 16 * k)
-            act(T.lm[:, C * k + m:C * k + C - m], T.rows[:, Lr + 1 + m:Lr + 1 + C - m], F.Sign, ["row0", "thrh"],
-                ["lm%d" % k, "lc%d" % k], "+ld%d" % t, bias=T.thrh[:, k:k + 1], scale=-1.0,
+            act(T.lm[:, C * k + m:C * k + C - m], T.rows[:, Lr + 1 + m:Lr + 1 + C - m], F.Sign, ["row0", "thrh2"],
+                ["lc%d" % k, "lm%d" % k], "+ld%d" % t, bias=T.thrh2[:, k:k + 1], scale=-1.0,
                 accum_out=T.lc[:, H * k + H - 1:H * k + H])
 
         def mask_v(k):
-            ts(T.lm[:, C * k:C * k + LW], T.rows[:, Lr + 1 + 16 * k:Lr + 1 + 16 * k + LW], T.thr[:, k:k + 1], A.is_le,
-               ["row0", "thr"], ["lm%d" % k], 2.0, A.mult)
+            ts(T.lm[:, C * k:C * k + LW], T.rows[:, Lr + 1 + 16 * k:Lr + 1 + 16 * k + LW], T.thr2[:, k:k + 1], A.is_le,
+               ["row0", "thr2"], ["lm%d" % k], 2.0, A.mult)
 
         def count_v(k):
             scan(T.lc[:, H * k + H - LW // 2:H * k + H], T.lm[:, C * k:C * k + LW // 2], T.lm[:, C * k + LW // 2:C * k + LW],
                  float(32 * k - C), A.add, A.add, ["lm%d" % k], ["lc%d" % k], "+lc%d" % t)
 
-        def border_offsets():
-            for j in (0, 2, 1, 3):
-                ts(T.offb[:, 4 * j:4 * j + 4], lends, 2.0, A.mult, lcs, ["offb%d" % j], float(640 + j), A.add)
+        def pick(r):
+            row, a = ((Lr, 0), (Lr, 1), (Nr, 0))[r]
+            select(turns(T.sel5, 5, r), T.rows[:, row + a:row + a + C], ["row%d" % row], ["s5%d" % r])
 
-        def border_gathers():
-            for j in range(4):
-                move(BQ[t][j], T.bt[:, b0 + j:b0 + 4 * K:4], x[:, 0:4 * C].indirect(T.offb[:, 4 * j:4 * j + 4]),
-                     xk + ["offb%d" % j], ["bt%d_%d" % (t, j)], "+b%d" % t)
+        def scatter(a, z):
+            copy(T.er[:, e0:e0 + EW - 16].indirect(T.offd[:, a:z]), T.cval[:, 16 * a:16 * z], ["cval", "offd"], ["er%d" % t])
 
-        def border_out():
-            quant(bq[:], bs[:], T.bt[:, 512 * t:512 * t + 512], ["btz"] + ["bt%d_%d" % (t, j) for j in range(4)], ["bq%d" % t])
-            lq, ls = land(T, t)
-            src_q, src_s = bq[:, c0:c0 + K].bitcast(dt.uint8), bs[:, c0:c0 + K]
-            if cq is None:
-                send(lq, src_q, "aq%d" % t, dst, 0, ["bq%d" % t])
-                send(ls, src_s, "as%d" % t, dst, 1, ["bq%d" % t])
-            else:
-                send(T["rq%d" % t][:].bitcast(dt.uint8), src_q, "aq%d" % t, cq, 0, ["bq%d" % t])
-                send(T["rs%d" % t][:], src_s, "as%d" % t, cs, 1, ["bq%d" % t])
-
-        def list_out():
+        copy(T.zz[:, 0:C:16], ends, cnts, ["zz2"])
+        scan(T.yb[:], T.chold[:], T.zz[:], 0.0, A.mult, A.add, ["chold", "zz2"], ["yb2"])
+        turn(T.yr[:], T.yb[:], ["yb2"], ["yr2"])
+        for step in ("c", "z", "spread", "turn", "n", "top", "bot", "d", "a", "e", "with", "past", "v", "run"):
+            lo[step]()
+            hi[step]()
+        act(T.thrh2[:], T.thrh[:], F.Identity, ["thrh", "vr0"], ["thrh2"], bias=il)
+        act(T.thr2[:], T.thr[:], F.Identity, ["thr", "vr0"], ["thr2"], bias=il)
+        ts(T.sn[:, 3:4], il, ih, A.add, ["vr0", "vr1"], ["shift"], C + 0.25, A.add)
+        mask_v(0)
+        count_s(1)
+        count_s(2)
+        mask_v(3)
+        count_v(0)
+        count_v(3)
+        for j in (0, 2, 1, 3):
+            ts(T.offb[:, 4 * j:4 * j + 4], lends, 2.0, A.mult, lcs, ["offb%d" % j], float(640 + j), A.add)
+        for j in range(4):
+            move(cf["bq"][j], T.bt[:, b0 + j:b0 + 4 * K:4], x[:, 0:4 * C].indirect(T.offb[:, 4 * j:4 * j + 4]),
+                 xk + ["offb%d" % j], ["bt%d_%d" % (t, j)], "+b%d" % t)
+        quant(bq[:], bs[:], T.bt[:, 256 * t:256 * t + 512], ["btz"] + ["bt%d_%d" % (t, j) for j in range(4)], ["bq%d" % t])
+        lq, ls = land(T, t)
+        src_q, src_s = bq[:, c0:c0 + K].bitcast(dt.uint8), bs[:, c0:c0 + K]
+        if cq is None:
+            send(lq, src_q, "aq%d" % t, dst, 0, ["bq%d" % t])
+            send(ls, src_s, "as%d" % t, dst, 1, ["bq%d" % t])
+        else:
+            send(T["rq%d" % t][:].bitcast(dt.uint8), src_q, "aq%d" % t, cq, 0, ["bq%d" % t])
+            send(T["rs%d" % t][:], src_s, "as%d" % t, cs, 1, ["bq%d" % t])
+        if last:
             ts(T.offl[:], lends, 0.5, A.mult, lcs, ["offl"], 160.0, A.add)
             if cq is None:
                 send(T.larr[:], T.offl[:], "al", dst, 1, ["offl"])
             else:
                 send(T.rl[:], T.offl[:], "al", cs, 1, ["offl"])
-
-        def pick(r):
-            row, a, key = ((Lr, 0, "row0"), (Lr, 1, "row0"), (Nr, 0, "row336"))[r]
-            select(turns(T.sel5, 5, r), T.rows[:, row + a:row + a + C], [key, "rows0"], ["s5%d" % r])
-
-        def places():
-            scan(T.al5[:], T.co5[:], T.sel5[:, 75::16], 0.0, A.mult, A.add,
-                 ["s5%d" % i for i in range(5)] + ["co5%d" % i for i in range(5)], ["al5"])
-
-        def place_offsets():
-            ts(T.offd[:], T.al5[:, 3::5], 2.0, A.mult, ["al5"], ["offd"], C + 0.25, A.add)
-
-        def scatter(a, z):
-            copy(T.er[:, e0:e0 + EW].indirect(T.offd[:, a:z]), T.cval[:, 16 * a:16 * z], ["cval", "offd"], ["er%d" % t])
-
-        def unit(b):
-            quant(T.eq4[:, 128 * b:128 * b + 128], T.es4[:, 128 * b:128 * b + 128], T.ew[:, 3 - b:515 - b], ["ew"], ["e%d" % b])
-
-        for step in ("c", "z", "spread", "turn", "out", "top"):
-            lo[step]()
-            hi[step]()
-        if t == 0:
-            lo["eq"]()
-            hi["n"]()
-            lo["v"]()
-            hi["eq"]()
-            lo["run"]()
-            hi["v"]()
-            count_s(1)
-            count_s(2)
-            mask_v(0)
-            mask_v(3)
-            count_v(0)
-            count_v(3)
-            hi["run"]()
-            border_offsets()
-            border_gathers()
-            pick(0)
-            border_out()
-            pick(1)
-            pick(2)
-            quant(T.lq[:, 64:192], T.ls[:, 64:192], T.bt[:, 256:768], ["btz"], ["lz"])
-            places()
-            unit(0)
-            place_offsets()
-            unit(1)
-            scatter(0, NPIV)
-            unit(2)
-        else:
-            lo["eq"]()
-            hi["n"]()
-            hi["eq"]()
-            lo["v"]()
-            hi["v"]()
-            lo["run"]()
-            hi["run"]()
-            count_s(1)
-            count_s(2)
-            mask_v(0)
-            mask_v(3)
-            pick(0)
-            count_v(0)
-            count_v(3)
-            pick(1)
-            pick(2)
-            border_offsets()
-            border_gathers()
-            places()
-            place_offsets()
-            scatter(0, SPLIT)
-            border_out()
-            scatter(SPLIT, NPIV)
-            list_out()
+        for r in range(3):
+            pick(r)
+        scan(T.al5[:], T.co5[:], T.sel5[:, 75::16], 0.0, A.mult, A.add,
+             ["s5%d" % i for i in range(5)] + ["co5%d" % i for i in range(5)], ["al5"])
+        ts(T.offd[:], T.al5[:, 3::5], 2.0, A.mult, ["al5", "shift"], ["offd"], T.sn[:, 3:4], A.add)
+        if cf["split"]:
+            scatter(0, cf["split"])
+        scatter(cf["split"], NPIV)
         scan(T.rows[:, Ar + 1:Ar + 1 + C], er, er, 1.0, A.add, A.max, ["er%d" % t], ["row672"])
         select(T.sel[:], er, ["er%d" % t], ["sel"])
         select(turns(T.sel3, 3, 0), T.rows[:, Ar + 1:Ar + 1 + C], ["row672"], ["s30"])
-        select(turns(T.sel3, 3, 1), T.rows[:, Ar:Ar + C], ["row672", "rows1"], ["s31"])
+        select(turns(T.sel3, 3, 1), T.rows[:, Ar:Ar + C], ["row672", "erz"], ["s31"])
         ts(sm(0), T.sel[:, 15::16], -1.0 / (512 * TINY), A.mult, ["sel"], ["sm0"], -0.25, A.max)
         scan(T.al3[:], T.co3[:], T.sel3[:, 45::16], 0.0, A.mult, A.add,
              ["s30", "s31", "s32", "co30", "co31", "co32"], ["al3"])
-        if t == 0:
-            unit(3)
         tt(sm(1), T.al3[:, 2::3], sm(0), A.min, ["al3", "sm0"], ["sm1"])
         if t == 0:
             quant(T.vq[:], T.vs[:], T.vt[:], ["vt"], ["vq"])
@@ -540,20 +533,20 @@ def rank_program(g, core, T, topo):
         if last:
             ts(T.offe[:], sm(1), -512.0, A.mult, ["sm1"], ["offe"], 192.0, A.add)
 
-        m0 = 128 * t
+        m0 = C + K * t - K
         for b in range(4):
-            mm(4 + b, 128, T.eq4[:, 128 * b:128 * b + 128], T.es4[:, 128 * b:128 * b + 128], T.lq[:, m0:m0 + 128],
-               T.ls[:, m0:m0 + 128], ["e%d" % b, "lz", "lq%d" % t, "ls%d" % t])
+            mm(4 + b, 128, T.eq4[:, 128 * b:128 * b + 128], T.es4[:, 128 * b:128 * b + 128], T.xq[:, m0:m0 + 128],
+               T.xs[:, m0:m0 + 128], ["e%d" % b, "lq%d" % t, "ls%d" % t] + (["lq0", "ls0"] if t else ["xq1"]))
         for b in range(4):
-            move(AQ[t][b], x[:, 4 * C + b:4 * (C + K):4], T["p%d" % (4 + b)][:, c0:c0 + K], ["#%d" % (4 + b)],
+            move(cf["aq"][b], x[:, 4 * C + b:4 * (C + K):4], T["p%d" % (4 + b)][:, K:2 * K], ["#%d" % (4 + b)],
                  ["ar%d_%d" % (t, b)], "+ar%d" % t)
 
-        run = (0, 16 * CUTS[t] - 2), (16 * CUTS[t] - 2, C)
-        slots = ((0, CUTS[t]), (CUTS[t], NPIV))
+        run = (0, FIRST), (FIRST, C)
+        slots = ((0, CUT), (CUT, NPIV))
 
-        def gather(h, j, q):
+        def gather(h, j):
             a, z = slots[h]
-            move(q, T.tb[:, 64 * a + j:64 * z:4], x[:].indirect(T.offt[:, NPIV * j + a:NPIV * j + z]),
+            move("vvssvsss"[4 * h + j], T.tb[:, 64 * a + j:64 * z:4], x[:].indirect(T.offt[:, NPIV * j + a:NPIV * j + z]),
                  xk + ["ar%d_%d" % (t, b) for b in range(4)] + ["offt%d" % j], ["tb%d_%d" % (h, j)], "+t%d_%d" % (t, h))
 
         def products(h):
@@ -573,16 +566,16 @@ def rank_program(g, core, T, topo):
             quant(T.t2q[:, a:z], T.t2s[:, a:z], T.tb[:, 4 * a + 4:4 * z + 4], rd + more, ["t2q%d" % h])
 
         tb0, tb1 = ["tb0_%d" % j for j in range(4)], ["tb1_%d" % j for j in range(4)]
-        for j, q in ((2, "s"), (0, "v"), (3, "s"), (1, "v")):
-            gather(0, j, q)
+        for j in (2, 0, 3, 1):
+            gather(0, j)
         for j in (2, 3, 1):
-            gather(1, j, "s")
+            gather(1, j)
         act(T.tb[:, 4 * C:4 * C + 4], T.tb[:, 0:4], F.Copy, tb0, ["tbw"])
         if last:
             act(T.olw[:, C:C + K], T.olw[:, 0:C].indirect(T.larr[:]), F.Identity, ["olw0", "larr"], ["olw1"], bias=float(C))
         taps(0, tb0, [])
         products(0)
-        gather(1, 0, "v")
+        gather(1, 0)
         taps(1, tb0 + tb1, ["tbw"])
         products(1)
         for h in range(2):
@@ -594,11 +587,7 @@ def rank_program(g, core, T, topo):
                     act(o, i, F.Copy, ["#%d" % (4 * h + b)], [nk[b]], "+xs%d_%d" % (t, h), scale=0.015625)
                 else:
                     ts(o, i, 0.015625, A.mult, ["#%d" % (4 * h + b)], [nk[b]], kind="+xv%d_%d" % (t, h))
-            if h == 1 and not last:
-                early(1)
             quant(T.xq[:, a:z], T.xs[:, a:z], X[t + 1][:, 4 * a:4 * z], nk, ["xq%d" % h])
-            if h == 0 and not last:
-                early(0)
             if last:
                 if h == 0:
                     act(T.olr[:], T.olw[:].indirect(T.offe[:]), F.Copy, ["olw0", "olw1", "offe"], ["olr"])
@@ -608,12 +597,26 @@ def rank_program(g, core, T, topo):
                     dma("s", T.y[:, 0:a], T.yo[:, 0:a], ["yo0"], ["o2_0"])
                 mm(h, z - a, T.vq[:], T.vs[:], T.xq[:, a:z], T.xs[:, a:z], ["vq", "xq%d" % h])
                 dma("y", T.oc[:, 4 * a:4 * z], T.xq[:, a:z].bitcast(dt.uint8), ["xq%d" % h], ["oc%d" % h])
+        if not last:
+            early(t + 1)
 
-    a = run[1][0]
-    copy(T.yo[:, a:C], T.p1[:, 0:C - a], ["#1"], ["yo1"])
+    copy(T.yo[:, FIRST:C], T.p1[:, 0:C - FIRST], ["#1"], ["yo1"])
     for k in range(4):
-        dma("y" if k < 2 else "s", T.osc[4 * k:4 * k + 4, :], T.xs[32 * k:32 * k + 4, :], both, ["o1_%d" % k])
-    dma("y", T.y[:, a:C], T.yo[:, a:C], ["yo1"], ["o2_1"])
+        dma("y" if k < 2 else "s", T.osc[4 * k:4 * k + 4, :], T.xs[32 * k:32 * k + 4, 0:C], both, ["o1_%d" % k])
+    dma("y", T.y[:, FIRST:C], T.yo[:, FIRST:C], ["yo1"], ["o2_1"])
     op("y", None, ["oc0", "oc1", "o2_0", "o2_1", "o3"] + ["o1_%d" % k for k in range(4)], [])
-    emit(g, T, ops)
-    g.wait_ge(T.sem.sent, sent[0])
+    return ops, sent[0]
+
+
+def rank_program(g, core, T, topo):
+    rank = T.rank_of(core)
+    if rank is None:
+        hand_on(g, core, T, topo)
+        return
+    kind = 0 if route(T, topo, rank)[1] is None else 1
+    ops, sent = plan(core, T, topo, CFG[kind])
+    code = ORDER[kind]
+    order = [62 * DIGITS.index(code[i]) + DIGITS.index(code[i + 1]) for i in range(0, len(code), 2)]
+    assert sorted(order) == list(range(len(ops)))
+    emit(g, T, [ops[i] for i in order])
+    g.wait_ge(T.sem.sent, sent)

from concourse.mybir import dt, AluOpType as A, ActivationFunctionType as F

C, K, R = 320, 64, 2
Q4, U8, BF, FP, I32, U16, HF = "float8_e4m3fn_x4", "uint8", "bfloat16", "float32", "int32", "uint16", "float16"
NPIV = C // 16
NG = NPIV // 2
H = C // 2
EARLY = 128
CUT = 10
FIRST = 16 * CUT - 2
SW = C + 2
CW = 8 * (H + 1) + 8
RW = 336
EW = 3 * C + 16
TINY = 2.0 ** -40
LW = C - K + 16

CFG = [
    [dict(bq="svsv", aq="ssvv", split=0), dict(bq="ssss", aq="ssss", split=6)],
    [dict(bq="svsv", aq="ssvv", split=0), dict(bq="svsv", aq="ssvv", split=0)],
]
DIGITS = "0123456789abcdefghijklmnopqrstuvwxyzABCDEFGHIJKLMNOPQRSTUVWXYZ"
ORDER = [
    "000102030405060C0d0e0g070F0E0f0i0G0D0h0O0I0H0J0Y0l0N0m120L0k0Z1110140T0n0P08130V0Q1J151b0W091i161f0a1g1k0o0b1a1d1h191x0c171B1s0j1A1l"
    "1z1q1y0q1r0r1w0s1e0p181j1m1v1n1D0t1o1c1t1C1u1E0u0v1p1G0w0x0X0y1F0K0z1I1H0A0M1O1L1P1Q1M0B1R1S1N1T1U1W1V1Y1X201Z220R210S2423262527282a"
    "292c2b2d2g2h2e1K2f2j2k2m2A2l2n2o2B2i2s2p2q2r2C2t2w2v2u0U2D2x2E2N2y2F2z2G2H2I2J2K2L2M2R2Q2P2O2V2S2T2Z2U2W2X2Y3233313035383739343i3c36"
    "3a3f3g3h3j3v3d3k3b3w3e3t3n3l3u3r3o3x3q3s3y3m3A3p3B3D3F3z3K3E3C3H3N3L3I3R3M3J3P3O3G3T3Q453S3W4443473V4841464a3X40494c3U3Y4b3Z4d424f4e"
    "4h4g4l4m4i4n4o4j4p4q4k4r4s4t4v4x4u4w4z4y4B4A4D4C4E4F4H4G4J4I4K4O4N4L4M4R4Q4T5b4S4U4V5a594Z4W4P5c534Y4X57505d51525e545f55565I585s5v5g"
    "5u5w5h5t5z5j5y5i5x5k5l5m5n5q5o5p5A5D5C5B5G5J5H5F5K5r5T5N5E5R5Q5S5U5M665V5L69675O5P5Y645W65615X68605Z6c626e636d6a6b6f6g6i6h6j6k6l6p6n"
    "6m6q6r6o6s",
    "000102030405060C0d0e0g070E0F0f0D0i0V0h0G0I0O0J0P0Q0Y0S0l0H0m0K120k0Z1110140n0813151b0W09161g1c0a181d1i0o1e0b171h1v1a0c1k1l1f0j1w1o1C"
    "1u1D1m0q1z1q0r0s1y1r0p1A191p1x0t1j1t1B1E1s0u0v1n1G0w0U0T0x0X1J1F0y1I0z1H0L0A1O1L1P1Q1M1S0B1N1U1R1W1Y1T0R1X22201V1K26241Z28212a2c2325"
    "2e2g2h0M272j2l2m2b2k2n2o2A2p2s2r2q292t2w2v2u2d2x2f2B2y2z2C2i2D0N2E2F2G2H2V2J2T2I2S2K2U2L2W2Z2X2M2Y2O2P2R2Q30313233342N383736393i3c35"
    "3b3f3e3j3g3v3k3a3u3d3h3m3t3l3w3n3q3x3p3o3A3r3z3s3y3D3K3B3F3E3C3J3O3L3G3R3N3I3P3M3H3T3Q44463X4c3U45404b3V4a3Z3S3W483Y474249434d414f4e"
    "4h4g4l4i4m4n4j4p4k4r4o4t4v4q4u4x4z4s4B4D4w4F4H4J4y4A4L4O4N4E4C4S4Q4T4G4R4U4V4K594Y4Z4X4W4I525351504M5a545b57554P565c585d5e5f5g5i5h5j"
    "5k5t5s5u5x5r5l5w5y5o5n5v5p5m5B5A5C5z5F5I5E5J5S5Q5H5K5D5q5M5N5G685P5T5L5U5O5R636164655V665X5Y675W5Z6c6b60626d696a6e6f6h6g6i6j6k6p6m6l"
    "6o6q6n6r",
]


def sb(n, t):
    return ("sbuf", [128, n], t)


SCRATCH = {
    "ut": sb(512, BF), "vt": sb(512, BF), "uq": sb(128, Q4), "us": sb(128, U8), "u2q": sb(256, Q4), "u2s": sb(256, U8),
    "vq": sb(128, Q4), "vs": sb(128, U8),
    "wq": sb(512, Q4), "wp": sb(512, U8), "zq": sb(512, Q4), "zp": sb(512, U8),
    "x0": sb(4 * (C + K), BF), "x1": sb(4 * (C + K), BF), "x2": sb(4 * C, BF),
    "xq": sb(C + R * K, Q4), "xs": sb(C + R * K, U8),
    "tt": sb(C, FP), "msk": sb(NPIV * SW, BF), "cum": sb(2 * CW, HF), "cnt": sb(NPIV, BF), "gsum": sb(NPIV, FP),
    "zr": sb(RW, BF), "zz": sb(C, BF), "yb": sb(C, BF), "yr": sb(C, BF),
    "zf": sb(2 * C, HF), "ybf": sb(2 * C, HF), "yrf": sb(2 * C, HF), "mxf": sb(2 * H, HF), "mx": sb(2 * H, BF),
    "sg": sb(2 * C, BF), "sn": sb(8, FP), "se": sb(8, BF), "cut": sb(2 * NPIV, BF),
    "wr": sb(2 * RW, BF), "eq": sb(2 * RW, BF), "vr": sb(2 * RW, BF), "rows": sb(3 * RW, BF),
    "lm": sb(4 * C, BF), "lc": sb(4 * H, FP),
    "sel": sb(C, BF), "sel5": sb(5 * C + 64, BF), "sel3": sb(3 * C + 32, BF), "co5": sb(5 * NPIV, FP), "co3": sb(3 * NPIV, FP),
    "al5": sb(5 * NPIV, FP), "al3": sb(3 * NPIV, FP), "sm": sb(2 * NPIV, FP), "er": sb(2 * EW, BF),
    "offb": sb(16, U16), "offt": sb(4 * NPIV, U16), "offd": sb(NPIV, U16), "offe": sb(NPIV, U16), "offu": sb(16, U16),
    "offl": sb(4, U16), "larr": sb(4, U16), "rl": sb(4, U16), "offw": sb(2, U16),
    "bt": sb(768, BF), "bq0": sb(128, Q4), "bs0": sb(128, U8), "bq1": sb(128, Q4), "bs1": sb(128, U8),
    "rq0": sb(K, Q4), "rs0": sb(K, U8), "rq1": sb(K, Q4), "rs1": sb(K, U8),
    "tb": sb(4 * C + 8, BF), "tq": sb(C, Q4), "ts": sb(C, U8), "t2q": sb(C, Q4), "t2s": sb(C, U8),
    "ew": sb(2 * C, BF), "eq4": sb(512, Q4), "es4": sb(512, U8), "j16": sb(16, BF), "oh": sb(16, BF),
    "iu": sb(16, I32), "qi": sb(2, I32), "qf": sb(1, FP), "kk": sb(NPIV, FP), "kq": sb(NPIV, FP), "rc": sb(NPIV, FP),
    "thr": sb(4, BF), "thrh": sb(4, FP), "thr2": sb(4, BF), "thrh2": sb(4, FP),
    "jm": sb(C, BF), "csel": sb(C, BF), "chold": sb(C, BF), "cval": sb(C, BF),
    "olw": sb(C + K, FP), "olr": sb(C, FP), "yo": sb(C, FP),
}
for _b in range(8):
    SCRATCH["p%d" % _b] = ("psum", [128, 512], FP)

POOLS = {"v": 46, "s": 28, "t": 20, "g": 30, "d": 20}
SEMAPHORES = ["aq0", "aq1", "as0", "as1", "al", "sent"] + ["%s%d" % (k, i) for k in POOLS for i in range(POOLS[k])]


def bits(engines):
    m = 0
    for e in engines:
        m |= 1 << e
    return m


def route(T, topo, r):
    src, dst = T.cores[r], T.cores[(r + 1) % len(T.cores)]
    if topo.may_write(src, dst):
        return dst, None, None
    able = [c for c in topo.cores_of(src) if T.rank_of(c) is None and topo.may_write(c, dst)]
    near = [c for c in able if topo.die(c) == topo.die(src)]
    far = [c for c in able if topo.die(c) != topo.die(src)]
    first = (near or able)[0]
    rest = [c for c in far + near if c != first]
    return dst, first, (rest or able)[0]


def halves(topo, src, dst):
    e = topo.engines(src, dst)
    return e[0::2], e[1::2]


def land(T, t):
    a = C + K * t
    return T.xq[:, a:a + K].bitcast(dt.uint8), T.xs[:, a:a + K]


def hand_on(g, core, T, topo):
    sent = 0
    for r in range(len(T.cores)):
        dst, cq, cs = route(T, topo, r)
        if core not in (cq, cs):
            continue
        ea, eb = halves(topo, T.cores[r], core)
        out = topo.engines(core, dst)
        rid, pid = topo.addr(dst, core)
        jobs = []
        for t in range(R):
            lq, ls = land(T, t)
            if core == cq:
                jobs.append(("aq%d" % t, len(ea), lq, T["rq%d" % t][:].bitcast(dt.uint8)))
            if core == cs:
                jobs.append(("as%d" % t, len(eb), ls, T["rs%d" % t][:]))
        if core == cs:
            jobs.append(("al", len(eb), T.larr[:], T.rl[:]))
        for sem, n, o, i in jobs:
            g.wait_ge(T.sem[sem], n)
            g.remote_dma(o, i, T.sem[sem], T.sem.sent, pid, rid, bits(out))
            sent += len(out)
    if sent:
        g.wait_ge(T.sem.sent, sent)


def emit(g, T, ops):
    queue = {"v": g.vector, "s": g.scalar, "t": g.tensor, "g": g, "y": g.sync}
    sets = {}
    for i, o in enumerate(ops):
        if o[4][:1] == "+":
            sets.setdefault(o[4], []).append(i)
    writer, readers, known = {}, {}, {q: set() for q in queue}
    waits, before, needed = [], [], set()
    for i, (q, fn, rd, wr, kind) in enumerate(ops):
        deps = set()
        if q != "x":
            for k in rd:
                if k in writer:
                    deps.add(writer[k])
                if k[0] == "#":
                    deps.update(j for j in readers.get(k, ()) if ops[j][0] != q)
            for k in wr:
                if k in writer and not (kind == "acc" and k[0] == "#"):
                    deps.add(writer[k])
                deps.update(readers.get(k, ()))
        mine = []
        for d in sorted(deps, reverse=True):
            if d not in known[q]:
                members = sets.get(ops[d][4], [d])
                assert members[-1] < i, "a wait inside a set"
                mine.append(members[-1])
                for j in members:
                    known[q].add(j)
                    known[q].update(before[j])
        waits.append(mine)
        needed.update(mine)
        before.append(frozenset(known[q]) if q != "x" else frozenset())
        for k in rd:
            readers.setdefault(k, []).append(i)
        for k in wr:
            writer[k] = i
            readers[k] = []
    last = {p: [] for p in POOLS}
    mark = {}
    for i, (q, fn, rd, wr, kind) in enumerate(ops):
        if q == "x":
            mark[i] = fn
            continue
        for d in waits[i]:
            queue[q].wait_ge(T.sem[mark[d][0]], mark[d][1])
        if fn is None:
            continue
        ins = fn(queue[q])
        members = sets.get(kind, [i])
        end = members[-1]
        if end not in needed:
            continue
        p = "d" if kind == "dma" else q
        step = 16 if kind == "dma" else 1
        if i == members[0]:
            free = [n for n, (j, c) in enumerate(last[p]) if j in before[i]]
            if free:
                n = free[0]
            else:
                n = len(last[p])
                assert n < POOLS[p], "out of semaphores: " + p
                last[p].append((i, 0))
            last[p][n] = (end, last[p][n][1] + step * len(members))
            mark[end] = ("%s%d" % (p, n), last[p][n][1])
        ins.then_inc(T.sem[mark[end][0]], step)


def plan(core, T, topo, cfg):
    rank = T.rank_of(core)
    n_ranks = len(T.cores)
    ops = []

    def op(q, fn, rd, wr, kind=""):
        ops.append((q, fn, list(rd), list(wr), kind))

    def dma(q, out, in_, rd, wr):
        op(q, lambda e: e.dma_start(out, in_), rd, wr, "dma")

    def ts(out, in0, s1, o0, rd, wr, s2=None, o1=None, kind=""):
        if o1 is None:
            op("v", lambda e: e.tensor_scalar(out, in0, s1, None, o0), rd, wr, kind)
        else:
            op("v", lambda e: e.tensor_scalar(out, in0, s1, s2, o0, o1), rd, wr, kind)

    def tt(out, a, b, o, rd, wr, kind=""):
        op("v", lambda e: e.tensor_tensor(out, a, b, o), rd, wr, kind)

    def scan(out, a, b, init, o0, o1, rd, wr, kind=""):
        op("v", lambda e: e.tensor_tensor_scan(out, a, b, init, o0, o1), rd, wr, kind)

    def copy(out, in_, rd, wr, kind=""):
        op("v", lambda e: e.tensor_copy(out, in_), rd, wr, kind)

    def act(out, in_, f, rd, wr, kind="", **kw):
        op("s", lambda e: e.activation(out, in_, f, **kw), rd, wr, kind)

    def move(q, out, in_, rd, wr, kind):
        if q == "s":
            act(out, in_, F.Copy, rd, wr, kind + q)
        else:
            copy(out, in_, rd, wr, kind + q)

    def quant(q, s, in_, rd, wr, kind=""):
        op("v", lambda e: e.quantize_mx(q, s, in_), rd, wr, kind)

    def mm(bank, n, lq, ls, rq, rs, rd, start=True, stop=True):
        op("t", lambda e: e.matmul_mx(T["p%d" % bank][:, 0:n], lq, ls, rq, rs, start, stop), rd, ["#%d" % bank],
           "" if start else "acc")

    def turn(out, in_, rd, wr):
        op("v", lambda e: e.transpose(out, in_), rd, wr)

    def iota(out, pattern, base, cm, wr, small=True):
        if small:
            op("g", lambda e: e.iota(out, pattern, base, cm, allow_small_or_imprecise_dtypes=True), [], wr)
        else:
            op("g", lambda e: e.iota(out, pattern, base, cm), [], wr)

    dst, cq, cs = route(T, topo, rank)
    prev = (rank - 1) % n_ranks
    _, pq, ps = route(T, topo, prev)
    if pq is None:
        ea, eb = halves(topo, T.cores[prev], core)
        nq, ns = len(ea), len(eb)
    else:
        nq, ns = len(topo.engines(pq, core)), len(topo.engines(ps, core))
    sent = [0]

    def send(out, in_, sem, to, half, rd):
        eng = halves(topo, core, to)[half]
        rid, pid = topo.addr(to, core)
        sent[0] += len(eng)
        op("g", lambda e: e.remote_dma(out, in_, T.sem[sem], T.sem.sent, pid, rid, bits(eng)), rd, [])

    for t in range(R):
        op("x", ("aq%d" % t, nq), [], ["lq%d" % t])
        op("x", ("as%d" % t, ns), [], ["ls%d" % t])
    op("x", ("al", ns), [], ["larr"])

    X = [T.x0, T.x1, T.x2]
    Lr, Nr, Ar = 0, RW, 2 * RW

    def xkeys(t, h):
        return ["x0_%d" % h] if t == 0 else ["x%d_%d_%d" % (t, h, b) for b in range(4)]

    def useg(i):
        return T.u2q[:, 128 * i:128 * i + 128], T.u2s[:, 128 * i:128 * i + 128]

    def tk(k):
        return "tta" if 16 * k < EARLY else "ttb"

    def mrow(k, a, z):
        s = SW * (k // 2 + NG * (k % 2))
        return T.msk[:, s + a:s + z]

    def sign(t, k, bank, a, z, wr):
        i = k // 2 + (NG if z < C else 0)
        act(mrow(k, a, z), T["p%d" % bank][:, a:z], F.Sign, ["#%d" % bank, tk(k), "gz"], wr, "+sg%d_%d" % (t, z == C),
            bias=T.tt[:, 16 * k:16 * k + 1], scale=-1.0, accum_out=T.gsum[:, i:i + 1])

    def above(t, k, bank, a, z, wr):
        ts(mrow(k, a, z), T["p%d" % bank][:, a:z], T.tt[:, 16 * k:16 * k + 1], A.is_gt, ["#%d" % bank, tk(k)], wr, -2.0, A.mult,
           "+cm%d_%d" % (t, k // NG) if z == C else "+ce%d" % t)

    def early(t):
        mm(0, EARLY, T.uq[:], T.us[:], T.xq[:, 0:EARLY], T.xs[:, 0:EARLY], ["uq", "xq0"])
        turn(T.tt[:, 0:EARLY], T.p0[:, 0:EARLY], ["#0"], ["tta"])
        for bank, i, call in ((1, 0, sign), (2, 1, above)):
            q, s = useg(i)
            mm(bank, FIRST, q, s, T.xq[:, 0:FIRST], T.xs[:, 0:FIRST], ["u2q", "u2s", "xq0"])
            for k in range(i, EARLY // 16, 2):
                call(t, k, bank, 0, FIRST, ["n%d" % k])

    def rest(t, k, call, bank):
        if 16 * k < EARLY:
            call(t, k, bank, FIRST, C, ["m%d" % k])
        else:
            call(t, k, bank, 0, C, ["m%d" % k, "n%d" % k])

    x0 = 4 * FIRST
    dma("y", T.ut[:], T.u[:], [], ["ut"])
    dma("s", T.x0[:, 0:x0], T.x[:, 0:x0], [], ["x0_0"])
    dma("y", T.x0[:, x0:4 * C], T.x[:, x0:4 * C], [], ["x0_1"])
    dma("y", T.wq[:].bitcast(dt.uint8), T.wc[:], ["x0_0", "x0_1"], ["wq"])
    dma("y", T.zq[:].bitcast(dt.uint8), T.zc[:], ["x0_1"], ["zq"])
    dma("y", T.wp[:], T.ws[:], ["x0_1"], ["wp"])
    dma("y", T.zp[:], T.zs[:], ["x0_1"], ["zp"])
    dma("y", T.vt[:], T.v[:], ["x0_1"], ["vt"])

    iota(T.qi[:, 0:1], [[0, 1]], 0, 1, ["qi0"], False)
    iota(T.j16[:], [[1, 16]], 0, 0, ["j16"])
    iota(T.iu[:], [[16, 2], [32, 4], [0, 2]], 0, 0, ["iu"], False)
    iota(T.kk[:], [[16, NPIV]], 0, 0, ["kk"])
    iota(T.jm[:], [[0, NPIV], [1, 16]], 0, 0, ["jm"])
    iota(T.gsum[:, NG:NPIV], [[0, NG]], 0, 0, ["gz"])
    iota(T.zr[:], [[0, RW]], 0, 0, ["zr"])
    iota(T.zz[:], [[0, C]], 0, 0, ["zz2"])
    iota(T.msk[:, C::SW], [[0, NPIV]], C, 0, ["pad0"])
    iota(T.msk[:, C + 1::SW], [[0, NPIV]], 0, 0, ["pad1"])
    iota(T.er[:, 16:16 + C], [[0, C]], 1, 0, ["er0"])
    op("g", lambda e: e.affine_select(T.chold[:], T.er[:, 16:16 + C], [[0, NPIV], [1, 16]], A.is_gt, 0.0, 0, 0), ["er0"], ["chold"])
    iota(T.bt[:, 256:512], [[0, 256]], 0, 0, ["btz"])
    iota(T.eq[:, C::RW], [[2 * K - C, 2]], -K, 0, ["eqp"])
    iota(T.vr[:, 0::RW], [[0, 2]], -1024, 0, ["vrp"])
    iota(T.wr[:, 0::RW], [[0, 2]], 0, 0, ["wrp"])
    iota(T.cval[:], [[1, C]], -192, 0, ["cval"])
    iota(T.co5[:, 0::5], [[0, NPIV]], 0, 0, ["co50"])
    iota(T.co5[:, 4::5], [[0, NPIV]], 0, 0, ["co54"])
    iota(T.sel5[:, 139::80], [[0, NPIV]], 0, 0, ["s54"])
    iota(T.rows[:, Ar:Ar + 1], [[0, 1]], 1, 0, ["erz"])
    iota(T.co3[:, 0::3], [[0, NPIV]], 0, 0, ["co30"])
    iota(T.co3[:, 2::3], [[0, NPIV]], 1, 0, ["co32"])
    iota(T.er[:, EW + 16:EW + 16 + C], [[0, C]], 1, 0, ["er1"])
    iota(T.olw[:, 0:C], [[1, C]], 0, 0, ["olw0"])
    op("v", lambda e: e.memset(T.ew[:], 0.0), [], ["ew"])
    copy(T.zf[:], T.ew[:], ["ew"], ["zz0", "zz1"])
    ts(T.qi[:, 1:2], T.qi[:, 0:1], 15, A.bitwise_and, ["qi0"], ["qi1"])
    ts(T.offw[:, 0:1], T.qi[:, 0:1], 4.0, A.mult, ["qi0"], ["offw"], 3.0, A.add)
    copy(T.qf[:], T.qi[:, 1:2], ["qi1"], ["qf"])
    copy(T.offu[:], T.iu[:], ["iu"], ["offu"])
    ts(T.oh[:], T.j16[:], T.qf[:], A.is_equal, ["j16", "qf"], ["oh"])
    copy(T.ew[:].indirect(T.offw[:, 0:1]), T.oh[:], ["oh", "offw"], ["ew"])
    for b in range(4):
        quant(T.eq4[:, 128 * b:128 * b + 128], T.es4[:, 128 * b:128 * b + 128], T.ew[:, 3 - b:515 - b], ["ew"], ["e%d" % b])
    act(T.kq[:], T.kk[:], F.Identity, ["kk", "qf"], ["kq"], bias=T.qf[:])
    act(T.co5[:, 2::5], T.kq[:], F.Identity, ["kq"], ["co52"], bias=float(-C), scale=-1.0)
    act(T.thr[:], T.kq[:, 0:4], F.Copy, ["kq"], ["thr"])
    act(T.thrh[:], T.kq[:, 0:4], F.Identity, ["kq"], ["thrh"], bias=0.5)
    act(T.sel5[:, 123::80], T.kq[:], F.Identity, ["kq"], ["s53"], bias=float(-H))
    act(T.co5[:, 3::5], T.kk[:], F.Identity, ["kk"], ["co53"], bias=-0.5, scale=0.0)
    act(T.co3[:, 1::3], T.kk[:], F.Identity, ["kk"], ["co31"], bias=-(1.0 + 1.0 / 512), scale=0.0)
    act(T.sel3[:, 77::48], T.kk[:], F.Identity, ["kk"], ["s32"], bias=386.0 / 512, scale=0.0)
    op("v", lambda e: e.reciprocal(T.rc[:], T.co5[:, 2::5]), ["co52"], ["rc"])
    act(T.co5[:, 1::5], T.rc[:], F.Identity, ["rc"], ["co51"], bias=-1.0)
    quant(T.uq[:], T.us[:], T.ut[:], ["ut"], ["uq"])
    quant(T.xq[:, 0:FIRST], T.xs[:, 0:FIRST], T.x0[:, 0:x0], ["x0_0"], ["xq0"])
    copy(T.u2q[:].bitcast(dt.uint32), T.uq[:].bitcast(dt.uint32).indirect(T.offu[:]), ["uq", "offu"], ["u2q"])
    act(T.u2s[:], T.us[:].indirect(T.offu[:]), F.Copy, ["uq", "offu"], ["u2s"])
    act(T.csel[:], T.jm[:], F.Abs, ["jm", "qf"], ["csel"], bias=T.qf[:], scale=-1.0)
    quant(T.xq[:, FIRST:C], T.xs[:, FIRST:C], T.x0[:, x0:4 * C], ["x0_1"], ["xq1"])
    early(0)

    ends = T.cnt[:]
    cnts = ["cnt0", "cnt1", "cnt11"]

    def cut(s, at, start, row):
        def k(name):
            return "%s%d" % (name, s)

        def w(buf, n=C):
            return buf[:, n * s:n * s + n]

        def key(i):
            return T.se[:, 4 * s + i:4 * s + i + 1]

        c, top, bot, a = w(T.cut, NPIV), T.mxf[:, H * s + H - 1:H * s + H], T.mx[:, H * s + H - 1:H * s + H], RW * s
        y0, y1, n = T.yrf[:, C * s:C * s + H], T.yrf[:, C * s + H:C * s + C], T.sn[:, 4 * s:4 * s + 1]
        return {
            "c": lambda: ts(c, ends, float(at), A.is_le, cnts, [k("cut")], 1024.0, A.mult),
            "z": lambda: tt(T.zf[:, C * s:C * s + C:16], ends, c, A.add, cnts + [k("cut")], [k("zz")]),
            "spread": lambda: scan(w(T.ybf), T.chold[:], w(T.zf), 0.0, A.mult, A.add, ["chold", k("zz")], [k("yb")]),
            "turn": lambda: turn(w(T.yrf), w(T.ybf), [k("yb")], [k("yr")]),
            "n": lambda: act(w(T.sg), T.yr[:], F.Sign, ["yr2"], [k("sn")], bias=-at - 0.5, accum_out=n),
            "top": lambda: scan(w(T.mxf, H), y0, y1, -2048.0, A.max, A.max, [k("yr")], [k("mx")]),
            "bot": lambda: scan(w(T.mx, H), y0, y1, 2048.0, A.min, A.min, [k("yr")], [k("mn")]),
            "d": lambda: ts(key(0), top, 1024.0, A.subtract, [k("mx")], [k("dd")]),
            "a": lambda: ts(key(1), n, float(-at), A.is_ge, [k("sn"), k("mn")], [k("aa")], bot, A.mult),
            "e": lambda: ts(key(2), n, float(-at), A.is_lt, [k("sn"), k("dd")], [k("ee")], key(0), A.mult),
            "with": lambda: ts(T.eq[:, a:a + C], T.yr[:], key(1), A.subtract, ["yr2", k("aa"), k("ee")], [k("eq")],
                               key(2), A.is_le),
            "past": lambda: ts(T.wr[:, a + 1:a + 1 + C], T.yr[:], key(1), A.subtract, ["yr2", k("aa"), k("ee")], [k("wr")],
                               key(2), A.is_lt),
            "v": lambda: scan(T.vr[:, a + 1:a + 2 + C], T.eq[:, a:a + C + 1], T.zr[:, 0:C + 1], float(start), A.add, A.add,
                              [k("eq"), "eqp", "zr"], [k("vr")]),
            "run": lambda: scan(T.rows[:, row:row + 1 + C], T.wr[:, a:a + 1 + C], T.vr[:, a:a + 1 + C],
                                T.vr[:, a + 1 + C:a + 2 + C], A.add, A.max, [k("wr"), k("vr"), "wrp", "vrp"], ["row%d" % row]),
        }

    lo, hi = cut(0, -192, -192, Lr), cut(1, 192, -128, Nr)
    il, ih = T.vr[:, C + 1:C + 2], T.vr[:, RW + C + 1:RW + C + 2]

    def select(out, row, rd, wr):
        scan(out, T.csel[:], row, 0.0, A.add, A.min, ["csel"] + rd, wr)

    def turns(buf, n, r):
        return buf[:, 16 * r:16 * r + n * (C - 1) + 1:n]

    def sm(i):
        return T.sm[:, NPIV * i:NPIV * i + NPIV]

    for t in range(R):
        x, xk, cf = X[t], xkeys(t, 0) + xkeys(t, 1), cfg[t]
        last = t == R - 1
        both = ["xq0", "xq1"]
        for bank, i in ((4, 1), (5, 0), (6, None)):
            if i is None:
                mm(bank, C - EARLY, T.uq[:], T.us[:], T.xq[:, EARLY:C], T.xs[:, EARLY:C], ["uq"] + both)
            else:
                a, b = useg(i)
                mm(bank, C, a, b, T.xq[:, 0:C], T.xs[:, 0:C], ["u2q", "u2s"] + both)

        rest(t, 1, above, 4)
        turn(T.tt[:, EARLY:C], T.p6[:, 0:C - EARLY], ["#6"], ["ttb"])
        for k in range(0, NPIV, 2):
            rest(t, k, sign, 5)
        for k in range(3, NPIV, 2):
            rest(t, k, above, 4)
        for i in range(2):
            ks, s0, n = range(1 + NG * i, NG + NG * i, 2), NG + NG // 2 * i, NG // 2 * (H + 1)
            scan(T.cum[:, CW * i:CW * i + n + 1], T.msk[:, SW * s0 - 2:SW * s0 + 2 * n:2], T.msk[:, SW * s0 - 1:SW * s0 + 2 * n:2],
                 0.0, A.add, A.add, ["pad0", "pad1"] + ["m%d" % k for k in ks] + ["n%d" % k for k in ks], ["cum%d" % i])
            tt(T.cnt[:, ks[0]:NG + NG * i:2], T.cum[:, CW * i + H + 1:CW * i + n + 1:H + 1], T.cum[:, CW * i:CW * i + n:H + 1],
               A.subtract, ["cum%d" % i], ["cnt%d" % ks[0]])
        tt(T.cnt[:, 0:NPIV:2], T.gsum[:, 0:NG], T.gsum[:, NG:NPIV], A.add,
           ["gz"] + [p + str(k) for k in range(0, NPIV, 2) for p in "mn"], ["cnt0"])

        if t == 0:
            act(T.csel[:], T.csel[:], F.Relu, ["csel"], ["csel"], bias=1024.0, scale=-1024.0)
            act(T.cval[:], T.cval[:], F.Copy, ["cval"], ["cval"], scale=TINY)
        lcs = ["lc%d" % k for k in range(4)]
        lends = T.lc[:, H - 1::H]
        b0, c0, e0 = 512 * t, K * t, EW * t + 16
        er = T.er[:, e0:e0 + C]
        bq, bs = T["bq%d" % t], T["bs%d" % t]

        def count_s(k):
            m = min(16 * k, C - LW - 16 * k)
            act(T.lm[:, C * k + m:C * k + C - m], T.rows[:, Lr + 1 + m:Lr + 1 + C - m], F.Sign, ["row0", "thrh2"],
                ["lc%d" % k, "lm%d" % k], "+ld%d" % t, bias=T.thrh2[:, k:k + 1], scale=-1.0,
                accum_out=T.lc[:, H * k + H - 1:H * k + H])

        def mask_v(k):
            ts(T.lm[:, C * k:C * k + LW], T.rows[:, Lr + 1 + 16 * k:Lr + 1 + 16 * k + LW], T.thr2[:, k:k + 1], A.is_le,
               ["row0", "thr2"], ["lm%d" % k], 2.0, A.mult)

        def count_v(k):
            scan(T.lc[:, H * k + H - LW // 2:H * k + H], T.lm[:, C * k:C * k + LW // 2], T.lm[:, C * k + LW // 2:C * k + LW],
                 float(32 * k - C), A.add, A.add, ["lm%d" % k], ["lc%d" % k], "+lc%d" % t)

        def pick(r):
            row, a = ((Lr, 0), (Lr, 1), (Nr, 0))[r]
            select(turns(T.sel5, 5, r), T.rows[:, row + a:row + a + C], ["row%d" % row], ["s5%d" % r])

        def scatter(a, z):
            copy(T.er[:, e0:e0 + EW - 16].indirect(T.offd[:, a:z]), T.cval[:, 16 * a:16 * z], ["cval", "offd"], ["er%d" % t])

        copy(T.zz[:, 0:C:16], ends, cnts, ["zz2"])
        scan(T.yb[:], T.chold[:], T.zz[:], 0.0, A.mult, A.add, ["chold", "zz2"], ["yb2"])
        turn(T.yr[:], T.yb[:], ["yb2"], ["yr2"])
        for step in ("c", "z", "spread", "turn", "n", "top", "bot", "d", "a", "e", "with", "past", "v", "run"):
            lo[step]()
            hi[step]()
        act(T.thrh2[:], T.thrh[:], F.Identity, ["thrh", "vr0"], ["thrh2"], bias=il)
        act(T.thr2[:], T.thr[:], F.Identity, ["thr", "vr0"], ["thr2"], bias=il)
        ts(T.sn[:, 3:4], il, ih, A.add, ["vr0", "vr1"], ["shift"], C + 0.25, A.add)
        mask_v(0)
        count_s(1)
        count_s(2)
        mask_v(3)
        count_v(0)
        count_v(3)
        for j in (0, 2, 1, 3):
            ts(T.offb[:, 4 * j:4 * j + 4], lends, 2.0, A.mult, lcs, ["offb%d" % j], float(640 + j), A.add)
        for j in range(4):
            move(cf["bq"][j], T.bt[:, b0 + j:b0 + 4 * K:4], x[:, 0:4 * C].indirect(T.offb[:, 4 * j:4 * j + 4]),
                 xk + ["offb%d" % j], ["bt%d_%d" % (t, j)], "+b%d" % t)
        quant(bq[:], bs[:], T.bt[:, 256 * t:256 * t + 512], ["btz"] + ["bt%d_%d" % (t, j) for j in range(4)], ["bq%d" % t])
        lq, ls = land(T, t)
        src_q, src_s = bq[:, c0:c0 + K].bitcast(dt.uint8), bs[:, c0:c0 + K]
        if cq is None:
            send(lq, src_q, "aq%d" % t, dst, 0, ["bq%d" % t])
            send(ls, src_s, "as%d" % t, dst, 1, ["bq%d" % t])
        else:
            send(T["rq%d" % t][:].bitcast(dt.uint8), src_q, "aq%d" % t, cq, 0, ["bq%d" % t])
            send(T["rs%d" % t][:], src_s, "as%d" % t, cs, 1, ["bq%d" % t])
        if last:
            ts(T.offl[:], lends, 0.5, A.mult, lcs, ["offl"], 160.0, A.add)
            if cq is None:
                send(T.larr[:], T.offl[:], "al", dst, 1, ["offl"])
            else:
                send(T.rl[:], T.offl[:], "al", cs, 1, ["offl"])
        for r in range(3):
            pick(r)
        scan(T.al5[:], T.co5[:], T.sel5[:, 75::16], 0.0, A.mult, A.add,
             ["s5%d" % i for i in range(5)] + ["co5%d" % i for i in range(5)], ["al5"])
        ts(T.offd[:], T.al5[:, 3::5], 2.0, A.mult, ["al5", "shift"], ["offd"], T.sn[:, 3:4], A.add)
        if cf["split"]:
            scatter(0, cf["split"])
        scatter(cf["split"], NPIV)
        scan(T.rows[:, Ar + 1:Ar + 1 + C], er, er, 1.0, A.add, A.max, ["er%d" % t], ["row672"])
        select(T.sel[:], er, ["er%d" % t], ["sel"])
        select(turns(T.sel3, 3, 0), T.rows[:, Ar + 1:Ar + 1 + C], ["row672"], ["s30"])
        select(turns(T.sel3, 3, 1), T.rows[:, Ar:Ar + C], ["row672", "erz"], ["s31"])
        ts(sm(0), T.sel[:, 15::16], -1.0 / (512 * TINY), A.mult, ["sel"], ["sm0"], -0.25, A.max)
        scan(T.al3[:], T.co3[:], T.sel3[:, 45::16], 0.0, A.mult, A.add,
             ["s30", "s31", "s32", "co30", "co31", "co32"], ["al3"])
        tt(sm(1), T.al3[:, 2::3], sm(0), A.min, ["al3", "sm0"], ["sm1"])
        if t == 0:
            quant(T.vq[:], T.vs[:], T.vt[:], ["vt"], ["vq"])
        for j in (2, 0, 3, 1):
            ts(T.offt[:, NPIV * j:NPIV * j + NPIV], sm(1), -2048.0, A.mult, ["sm1"], ["offt%d" % j], float(768 + j), A.add)
        if last:
            ts(T.offe[:], sm(1), -512.0, A.mult, ["sm1"], ["offe"], 192.0, A.add)

        m0 = C + K * t - K
        for b in range(4):
            mm(4 + b, 128, T.eq4[:, 128 * b:128 * b + 128], T.es4[:, 128 * b:128 * b + 128], T.xq[:, m0:m0 + 128],
               T.xs[:, m0:m0 + 128], ["e%d" % b, "lq%d" % t, "ls%d" % t] + (["lq0", "ls0"] if t else ["xq1"]))
        for b in range(4):
            move(cf["aq"][b], x[:, 4 * C + b:4 * (C + K):4], T["p%d" % (4 + b)][:, K:2 * K], ["#%d" % (4 + b)],
                 ["ar%d_%d" % (t, b)], "+ar%d" % t)

        run = (0, FIRST), (FIRST, C)
        slots = ((0, CUT), (CUT, NPIV))

        def gather(h, j):
            a, z = slots[h]
            move("vvssvsss"[4 * h + j], T.tb[:, 64 * a + j:64 * z:4], x[:].indirect(T.offt[:, NPIV * j + a:NPIV * j + z]),
                 xk + ["ar%d_%d" % (t, b) for b in range(4)] + ["offt%d" % j], ["tb%d_%d" % (h, j)], "+t%d_%d" % (t, h))

        def products(h):
            a, z = run[h]
            for w, b in ((1, 0), (1, 1), (1, 2), (0, 0), (0, 1), (0, 2), (1, 3), (0, 3)):
                cols = slice(128 * b, 128 * b + 128)
                if w:
                    mm(4 * h + b, z - a, T.wq[:, cols], T.wp[:, cols], T.tq[:, a:z], T.ts[:, a:z], ["wq", "wp", "tq%d" % h],
                       True, False)
                else:
                    mm(4 * h + b, z - a, T.zq[:, cols], T.zp[:, cols], T.t2q[:, a:z], T.t2s[:, a:z],
                       ["zq", "zp", "t2q%d" % h], False, True)

        def taps(h, rd, more):
            a, z = run[h]
            quant(T.tq[:, a:z], T.ts[:, a:z], T.tb[:, 4 * a:4 * z], rd, ["tq%d" % h])
            quant(T.t2q[:, a:z], T.t2s[:, a:z], T.tb[:, 4 * a + 4:4 * z + 4], rd + more, ["t2q%d" % h])

        tb0, tb1 = ["tb0_%d" % j for j in range(4)], ["tb1_%d" % j for j in range(4)]
        for j in (2, 0, 3, 1):
            gather(0, j)
        for j in (2, 3, 1):
            gather(1, j)
        act(T.tb[:, 4 * C:4 * C + 4], T.tb[:, 0:4], F.Copy, tb0, ["tbw"])
        if last:
            act(T.olw[:, C:C + K], T.olw[:, 0:C].indirect(T.larr[:]), F.Identity, ["olw0", "larr"], ["olw1"], bias=float(C))
        taps(0, tb0, [])
        products(0)
        gather(1, 0)
        taps(1, tb0 + tb1, ["tbw"])
        products(1)
        for h in range(2):
            a, z = run[h]
            nk = xkeys(t + 1, h)
            for b in range(4):
                o, i = X[t + 1][:, 4 * a + b:4 * z:4], T["p%d" % (4 * h + b)][:, 0:z - a]
                if b % 2 == 0:
                    act(o, i, F.Copy, ["#%d" % (4 * h + b)], [nk[b]], "+xs%d_%d" % (t, h), scale=0.015625)
                else:
                    ts(o, i, 0.015625, A.mult, ["#%d" % (4 * h + b)], [nk[b]], kind="+xv%d_%d" % (t, h))
            quant(T.xq[:, a:z], T.xs[:, a:z], X[t + 1][:, 4 * a:4 * z], nk, ["xq%d" % h])
            if last:
                if h == 0:
                    act(T.olr[:], T.olw[:].indirect(T.offe[:]), F.Copy, ["olw0", "olw1", "offe"], ["olr"])
                    dma("y", T.ol[:], T.olr[0:128:16, :], ["olr"], ["o3"])
                else:
                    act(T.yo[:, 0:a], T.p0[:, 0:a], F.Copy, ["#0"], ["yo0"])
                    dma("s", T.y[:, 0:a], T.yo[:, 0:a], ["yo0"], ["o2_0"])
                mm(h, z - a, T.vq[:], T.vs[:], T.xq[:, a:z], T.xs[:, a:z], ["vq", "xq%d" % h])
                dma("y", T.oc[:, 4 * a:4 * z], T.xq[:, a:z].bitcast(dt.uint8), ["xq%d" % h], ["oc%d" % h])
        if not last:
            early(t + 1)

    copy(T.yo[:, FIRST:C], T.p1[:, 0:C - FIRST], ["#1"], ["yo1"])
    for k in range(4):
        dma("y" if k < 2 else "s", T.osc[4 * k:4 * k + 4, :], T.xs[32 * k:32 * k + 4, 0:C], both, ["o1_%d" % k])
    dma("y", T.y[:, FIRST:C], T.yo[:, FIRST:C], ["yo1"], ["o2_1"])
    op("y", None, ["oc0", "oc1", "o2_0", "o2_1", "o3"] + ["o1_%d" % k for k in range(4)], [])
    return ops, sent[0]


def rank_program(g, core, T, topo):
    rank = T.rank_of(core)
    if rank is None:
        hand_on(g, core, T, topo)
        return
    kind = 0 if route(T, topo, rank)[1] is None else 1
    ops, sent = plan(core, T, topo, CFG[kind])
    code = ORDER[kind]
    order = [62 * DIGITS.index(code[i]) + DIGITS.index(code[i + 1]) for i in range(0, len(code), 2)]
    assert sorted(order) == list(range(len(ops)))
    emit(g, T, [ops[i] for i in order])
    g.wait_ge(T.sem.sent, sent)
